import numpy as np
import ml_dtypes


def mxq(x, axis, fmt="e4m3"):
    dtype, down = {"e4m3": (ml_dtypes.float8_e4m3fn, 7), "e5m2": (ml_dtypes.float8_e5m2, 14)}[fmt]
    v = np.moveaxis(np.asarray(x, np.float32).astype(ml_dtypes.bfloat16).astype(np.float64), axis, -1)
    blocks = v.reshape(v.shape[:-1] + (-1, 32))
    amax = np.abs(blocks).max(-1, keepdims=True)
    byte = np.maximum(np.where(amax > 0, np.frexp(amax)[1] - 1 + 127, 0) - down, 1)
    scale = np.exp2(byte - 127.0)
    codes = (blocks / scale).astype(np.float32).astype(dtype).astype(np.float64)
    return np.moveaxis((codes * scale).reshape(v.shape), -1, axis)


WIDE = False


def mx_kscale(k):
    if not WIDE:
        return np.ones(k)
    levels = np.array([10, -10, 5, -5, 0])
    if k % 512:
        return np.exp2(np.random.permutation(np.resize(levels, k // 32))).repeat(32)
    a = np.empty((k // 512, 16))
    for p in range(k // 512):
        a[p, :8] = np.random.permutation(np.resize(levels, 8))
        for g in range(8):
            far = levels[np.abs(levels - a[p, g]) >= 10]
            a[p, g + 8] = far[np.random.randint(len(far))]
    return np.exp2(a.ravel()).repeat(32)


def f64(x):
    return np.asarray(x).astype(np.float64)


def striped(idx):
    return np.tile(idx.reshape(-1, 16).T, (8, 1)).astype(np.uint16)


def unstriped(offs):
    return offs[:16].T.reshape(-1).astype(np.int64)


E2M1 = np.array([0.0, 0.5, 1.0, 1.5, 2.0, 3.0, 4.0, 6.0, -0.0, -0.5, -1.0, -1.5, -2.0, -3.0, -4.0, -6.0])


def pack_weight(w, fmt):
    k, n = w.shape
    w = f64(np.asarray(w, np.float32).astype(ml_dtypes.bfloat16)).reshape(k // 32, 32, n)
    amax = np.abs(w).max(1)
    if fmt == "e4m3":
        byte = np.frexp(amax)[1] - 1 + 127 - 7
    else:
        mant, ex = np.frexp(amax / 6.0)
        byte = np.where(mant > 0.5, ex, ex - 1) + 127
    byte = np.clip(np.where(amax > 0, byte, 1), 1, 254)
    scaled = (w * np.exp2(127.0 - byte)[:, None, :]).reshape(k, n).astype(np.float32)
    by_word = np.ascontiguousarray(scaled.reshape(k // 512, 128, 4, n).transpose(0, 1, 3, 2))
    if fmt == "e4m3":
        words = by_word.astype(ml_dtypes.float8_e4m3fn).view(np.uint8)
    else:
        c = by_word.astype(ml_dtypes.float4_e2m1fn).view(np.uint8) & 0xF
        words = (c[..., 0::2] | (c[..., 1::2] << 4)).reshape(k // 512, 128, 2 * n)
    return np.ascontiguousarray(words), np.ascontiguousarray(byte.astype(np.uint8).reshape(k // 512, 16, n))


def unpack_weight(words, scales, fmt):
    g, _, n = scales.shape
    words = np.ascontiguousarray(words).reshape(g, 128, n, -1)
    if fmt == "e4m3":
        vals = words.view(ml_dtypes.float8_e4m3fn).astype(np.float64)
    else:
        nib = np.empty((g, 128, n, 4), np.uint8)
        nib[..., 0::2] = words & 0xF
        nib[..., 1::2] = words >> 4
        vals = E2M1[nib]
    vals = vals * np.repeat(np.exp2(scales.astype(np.float64) - 127.0), 8, axis=1)[..., None]
    return vals.transpose(0, 1, 3, 2).reshape(g * 512, n)


def gelu(v):
    return 0.5 * v * (1.0 + np.tanh(np.sqrt(2.0 / np.pi) * (v + 0.044715 * v**3)))


K, R, N, T, T2, S = 1024, 1024, 512, 2048, 2048, 1024

def setup_inputs():
    n = np.random.standard_normal
    s = mx_kscale(K)[:, None]
    u = mx_kscale(R)[:, None]
    tab_words, tab_scales = pack_weight(n((K, T)) * s, "e4m3")
    wf = (0.6 * n((K, R)) / np.sqrt(K) / s).astype(np.float32)
    wb_words, wb_scales = pack_weight(0.6 * n((K, R)) / np.sqrt(K) / s, "e4m3")
    kappa = (np.exp(0.3 * n(R)) * u[:, 0]).astype(np.float32)
    ws_words, ws_scales = pack_weight(n((R, N)) / np.sqrt(R) / u, "e2m1")
    wgo = np.exp(0.3 * n((128, S))).astype(np.float32)
    offs = striped(np.random.permutation(T)[:S])
    offs2 = striped(np.random.permutation(T2)[:S])
    return dict(tab_words=tab_words, tab_scales=tab_scales, wf=wf,
                wb_words=wb_words, wb_scales=wb_scales, kappa=kappa,
                ws_words=ws_words, ws_scales=ws_scales, wgo=wgo, offs=offs, offs2=offs2)

def reference(tab_words, tab_scales, wf, wb_words, wb_scales, kappa, ws_words, ws_scales, wgo, offs, offs2):
    v = unpack_weight(tab_words, tab_scales, "e4m3")[:, unstriped(offs)]
    wfq = mxq(f64(wf), 0, "e4m3")
    wb = unpack_weight(wb_words, wb_scales, "e4m3")
    ws = unpack_weight(ws_words, ws_scales, "e2m1")
    fwd = np.exp(wfq.T @ v)
    bwd = np.exp(wb.T @ v)
    h = f64(kappa)[:, None] * (fwd - bwd)
    hq = mxq(h, 0, "e4m3")
    y = ws.T @ hq
    out = np.zeros((N, T2))
    out[:, unstriped(offs2)] = np.tile(f64(wgo), (N // 128, 1)) * y
    return out

@@ -1,0 +1,372 @@
+from contextlib import ExitStack
+
+import concourse.mybir as mybir
+
+K, R, N, T, T2, S = 1024, 1024, 512, 2048, 2048, 1024
+FLOPS = 2 * S * (2 * K * R + R * N)
+
+F32 = mybir.dt.float32
+BF16 = mybir.dt.bfloat16
+I32 = mybir.dt.int32
+U32 = mybir.dt.uint32
+U16 = mybir.dt.uint16
+U8 = mybir.dt.uint8
+FP8X4 = mybir.dt.float8_e4m3fn_x4
+FP4X4 = mybir.dt.float4_e2m1fn_x4
+EXP = mybir.ActivationFunctionType.Exp
+COPY = mybir.ActivationFunctionType.Copy
+MULT = mybir.AluOpType.mult
+SUB = mybir.AluOpType.subtract
+
+P = 128
+PACK = 4
+KP = P * PACK
+PASSES = K // KP
+GROUPS = R // KP
+JC = 256
+CHUNKS = S // JC
+NT = N // P
+LC = JC // 16
+FWD, BWD = 0, 1
+
+STEPS = [
+    ("rw", 0, 0, "S"),
+    ("ps",),
+    ("pw", 1),
+    ("rw", 0, 1, "S", 0),
+    ("rw", 0, 1, "V", 1),
+    ("gw", 0, 0, 2),
+    ("pw", 0),
+    ("qw", 0, 0),
+    ("gw", 0, 2, 4),
+    ("gs", 0, 1),
+    ("gs", 1, 2),
+    ("gw", 1, 1, 2),
+    ("gw", 1, 0, 1),
+    ("e", 1, 1, 0),
+    ("rw", 1, 0, "V", 0),
+    ("rw", 1, 0, "S", 1),
+    ("e", 1, 0, 0),
+    ("qw", 0, 1),
+    ("e", 0, 1, 0),
+    ("e", 0, 0, 0),
+    ("qw", 1, 0),
+    ("e", 1, 1, 1),
+    ("e", 1, 0, 1),
+    ("rw", 1, 1, "V"),
+    ("gw", 1, 2, 4),
+    ("qw", 1, 1),
+    ("e", 0, 0, 1),
+    ("gs", 2, 4),
+    ("e", 1, 2, 0),
+    ("h", 1, 0),
+    ("e", 0, 1, 1),
+    ("h", 0, 0),
+    ("qh", 1, 0),
+    ("h", 0, 1),
+    ("e", 0, 2, 0),
+    ("qh", 0, 1),
+    ("k", 2, 0),
+    ("qh", 0, 0),
+    ("h", 1, 1),
+    ("y", 0, 0),
+    ("qh", 1, 1),
+    ("e", 0, 2, 1),
+    ("h", 2, 0),
+    ("y", 0, 1),
+    ("y", 1, 0),
+    ("ev", 0, 0),
+    ("e", 1, 2, 1),
+    ("ev", 0, 1),
+    ("k", 2, 1),
+    ("y", 1, 1),
+    ("h", 2, 1),
+    ("ev", 1, 1),
+    ("sc", 1, 3),
+    ("e", 1, 3, 1),
+    ("e", 0, 3, 1),
+    ("qh", 2, 0),
+    ("k", 3, 1),
+    ("ev", 1, 0),
+    ("qh", 2, 1),
+    ("sc", 0, 2),
+    ("sc", 0, 0),
+    ("sc", 1, 0),
+    ("y", 2, 0),
+    ("e", 0, 3, 0),
+    ("sc", 0, 3),
+    ("e", 1, 3, 0),
+    ("h", 3, 1),
+    ("k", 3, 0),
+    ("h", 3, 0),
+    ("qh", 3, 0),
+    ("sc", 1, 2),
+    ("qh", 3, 1),
+    ("ev", 2, 0),
+    ("y", 3, 1),
+    ("y", 2, 1),
+    ("ev", 3, 1),
+    ("y", 3, 0),
+    ("ev", 2, 1),
+    ("sc", 0, 1),
+    ("sc", 2, 2),
+    ("ev", 3, 0),
+    ("sc", 1, 1),
+    ("sc", 2, 1),
+    ("sc", 3, 2),
+    ("sc", 3, 1),
+    ("sc", 2, 3),
+    ("sc", 3, 0),
+    ("sc", 2, 0),
+    ("st", 2),
+    ("sc", 3, 3),
+    ("st", 3),
+    ("st", 1),
+    ("st", 0),
+]
+
+
+def tile_list_reversible_reaction_rates_kernel(
+    tc, tab_words, tab_scales, wf, wb_words, wb_scales, kappa, ws_words, ws_scales, wgo, offs, offs2, out
+):
+    nc = tc.nc
+    with ExitStack() as ctx:
+        keep = ctx.enter_context(tc.tile_pool(name="keep", bufs=1))
+        psum = ctx.enter_context(tc.psum_pool(name="psum", bufs=1))
+        banks = []
+
+        def next_bank():
+            banks.append(psum.tile([P, 2, JC], F32, name=f"bank{len(banks)}", tag=f"bank{len(banks) % 8}"))
+            return banks[-1]
+
+        def held(shape, dtype, name):
+            return keep.tile(shape, dtype, name=name, align_bytes=64)
+
+        idx = held([P, S // 16], U16, "idx")
+        idx2 = held([P, S // 16], U16, "idx2")
+        tabw = [held([P, T], I32, f"tabw{a}") for a in range(PASSES)]
+        tabs = held([P, T // 4], I32, "tabs")
+        wbs_raw = held([P, R // 4], I32, "wbs_raw")
+        wbw_raw = [held([P, PASSES, KP], I32, f"wbw_raw{g}") for g in range(GROUPS)]
+        wf_raw = {(g, a): keep.tile([P, PACK, KP], F32, name=f"wf_raw{g}{a}", tag=f"big{4 + 2 * g + a}", align_bytes=64) for g in range(GROUPS) for a in range(PASSES)}
+        wsw = held([P, GROUPS, 2 * N], U8, "wsw")
+        wss = held([P, GROUPS, N // 4], I32, "wss")
+        kap = held([P, GROUPS, PACK], F32, "kap")
+        wg = held([P, S], F32, "wg")
+        store = [held([P, T2], F32, f"store{n}") for n in range(NT)]
+
+        nc.vector.memset(tabs[:], 0)
+        nc.vector.memset(wbs_raw[:], 0)
+        nc.gpsimd.memset(wss[:], 0)
+
+        def load_wbw(g):
+            rows = wb_words.rearrange("a p c i -> p a (c i)")[:, :, g * KP * 4 : (g + 1) * KP * 4]
+            nc.sync.dma_start(out=wbw_raw[g][:], in_=rows.bitcast(I32))
+
+        def load_wf(g, a):
+            rows = wf[a * KP : (a + 1) * KP, g * KP : (g + 1) * KP]
+            nc.sync.dma_start(out=wf_raw[g, a][:], in_=rows.rearrange("(p i) c -> p i c", i=PACK))
+
+        def load_tabw(a):
+            nc.sync.dma_start(out=tabw[a][:], in_=tab_words[a].rearrange("p t i -> p (t i)").bitcast(I32))
+
+        def load_wss(queue):
+            for q in range(4):
+                rows = ws_scales[:, 4 * q : 4 * q + 4, :].rearrange("g q c -> q g c")
+                queue.dma_start(out=wss[32 * q : 32 * q + 4, :, :], in_=rows.bitcast(I32))
+
+        def load_packed(queue, dst, src):
+            for q in range(4):
+                queue.dma_start(out=dst[32 * q : 32 * q + 8, :], in_=src[:, 4 * q : 4 * q + 4, :].bitcast(I32))
+
+        load_tabw(0)
+        load_packed(nc.sync, tabs, tab_scales)
+        nc.sync.dma_start(idx[:], offs)
+        load_tabw(1)
+        load_wf(0, 0)
+        load_wf(0, 1)
+        load_wf(1, 0)
+        load_wbw(1)
+        load_wbw(0)
+        nc.sync.dma_start(out=kap[:], in_=kappa.rearrange("(g p t) -> p g t", g=GROUPS, t=PACK))
+        load_packed(nc.sync, wbs_raw, wb_scales)
+        load_wf(1, 1)
+        nc.sync.dma_start(idx2[:], offs2)
+        nc.sync.dma_start(out=wsw[:].bitcast(I32), in_=ws_words.rearrange("g p c -> p g c").bitcast(I32))
+        load_wss(nc.sync)
+        nc.sync.dma_start(out=wg[:], in_=wgo)
+        for n in range(NT):
+            nc.gpsimd.memset(store[n][:], 0.0)
+
+        vw = [held([P, S], U32, f"vw{a}") for a in range(PASSES)]
+        vs = held([P, S], U8, "vs")
+
+        def gather_words(a, c0, c1):
+            nc.vector.tensor_copy(
+                out=vw[a][:, c0 * JC : c1 * JC], in_=tabw[a][:].bitcast(U32).indirect(idx[:, c0 * LC : c1 * LC])
+            )
+
+        def gather_scales(c0, c1):
+            nc.vector.tensor_copy(
+                out=vs[:, c0 * JC : c1 * JC], in_=tabs[:].bitcast(U8).indirect(idx[:, c0 * LC : c1 * LC])
+            )
+
+        wbw = [held([P, PASSES, PACK, P], I32, f"wbw{g}") for g in range(GROUPS)]
+        wbs = held([P, GROUPS, PACK, P], U8, "wbs")
+        wfw = {(g, a): held([P, KP], U32, f"wfw{g}{a}") for g in range(GROUPS) for a in range(PASSES)}
+        wfs = {(g, a): held([P, KP], U8, f"wfs{g}{a}") for g in range(GROUPS) for a in range(PASSES)}
+
+        def permute_wbs():
+            nc.vector.tensor_copy(
+                out=wbs[:], in_=wbs_raw[:].bitcast(U8).rearrange("p (g m t) -> p g t m", g=GROUPS, t=PACK)
+            )
+
+        def permute_wbw(g):
+            nc.vector.tensor_copy(
+                out=wbw[g][:].rearrange("p a t m -> p a m t"),
+                in_=wbw_raw[g][:].rearrange("p a (m t) -> p a m t", t=PACK),
+            )
+
+        wf_bf = {}
+
+        def round_wf(g, a, engine, half=None):
+            if (g, a) not in wf_bf:
+                wf_bf[g, a] = keep.tile(
+                    [P, PACK, P, PACK], BF16, name=f"wf_bf{g}{a}", tag=f"wf_bf{len(wf_bf) % 2}", align_bytes=64
+                )
+            ms = slice(0, P) if half is None else slice(half * P // 2, (half + 1) * P // 2)
+            dst = wf_bf[g, a][:].rearrange("p t m i -> p m i t")[:, ms]
+            src = wf_raw[g, a][:].rearrange("p i (m t) -> p m i t", t=PACK)[:, ms]
+            if engine == "S":
+                nc.scalar.copy(out=dst, in_=src)
+            else:
+                nc.vector.tensor_copy(out=dst, in_=src)
+
+        def quantize_wf(g, a):
+            nc.vector.quantize_mx(
+                out=wfw[g, a][:].bitcast(FP8X4),
+                scales=wfs[g, a][:],
+                in_=wf_bf[g, a][:].rearrange("p t m i -> p (t m i)"),
+            )
+
+        rates = {}
+
+        def exps(side, c, g):
+            if (c, g) not in rates:
+                rates[c, g] = keep.tile([P, 2, PACK, JC], F32, name=f"rates{c}{g}", tag=f"big{len(rates)}", align_bytes=64)
+            cols = slice(c * JC, (c + 1) * JC)
+            for t0 in range(0, PACK, 2):
+                bank = next_bank()
+                for t in (t0, t0 + 1):
+                    for a in range(PASSES):
+                        if side == FWD:
+                            lhsT = wfw[g, a][:, t * P : (t + 1) * P]
+                            lhsT_scale = wfs[g, a][:, t * P : (t + 1) * P]
+                        else:
+                            lhsT = wbw[g][:, a, t, :]
+                            lhsT_scale = wbs[4 * a :, g, t, :]
+                        nc.tensor.matmul_mx(
+                            out=bank[:, t - t0, :],
+                            lhsT=lhsT.bitcast(FP8X4),
+                            lhsT_scale=lhsT_scale,
+                            rhs=vw[a][:, cols].bitcast(FP8X4),
+                            rhs_scale=vs[4 * a :, cols],
+                            start=(a == 0),
+                            stop=(a == PASSES - 1),
+                        )
+                nc.scalar.activation(out=rates[c, g][:, side, t0 : t0 + 2, :], in_=bank[:], func=EXP)
+
+        hw = {}
+        hs = {}
+        h_bf = {}
+
+        def by_four(plane_major):
+            return plane_major.rearrange("p t (u i) -> p u t i", i=4)
+
+        scaled = set()
+        diffs = []
+
+        def scale_rates(c, g):
+            e = rates[c, g]
+            scaled.add((c, g))
+            for t in range(PACK):
+                nc.scalar.activation(out=e[:, :, t, :], in_=e[:, :, t, :], func=COPY, scale=kap[:, g, t : t + 1])
+
+        def net_rate(c, g):
+            e = rates[c, g]
+            grouped = keep.tile([P, JC, PACK], BF16, name=f"h_bf{c}{g}", tag=f"h_bf{len(h_bf) % 3}", align_bytes=64)
+            h_bf[c, g] = grouped
+            dst = grouped[:].rearrange("p (u i) t -> p u t i", i=4)
+            if (c, g) in scaled:
+                nc.vector.tensor_tensor(out=dst, in0=by_four(e[:, FWD]), in1=by_four(e[:, BWD]), op=SUB)
+            else:
+                diff = keep.tile([P, PACK, JC], F32, name=f"diff{c}{g}", tag=f"diff{len(diffs) % 2}", align_bytes=64)
+                diffs.append(diff)
+                nc.vector.tensor_tensor(out=diff[:], in0=e[:, FWD], in1=e[:, BWD], op=SUB)
+                factor = kap[:, g, :].unsqueeze(1).unsqueeze(3).to_broadcast([P, JC // 4, PACK, 4])
+                nc.vector.tensor_tensor(out=dst, in0=by_four(diff[:]), in1=factor, op=MULT)
+
+        def quantize_h(c, g):
+            hw[c, g] = held([P, JC], U32, f"hw{c}{g}")
+            hs[c, g] = held([P, JC], U8, f"hs{c}{g}")
+            nc.vector.quantize_mx(
+                out=hw[c, g][:].bitcast(FP8X4),
+                scales=hs[c, g][:],
+                in_=h_bf[c, g][:].rearrange("p j t -> p (j t)"),
+            )
+
+        ys = {}
+
+        ybank = {}
+
+        def species(c, pair):
+            bank = next_bank()
+            ybank[c, pair] = bank
+            for n in (2 * pair, 2 * pair + 1):
+                for j0 in range(0, JC, P):
+                    for g in range(GROUPS):
+                        nc.tensor.matmul_mx(
+                            out=bank[:, n - 2 * pair, j0 : j0 + P],
+                            lhsT=wsw[:, g, 2 * n * P : 2 * (n + 1) * P].bitcast(FP4X4),
+                            lhsT_scale=wss[:, g, n * P // 4 : (n + 1) * P // 4].bitcast(U8),
+                            rhs=hw[c, g][:, j0 : j0 + P].bitcast(FP8X4),
+                            rhs_scale=hs[c, g][:, j0 : j0 + P],
+                            start=(g == 0),
+                            stop=(g == GROUPS - 1),
+                        )
+
+        def evacuate(c, pair):
+            y = held([P, 2, JC], F32, f"y{c}{pair}")
+            nc.scalar.copy(out=y[:], in_=ybank[c, pair][:])
+            ys[c, 2 * pair] = y[:, 0, :]
+            ys[c, 2 * pair + 1] = y[:, 1, :]
+
+        def write_out(n):
+            nc.sync.dma_start(out=out[n * P : (n + 1) * P, :], in_=store[n][:])
+
+        def scatter(c, n):
+            nc.vector.tensor_tensor(
+                out=store[n][:].indirect(idx2[:, c * LC : (c + 1) * LC]),
+                in0=ys[c, n],
+                in1=wg[:, c * JC : (c + 1) * JC],
+                op=MULT,
+            )
+
+        calls = {
+            "gw": gather_words,
+            "gs": gather_scales,
+            "ps": permute_wbs,
+            "pw": permute_wbw,
+            "rw": round_wf,
+            "qw": quantize_wf,
+            "e": exps,
+            "h": net_rate,
+            "qh": quantize_h,
+            "y": species,
+            "k": scale_rates,
+            "ev": evacuate,
+            "sc": scatter,
+            "st": write_out,
+        }
+        for step in STEPS:
+            calls[step[0]](*step[1:])

@@ -1,6 +1,7 @@
 from contextlib import ExitStack
 
 import concourse.mybir as mybir
+from concourse.masks import make_identity
 
 K, R, N, T, T2, S = 1024, 1024, 512, 2048, 2048, 1024
 FLOPS = 2 * S * (2 * K * R + R * N)
@@ -16,7 +17,6 @@ FP4X4 = mybir.dt.float4_e2m1fn_x4
 EXP = mybir.ActivationFunctionType.Exp
 COPY = mybir.ActivationFunctionType.Copy
 MULT = mybir.AluOpType.mult
-SUB = mybir.AluOpType.subtract
 
 P = 128
 PACK = 4
@@ -25,105 +25,10 @@ PASSES = K // KP
 GROUPS = R // KP
 JC = 256
 CHUNKS = S // JC
+TILES = JC // P
 NT = N // P
-LC = JC // 16
-FWD, BWD = 0, 1
-
-STEPS = [
-    ("rw", 0, 0, "S"),
-    ("ps",),
-    ("pw", 1),
-    ("rw", 0, 1, "S", 0),
-    ("rw", 0, 1, "V", 1),
-    ("gw", 0, 0, 2),
-    ("pw", 0),
-    ("qw", 0, 0),
-    ("gw", 0, 2, 4),
-    ("gs", 0, 1),
-    ("gs", 1, 2),
-    ("gw", 1, 1, 2),
-    ("gw", 1, 0, 1),
-    ("e", 1, 1, 0),
-    ("rw", 1, 0, "V", 0),
-    ("rw", 1, 0, "S", 1),
-    ("e", 1, 0, 0),
-    ("qw", 0, 1),
-    ("e", 0, 1, 0),
-    ("e", 0, 0, 0),
-    ("qw", 1, 0),
-    ("e", 1, 1, 1),
-    ("e", 1, 0, 1),
-    ("rw", 1, 1, "V"),
-    ("gw", 1, 2, 4),
-    ("qw", 1, 1),
-    ("e", 0, 0, 1),
-    ("gs", 2, 4),
-    ("e", 1, 2, 0),
-    ("h", 1, 0),
-    ("e", 0, 1, 1),
-    ("h", 0, 0),
-    ("qh", 1, 0),
-    ("h", 0, 1),
-    ("e", 0, 2, 0),
-    ("qh", 0, 1),
-    ("k", 2, 0),
-    ("qh", 0, 0),
-    ("h", 1, 1),
-    ("y", 0, 0),
-    ("qh", 1, 1),
-    ("e", 0, 2, 1),
-    ("h", 2, 0),
-    ("y", 0, 1),
-    ("y", 1, 0),
-    ("ev", 0, 0),
-    ("e", 1, 2, 1),
-    ("ev", 0, 1),
-    ("k", 2, 1),
-    ("y", 1, 1),
-    ("h", 2, 1),
-    ("ev", 1, 1),
-    ("sc", 1, 3),
-    ("e", 1, 3, 1),
-    ("e", 0, 3, 1),
-    ("qh", 2, 0),
-    ("k", 3, 1),
-    ("ev", 1, 0),
-    ("qh", 2, 1),
-    ("sc", 0, 2),
-    ("sc", 0, 0),
-    ("sc", 1, 0),
-    ("y", 2, 0),
-    ("e", 0, 3, 0),
-    ("sc", 0, 3),
-    ("e", 1, 3, 0),
-    ("h", 3, 1),
-    ("k", 3, 0),
-    ("h", 3, 0),
-    ("qh", 3, 0),
-    ("sc", 1, 2),
-    ("qh", 3, 1),
-    ("ev", 2, 0),
-    ("y", 3, 1),
-    ("y", 2, 1),
-    ("ev", 3, 1),
-    ("y", 3, 0),
-    ("ev", 2, 1),
-    ("sc", 0, 1),
-    ("sc", 2, 2),
-    ("ev", 3, 0),
-    ("sc", 1, 1),
-    ("sc", 2, 1),
-    ("sc", 3, 2),
-    ("sc", 3, 1),
-    ("sc", 2, 3),
-    ("sc", 3, 0),
-    ("sc", 2, 0),
-    ("st", 2),
-    ("sc", 3, 3),
-    ("st", 3),
-    ("st", 1),
-    ("st", 0),
-]
+PER_COL = 16
+RING = 3
 
 
 def tile_list_reversible_reaction_rates_kernel(
@@ -133,35 +38,35 @@ def tile_list_reversible_reaction_rates_kernel(
     with ExitStack() as ctx:
         keep = ctx.enter_context(tc.tile_pool(name="keep", bufs=1))
         psum = ctx.enter_context(tc.psum_pool(name="psum", bufs=1))
-        banks = []
-
-        def next_bank():
-            banks.append(psum.tile([P, 2, JC], F32, name=f"bank{len(banks)}", tag=f"bank{len(banks) % 8}"))
-            return banks[-1]
 
         def held(shape, dtype, name):
             return keep.tile(shape, dtype, name=name, align_bytes=64)
 
-        idx = held([P, S // 16], U16, "idx")
-        idx2 = held([P, S // 16], U16, "idx2")
+        idx = held([P, S // PER_COL], U16, "idx")
+        idx2 = held([P, S // PER_COL], U16, "idx2")
         tabw = [held([P, T], I32, f"tabw{a}") for a in range(PASSES)]
         tabs = held([P, T // 4], I32, "tabs")
-        wbs_raw = held([P, R // 4], I32, "wbs_raw")
-        wbw_raw = [held([P, PASSES, KP], I32, f"wbw_raw{g}") for g in range(GROUPS)]
-        wf_raw = {(g, a): keep.tile([P, PACK, KP], F32, name=f"wf_raw{g}{a}", tag=f"big{4 + 2 * g + a}", align_bytes=64) for g in range(GROUPS) for a in range(PASSES)}
+        wbs = held([P, R // 4], I32, "wbs")
+        wbw = [held([P, PASSES, KP], I32, f"wbw{g}") for g in range(GROUPS)]
+        wf_raw = {(g, a): held([P, PACK, KP], F32, f"wf_raw{g}{a}") for g in range(GROUPS) for a in range(PASSES)}
         wsw = held([P, GROUPS, 2 * N], U8, "wsw")
         wss = held([P, GROUPS, N // 4], I32, "wss")
         kap = held([P, GROUPS, PACK], F32, "kap")
         wg = held([P, S], F32, "wg")
         store = [held([P, T2], F32, f"store{n}") for n in range(NT)]
+        ident = held([P, P], F32, "ident")
+        y = held([P, NT, S], F32, "y")
 
         nc.vector.memset(tabs[:], 0)
-        nc.vector.memset(wbs_raw[:], 0)
-        nc.gpsimd.memset(wss[:], 0)
+        nc.vector.memset(wbs[:], 0)
+        nc.vector.memset(wss[:], 0)
+        for n in range(NT):
+            nc.vector.memset(store[n][:], 0.0)
+        make_identity(nc, ident[:])
 
         def load_wbw(g):
             rows = wb_words.rearrange("a p c i -> p a (c i)")[:, :, g * KP * 4 : (g + 1) * KP * 4]
-            nc.sync.dma_start(out=wbw_raw[g][:], in_=rows.bitcast(I32))
+            nc.sync.dma_start(out=wbw[g][:], in_=rows.bitcast(I32))
 
         def load_wf(g, a):
             rows = wf[a * KP : (a + 1) * KP, g * KP : (g + 1) * KP]
@@ -170,163 +75,175 @@ def tile_list_reversible_reaction_rates_kernel(
         def load_tabw(a):
             nc.sync.dma_start(out=tabw[a][:], in_=tab_words[a].rearrange("p t i -> p (t i)").bitcast(I32))
 
-        def load_wss(queue):
+        def load_packed(dst, src):
             for q in range(4):
-                rows = ws_scales[:, 4 * q : 4 * q + 4, :].rearrange("g q c -> q g c")
-                queue.dma_start(out=wss[32 * q : 32 * q + 4, :, :], in_=rows.bitcast(I32))
+                nc.scalar.dma_start(out=dst[32 * q : 32 * q + 8, :], in_=src[:, 4 * q : 4 * q + 4, :].bitcast(I32))
 
-        def load_packed(queue, dst, src):
-            for q in range(4):
-                queue.dma_start(out=dst[32 * q : 32 * q + 8, :], in_=src[:, 4 * q : 4 * q + 4, :].bitcast(I32))
-
-        load_tabw(0)
-        load_packed(nc.sync, tabs, tab_scales)
         nc.sync.dma_start(idx[:], offs)
+        load_tabw(0)
+        load_packed(tabs, tab_scales)
         load_tabw(1)
+        load_packed(wbs, wb_scales)
+        load_wbw(0)
         load_wf(0, 0)
         load_wf(0, 1)
-        load_wf(1, 0)
+        nc.scalar.dma_start(out=kap[:], in_=kappa.rearrange("(g p t) -> p g t", g=GROUPS, t=PACK))
         load_wbw(1)
-        load_wbw(0)
-        nc.sync.dma_start(out=kap[:], in_=kappa.rearrange("(g p t) -> p g t", g=GROUPS, t=PACK))
-        load_packed(nc.sync, wbs_raw, wb_scales)
+        load_wf(1, 0)
         load_wf(1, 1)
-        nc.sync.dma_start(idx2[:], offs2)
+        for q in range(4):
+            rows = ws_scales[:, 4 * q : 4 * q + 4, :].rearrange("g q c -> q g c")
+            nc.sync.dma_start(out=wss[32 * q : 32 * q + 4, :, :], in_=rows.bitcast(I32))
         nc.sync.dma_start(out=wsw[:].bitcast(I32), in_=ws_words.rearrange("g p c -> p g c").bitcast(I32))
-        load_wss(nc.sync)
+        nc.sync.dma_start(idx2[:], offs2)
         nc.sync.dma_start(out=wg[:], in_=wgo)
-        for n in range(NT):
-            nc.gpsimd.memset(store[n][:], 0.0)
 
         vw = [held([P, S], U32, f"vw{a}") for a in range(PASSES)]
         vs = held([P, S], U8, "vs")
 
-        def gather_words(a, c0, c1):
-            nc.vector.tensor_copy(
-                out=vw[a][:, c0 * JC : c1 * JC], in_=tabw[a][:].bitcast(U32).indirect(idx[:, c0 * LC : c1 * LC])
-            )
+        def entries(lst, j0, j1):
+            return lst[:, j0 // PER_COL : j1 // PER_COL]
 
-        def gather_scales(c0, c1):
-            nc.vector.tensor_copy(
-                out=vs[:, c0 * JC : c1 * JC], in_=tabs[:].bitcast(U8).indirect(idx[:, c0 * LC : c1 * LC])
-            )
+        def gather_words(a, j0, j1):
+            nc.vector.tensor_copy(out=vw[a][:, j0:j1], in_=tabw[a][:].bitcast(U32).indirect(entries(idx, j0, j1)))
 
-        wbw = [held([P, PASSES, PACK, P], I32, f"wbw{g}") for g in range(GROUPS)]
-        wbs = held([P, GROUPS, PACK, P], U8, "wbs")
+        def gather_scales(j0, j1):
+            nc.vector.tensor_copy(out=vs[:, j0:j1], in_=tabs[:].bitcast(U8).indirect(entries(idx, j0, j1)))
+
+        for half in range(2):
+            lo, hi = half * S // 2, (half + 1) * S // 2
+            gather_words(0, lo, hi)
+            gather_scales(lo, hi)
+            gather_words(1, lo, hi)
+
         wfw = {(g, a): held([P, KP], U32, f"wfw{g}{a}") for g in range(GROUPS) for a in range(PASSES)}
         wfs = {(g, a): held([P, KP], U8, f"wfs{g}{a}") for g in range(GROUPS) for a in range(PASSES)}
 
-        def permute_wbs():
-            nc.vector.tensor_copy(
-                out=wbs[:], in_=wbs_raw[:].bitcast(U8).rearrange("p (g m t) -> p g t m", g=GROUPS, t=PACK)
-            )
-
-        def permute_wbw(g):
-            nc.vector.tensor_copy(
-                out=wbw[g][:].rearrange("p a t m -> p a m t"),
-                in_=wbw_raw[g][:].rearrange("p a (m t) -> p a m t", t=PACK),
-            )
-
-        wf_bf = {}
-
-        def round_wf(g, a, engine, half=None):
-            if (g, a) not in wf_bf:
-                wf_bf[g, a] = keep.tile(
-                    [P, PACK, P, PACK], BF16, name=f"wf_bf{g}{a}", tag=f"wf_bf{len(wf_bf) % 2}", align_bytes=64
-                )
-            ms = slice(0, P) if half is None else slice(half * P // 2, (half + 1) * P // 2)
-            dst = wf_bf[g, a][:].rearrange("p t m i -> p m i t")[:, ms]
-            src = wf_raw[g, a][:].rearrange("p i (m t) -> p m i t", t=PACK)[:, ms]
-            if engine == "S":
+        def round_wf(g, a, c0, c1, on_scalar):
+            grouped = held([P, c1 - c0, PACK], BF16, f"wf_bf{g}{a}{c0}")
+            dst = grouped[:].rearrange("p (u i) t -> p u t i", i=4)
+            src = wf_raw[g, a][:, :, c0:c1].rearrange("p t (u i) -> p u t i", i=4)
+            if on_scalar:
                 nc.scalar.copy(out=dst, in_=src)
             else:
                 nc.vector.tensor_copy(out=dst, in_=src)
+            return grouped
 
-        def quantize_wf(g, a):
+        def quantize_wf(g, a, c0, c1, grouped):
             nc.vector.quantize_mx(
-                out=wfw[g, a][:].bitcast(FP8X4),
-                scales=wfs[g, a][:],
-                in_=wf_bf[g, a][:].rearrange("p t m i -> p (t m i)"),
+                out=wfw[g, a][:, c0:c1].bitcast(FP8X4),
+                scales=wfs[g, a][:, c0:c1],
+                in_=grouped[:].rearrange("p c t -> p (c t)"),
             )
 
-        rates = {}
+        def prepare_whole(g, a, on_scalar):
+            quantize_wf(g, a, 0, KP, round_wf(g, a, 0, KP, on_scalar))
 
-        def exps(side, c, g):
-            if (c, g) not in rates:
-                rates[c, g] = keep.tile([P, 2, PACK, JC], F32, name=f"rates{c}{g}", tag=f"big{len(rates)}", align_bytes=64)
-            cols = slice(c * JC, (c + 1) * JC)
-            for t0 in range(0, PACK, 2):
-                bank = next_bank()
-                for t in (t0, t0 + 1):
-                    for a in range(PASSES):
-                        if side == FWD:
-                            lhsT = wfw[g, a][:, t * P : (t + 1) * P]
-                            lhsT_scale = wfs[g, a][:, t * P : (t + 1) * P]
-                        else:
-                            lhsT = wbw[g][:, a, t, :]
-                            lhsT_scale = wbs[4 * a :, g, t, :]
-                        nc.tensor.matmul_mx(
-                            out=bank[:, t - t0, :],
-                            lhsT=lhsT.bitcast(FP8X4),
-                            lhsT_scale=lhsT_scale,
-                            rhs=vw[a][:, cols].bitcast(FP8X4),
-                            rhs_scale=vs[4 * a :, cols],
-                            start=(a == 0),
-                            stop=(a == PASSES - 1),
-                        )
-                nc.scalar.activation(out=rates[c, g][:, side, t0 : t0 + 2, :], in_=bank[:], func=EXP)
+        def prepare_shared(g, a):
+            low = round_wf(g, a, 0, KP // 2, False)
+            high = round_wf(g, a, KP // 2, KP, True)
+            quantize_wf(g, a, 0, KP // 2, low)
+            quantize_wf(g, a, KP // 2, KP, high)
+
+        for g in range(GROUPS):
+            for a in range(PASSES):
+                prepare_whole(g, a, False)
+
+        banks = [psum.tile([P, KP], F32, name=f"bank{b}") for b in range(8)]
+        fwd_ring = [held([P, TILES, PACK, P], F32, f"fwd{r}") for r in range(RING)]
+        bwd_ring = [held([P, TILES, PACK, P], F32, f"bwd{r}") for r in range(RING)]
+        h_ring = [held([P, JC, PACK], BF16, f"h_bf{r}") for r in range(RING)]
+
+        def product(bank, cells, words, scales):
+            for a in range(PASSES):
+                nc.tensor.matmul_mx(
+                    out=bank[:],
+                    lhsT=vw[a][:, cells].bitcast(FP8X4),
+                    lhsT_scale=vs[4 * a :, cells],
+                    rhs=words(a).bitcast(FP8X4),
+                    rhs_scale=scales(a),
+                    start=(a == 0),
+                    stop=(a == PASSES - 1),
+                )
+
+        def exp_out(dst, bank):
+            nc.scalar.activation(out=dst, in_=bank[:].rearrange("p (m i) -> p i m", i=PACK), func=EXP)
+
+        steps = [(c, g) for c in range(CHUNKS) for g in range(GROUPS)]
+
+        slot = [0, 2, 1, 2, 0, 1, 2, 0]
+
+        def cells(c, u):
+            return slice(c * JC + u * P, c * JC + (u + 1) * P)
+
+        def backward(s):
+            c, g = steps[s]
+            group = slice(g * KP, (g + 1) * KP)
+            for u in range(TILES):
+                product(banks[u], cells(c, u), lambda a: wbw[g][:, a, :], lambda a: wbs[4 * a :, :].bitcast(U8)[:, group])
+                exp_out(bwd_ring[slot[s]][:, u], banks[u])
+            negate(s)
+
+        def negate(s):
+            bwd = bwd_ring[slot[s]]
+            if s < 0:
+                nc.vector.tensor_scalar(out=bwd[:], in0=bwd[:], scalar1=-1.0, scalar2=None, op0=MULT)
+            else:
+                nc.scalar.activation(out=bwd[:], in_=bwd[:], func=COPY, scale=-1.0)
+
+        def forward(s):
+            c, g = steps[s]
+            for u in range(TILES):
+                product(banks[TILES + u], cells(c, u), lambda a: wfw[g, a][:], lambda a: wfs[g, a][:])
+                exp_out(fwd_ring[slot[s]][:, u], banks[TILES + u])
+
+        planes = held([P, PACK, JC], BF16, "planes")
+        late = []
+
+        def late_bank():
+            late.append(banks[4 + len(late) % 4])
+            return late[-1]
 
         hw = {}
         hs = {}
-        h_bf = {}
 
-        def by_four(plane_major):
-            return plane_major.rearrange("p t (u i) -> p u t i", i=4)
-
-        scaled = set()
-        diffs = []
-
-        def scale_rates(c, g):
-            e = rates[c, g]
-            scaled.add((c, g))
-            for t in range(PACK):
-                nc.scalar.activation(out=e[:, :, t, :], in_=e[:, :, t, :], func=COPY, scale=kap[:, g, t : t + 1])
-
-        def net_rate(c, g):
-            e = rates[c, g]
-            grouped = keep.tile([P, JC, PACK], BF16, name=f"h_bf{c}{g}", tag=f"h_bf{len(h_bf) % 3}", align_bytes=64)
-            h_bf[c, g] = grouped
-            dst = grouped[:].rearrange("p (u i) t -> p u t i", i=4)
-            if (c, g) in scaled:
-                nc.vector.tensor_tensor(out=dst, in0=by_four(e[:, FWD]), in1=by_four(e[:, BWD]), op=SUB)
-            else:
-                diff = keep.tile([P, PACK, JC], F32, name=f"diff{c}{g}", tag=f"diff{len(diffs) % 2}", align_bytes=64)
-                diffs.append(diff)
-                nc.vector.tensor_tensor(out=diff[:], in0=e[:, FWD], in1=e[:, BWD], op=SUB)
-                factor = kap[:, g, :].unsqueeze(1).unsqueeze(3).to_broadcast([P, JC // 4, PACK, 4])
-                nc.vector.tensor_tensor(out=dst, in0=by_four(diff[:]), in1=factor, op=MULT)
-
-        def quantize_h(c, g):
+        def net_rates(s):
+            c, g = steps[s]
+            fwd, bwd, grouped = fwd_ring[slot[s]], bwd_ring[slot[s]], h_ring[s % RING]
+            factor = kap[:, g, :].unsqueeze(1).to_broadcast([P, P, PACK])
+            for u in range(TILES):
+                bank = late_bank()[:].rearrange("p (i j) -> p i j", i=PACK)
+                for i in range(PACK):
+                    for side, first in ((fwd, True), (bwd, False)):
+                        nc.tensor.matmul(
+                            out=bank[:, i, :], lhsT=side[:, u, i, :], rhs=ident[:], is_transpose=True, start=first, stop=not first
+                        )
+                if s > 9:
+                    for i in range(PACK):
+                        nc.scalar.activation(
+                            out=planes[:, i, u * P : (u + 1) * P], in_=bank[:, i, :], func=COPY, scale=kap[:, g, i : i + 1]
+                        )
+                else:
+                    nc.vector.tensor_tensor(
+                        out=grouped[:, u * P : (u + 1) * P, :], in0=bank.rearrange("p i j -> p j i"), in1=factor, op=MULT
+                    )
+            if s > 9:
+                nc.scalar.copy(
+                    out=grouped[:].rearrange("p (w e) t -> p w t e", e=4), in_=planes[:].rearrange("p t (w e) -> p w t e", e=4)
+                )
             hw[c, g] = held([P, JC], U32, f"hw{c}{g}")
             hs[c, g] = held([P, JC], U8, f"hs{c}{g}")
             nc.vector.quantize_mx(
-                out=hw[c, g][:].bitcast(FP8X4),
-                scales=hs[c, g][:],
-                in_=h_bf[c, g][:].rearrange("p j t -> p (j t)"),
+                out=hw[c, g][:].bitcast(FP8X4), scales=hs[c, g][:], in_=grouped[:].rearrange("p j t -> p (j t)")
             )
 
-        ys = {}
-
-        ybank = {}
-
-        def species(c, pair):
-            bank = next_bank()
-            ybank[c, pair] = bank
-            for n in (2 * pair, 2 * pair + 1):
+        def species(c, n0, n1):
+            bank = late_bank()[:].rearrange("p (n j) -> p n j", j=JC)
+            for n in range(n0, n1):
                 for j0 in range(0, JC, P):
                     for g in range(GROUPS):
                         nc.tensor.matmul_mx(
-                            out=bank[:, n - 2 * pair, j0 : j0 + P],
+                            out=bank[:, n - n0, j0 : j0 + P],
                             lhsT=wsw[:, g, 2 * n * P : 2 * (n + 1) * P].bitcast(FP4X4),
                             lhsT_scale=wss[:, g, n * P // 4 : (n + 1) * P // 4].bitcast(U8),
                             rhs=hw[c, g][:, j0 : j0 + P].bitcast(FP8X4),
@@ -334,39 +251,52 @@ def tile_list_reversible_reaction_rates_kernel(
                             start=(g == 0),
                             stop=(g == GROUPS - 1),
                         )
+            nc.scalar.copy(out=y[:, n0:n1, c * JC : (c + 1) * JC], in_=bank[:, : n1 - n0, :])
 
-        def evacuate(c, pair):
-            y = held([P, 2, JC], F32, f"y{c}{pair}")
-            nc.scalar.copy(out=y[:], in_=ybank[c, pair][:])
-            ys[c, 2 * pair] = y[:, 0, :]
-            ys[c, 2 * pair + 1] = y[:, 1, :]
-
-        def write_out(n):
-            nc.sync.dma_start(out=out[n * P : (n + 1) * P, :], in_=store[n][:])
-
-        def scatter(c, n):
+        def scatter(n, j0, j1):
             nc.vector.tensor_tensor(
-                out=store[n][:].indirect(idx2[:, c * LC : (c + 1) * LC]),
-                in0=ys[c, n],
-                in1=wg[:, c * JC : (c + 1) * JC],
-                op=MULT,
+                out=store[n][:].indirect(entries(idx2, j0, j1)), in0=y[:, n, j0:j1], in1=wg[:, j0:j1], op=MULT
             )
+            if j1 == S:
+                nc.sync.dma_start(out=out[n * P : (n + 1) * P, :], in_=store[n][:])
 
-        calls = {
-            "gw": gather_words,
-            "gs": gather_scales,
-            "ps": permute_wbs,
-            "pw": permute_wbw,
-            "rw": round_wf,
-            "qw": quantize_wf,
-            "e": exps,
-            "h": net_rate,
-            "qh": quantize_h,
-            "y": species,
-            "k": scale_rates,
-            "ev": evacuate,
-            "sc": scatter,
-            "st": write_out,
-        }
-        for step in STEPS:
-            calls[step[0]](*step[1:])
+        def place(c, n0, n1):
+            species(c, n0, n1)
+            for n in range(n0, n1):
+                scatter(n, c * JC, (c + 1) * JC)
+
+        backward(0)
+        backward(2)
+        forward(0)
+        backward(1)
+        forward(2)
+        net_rates(0)
+        forward(1)
+        net_rates(1)
+        net_rates(2)
+        place(0, 0, 2)
+        backward(3)
+        forward(3)
+        place(0, 2, 3)
+        backward(4)
+        forward(4)
+        for c in range(1, CHUNKS - 1):
+            s = 2 * c + 1
+            net_rates(s)
+            backward(s + 2)
+            place(c - 1, 3, 4)
+            forward(s + 2)
+            place(c, 0, 1)
+            net_rates(s + 1)
+            place(c, 1, 3 if c + 2 < CHUNKS else 2)
+            if s + 3 < len(steps):
+                backward(s + 3)
+                forward(s + 3)
+        last = CHUNKS - 1
+        net_rates(len(steps) - 1)
+        place(last - 1, 2, 3)
+        species(last - 1, 3, 4)
+        place(last, 0, 1)
+        place(last, 1, 3)
+        species(last, 3, 4)
+        scatter(3, (last - 1) * JC, S)

@@ -29,6 +29,7 @@ TILES = JC // P
 NT = N // P
 PER_COL = 16
 RING = 3
+SLOTS = [0, 2, 1, 2, 0, 1, 2, 0]
 
 
 def tile_list_reversible_reaction_rates_kernel(
@@ -48,7 +49,8 @@ def tile_list_reversible_reaction_rates_kernel(
         tabs = held([P, T // 4], I32, "tabs")
         wbs = held([P, R // 4], I32, "wbs")
         wbw = [held([P, PASSES, KP], I32, f"wbw{g}") for g in range(GROUPS)]
-        wf_raw = {(g, a): held([P, PACK, KP], F32, f"wf_raw{g}{a}") for g in range(GROUPS) for a in range(PASSES)}
+        pieces = [(0, 0, 0, KP), (0, 1, 0, KP), (1, 0, 0, KP), (1, 1, 0, KP // 2), (1, 1, KP // 2, KP)]
+        wf_raw = {(g, a, c0): held([P, PACK, c1 - c0], F32, f"wf_raw{g}{a}{c0}") for g, a, c0, c1 in pieces}
         wsw = held([P, GROUPS, 2 * N], U8, "wsw")
         wss = held([P, GROUPS, N // 4], I32, "wss")
         kap = held([P, GROUPS, PACK], F32, "kap")
@@ -60,17 +62,19 @@ def tile_list_reversible_reaction_rates_kernel(
         nc.vector.memset(tabs[:], 0)
         nc.vector.memset(wbs[:], 0)
         nc.vector.memset(wss[:], 0)
-        for n in range(NT):
-            nc.vector.memset(store[n][:], 0.0)
+        for n in range(NT // 2):
+            nc.vector.memset(store[n][:].bitcast(I32), 0)
         make_identity(nc, ident[:])
+        for n in range(NT // 2, NT):
+            nc.gpsimd.memset(store[n][:].bitcast(I32), 0)
 
         def load_wbw(g):
             rows = wb_words.rearrange("a p c i -> p a (c i)")[:, :, g * KP * 4 : (g + 1) * KP * 4]
             nc.sync.dma_start(out=wbw[g][:], in_=rows.bitcast(I32))
 
-        def load_wf(g, a):
-            rows = wf[a * KP : (a + 1) * KP, g * KP : (g + 1) * KP]
-            nc.sync.dma_start(out=wf_raw[g, a][:], in_=rows.rearrange("(p i) c -> p i c", i=PACK))
+        def load_wf(g, a, c0, c1):
+            rows = wf[a * KP : (a + 1) * KP, g * KP + c0 : g * KP + c1]
+            nc.sync.dma_start(out=wf_raw[g, a, c0][:], in_=rows.rearrange("(p i) c -> p i c", i=PACK))
 
         def load_tabw(a):
             nc.sync.dma_start(out=tabw[a][:], in_=tab_words[a].rearrange("p t i -> p (t i)").bitcast(I32))
@@ -85,12 +89,13 @@ def tile_list_reversible_reaction_rates_kernel(
         load_tabw(1)
         load_packed(wbs, wb_scales)
         load_wbw(0)
-        load_wf(0, 0)
-        load_wf(0, 1)
+        load_wf(*pieces[0])
+        load_wf(*pieces[1])
         nc.scalar.dma_start(out=kap[:], in_=kappa.rearrange("(g p t) -> p g t", g=GROUPS, t=PACK))
         load_wbw(1)
-        load_wf(1, 0)
-        load_wf(1, 1)
+        load_wf(*pieces[2])
+        load_wf(*pieces[3])
+        load_wf(*pieces[4])
         for q in range(4):
             rows = ws_scales[:, 4 * q : 4 * q + 4, :].rearrange("g q c -> q g c")
             nc.sync.dma_start(out=wss[32 * q : 32 * q + 4, :, :], in_=rows.bitcast(I32))
@@ -119,10 +124,12 @@ def tile_list_reversible_reaction_rates_kernel(
         wfw = {(g, a): held([P, KP], U32, f"wfw{g}{a}") for g in range(GROUPS) for a in range(PASSES)}
         wfs = {(g, a): held([P, KP], U8, f"wfs{g}{a}") for g in range(GROUPS) for a in range(PASSES)}
 
+        wf_bf = {(g, a): held([P, KP, PACK], BF16, f"wf_bf{g}{a}") for g in range(GROUPS) for a in range(PASSES)}
+
         def round_wf(g, a, c0, c1, on_scalar):
-            grouped = held([P, c1 - c0, PACK], BF16, f"wf_bf{g}{a}{c0}")
+            grouped = wf_bf[g, a][:, c0:c1]
             dst = grouped[:].rearrange("p (u i) t -> p u t i", i=4)
-            src = wf_raw[g, a][:, :, c0:c1].rearrange("p t (u i) -> p u t i", i=4)
+            src = wf_raw[g, a, c0][:].rearrange("p t (u i) -> p u t i", i=4)
             if on_scalar:
                 nc.scalar.copy(out=dst, in_=src)
             else:
@@ -145,14 +152,12 @@ def tile_list_reversible_reaction_rates_kernel(
             quantize_wf(g, a, 0, KP // 2, low)
             quantize_wf(g, a, KP // 2, KP, high)
 
-        for g in range(GROUPS):
-            for a in range(PASSES):
-                prepare_whole(g, a, False)
+        for piece in pieces:
+            quantize_wf(*piece, round_wf(*piece, False))
 
         banks = [psum.tile([P, KP], F32, name=f"bank{b}") for b in range(8)]
         fwd_ring = [held([P, TILES, PACK, P], F32, f"fwd{r}") for r in range(RING)]
         bwd_ring = [held([P, TILES, PACK, P], F32, f"bwd{r}") for r in range(RING)]
-        h_ring = [held([P, JC, PACK], BF16, f"h_bf{r}") for r in range(RING)]
 
         def product(bank, cells, words, scales):
             for a in range(PASSES):
@@ -170,23 +175,23 @@ def tile_list_reversible_reaction_rates_kernel(
             nc.scalar.activation(out=dst, in_=bank[:].rearrange("p (m i) -> p i m", i=PACK), func=EXP)
 
         steps = [(c, g) for c in range(CHUNKS) for g in range(GROUPS)]
-
-        slot = [0, 2, 1, 2, 0, 1, 2, 0]
+        slot = SLOTS
+        planes = held([P, PACK, JC], BF16, "planes")
+        h_bf = [wf_bf[1, 1 - r][:].rearrange("p (g j) t -> p g j t", g=GROUPS) for r in range(2)]
+        hw = [held([P, GROUPS, JC], U32, f"hw{c}") for c in range(CHUNKS)]
+        hs = [held([P, GROUPS, JC], U8, f"hs{c}") for c in range(CHUNKS)]
 
         def cells(c, u):
             return slice(c * JC + u * P, c * JC + (u + 1) * P)
 
-        def backward(s):
+        def backward(s, on_vector=False):
             c, g = steps[s]
             group = slice(g * KP, (g + 1) * KP)
+            bwd = bwd_ring[slot[s]]
             for u in range(TILES):
                 product(banks[u], cells(c, u), lambda a: wbw[g][:, a, :], lambda a: wbs[4 * a :, :].bitcast(U8)[:, group])
-                exp_out(bwd_ring[slot[s]][:, u], banks[u])
-            negate(s)
-
-        def negate(s):
-            bwd = bwd_ring[slot[s]]
-            if s < 0:
+                exp_out(bwd[:, u], banks[u])
+            if on_vector:
                 nc.vector.tensor_scalar(out=bwd[:], in0=bwd[:], scalar1=-1.0, scalar2=None, op0=MULT)
             else:
                 nc.scalar.activation(out=bwd[:], in_=bwd[:], func=COPY, scale=-1.0)
@@ -197,44 +202,49 @@ def tile_list_reversible_reaction_rates_kernel(
                 product(banks[TILES + u], cells(c, u), lambda a: wfw[g, a][:], lambda a: wfs[g, a][:])
                 exp_out(fwd_ring[slot[s]][:, u], banks[TILES + u])
 
-        planes = held([P, PACK, JC], BF16, "planes")
         late = []
 
         def late_bank():
             late.append(banks[4 + len(late) % 4])
             return late[-1]
 
-        hw = {}
-        hs = {}
-
-        def net_rates(s):
-            c, g = steps[s]
-            fwd, bwd, grouped = fwd_ring[slot[s]], bwd_ring[slot[s]], h_ring[s % RING]
-            factor = kap[:, g, :].unsqueeze(1).to_broadcast([P, P, PACK])
+        def differences(s):
+            made = []
             for u in range(TILES):
                 bank = late_bank()[:].rearrange("p (i j) -> p i j", i=PACK)
                 for i in range(PACK):
-                    for side, first in ((fwd, True), (bwd, False)):
+                    for side, first in ((fwd_ring[slot[s]], True), (bwd_ring[slot[s]], False)):
                         nc.tensor.matmul(
                             out=bank[:, i, :], lhsT=side[:, u, i, :], rhs=ident[:], is_transpose=True, start=first, stop=not first
                         )
-                if s > 9:
-                    for i in range(PACK):
-                        nc.scalar.activation(
-                            out=planes[:, i, u * P : (u + 1) * P], in_=bank[:, i, :], func=COPY, scale=kap[:, g, i : i + 1]
-                        )
-                else:
-                    nc.vector.tensor_tensor(
-                        out=grouped[:, u * P : (u + 1) * P, :], in0=bank.rearrange("p i j -> p j i"), in1=factor, op=MULT
-                    )
-            if s > 9:
-                nc.scalar.copy(
-                    out=grouped[:].rearrange("p (w e) t -> p w t e", e=4), in_=planes[:].rearrange("p t (w e) -> p w t e", e=4)
+                made.append(bank)
+            return made
+
+        def rates_on_vector(s, made):
+            c, g = steps[s]
+            factor = kap[:, g, :].unsqueeze(1).to_broadcast([P, P, PACK])
+            for u, bank in enumerate(made):
+                nc.vector.tensor_tensor(
+                    out=h_bf[c % 2][:, g, u * P : (u + 1) * P, :], in0=bank.rearrange("p i j -> p j i"), in1=factor, op=MULT
                 )
-            hw[c, g] = held([P, JC], U32, f"hw{c}{g}")
-            hs[c, g] = held([P, JC], U8, f"hs{c}{g}")
+
+        def rates_on_scalar(s, made):
+            c, g = steps[s]
+            for u, bank in enumerate(made):
+                for i in range(PACK):
+                    nc.scalar.activation(
+                        out=planes[:, i, u * P : (u + 1) * P], in_=bank[:, i, :], func=COPY, scale=kap[:, g, i : i + 1]
+                    )
+            nc.scalar.copy(
+                out=h_bf[c % 2][:, g].rearrange("p (w e) t -> p w t e", e=4),
+                in_=planes[:].rearrange("p t (w e) -> p w t e", e=4),
+            )
+
+        def quantize_h(c, g0, g1):
             nc.vector.quantize_mx(
-                out=hw[c, g][:].bitcast(FP8X4), scales=hs[c, g][:], in_=grouped[:].rearrange("p j t -> p (j t)")
+                out=hw[c][:, g0:g1].rearrange("p g j -> p (g j)").bitcast(FP8X4),
+                scales=hs[c][:, g0:g1].rearrange("p g j -> p (g j)"),
+                in_=h_bf[c % 2][:, g0:g1].rearrange("p g j t -> p (g j t)"),
             )
 
         def species(c, n0, n1):
@@ -246,8 +256,8 @@ def tile_list_reversible_reaction_rates_kernel(
                             out=bank[:, n - n0, j0 : j0 + P],
                             lhsT=wsw[:, g, 2 * n * P : 2 * (n + 1) * P].bitcast(FP4X4),
                             lhsT_scale=wss[:, g, n * P // 4 : (n + 1) * P // 4].bitcast(U8),
-                            rhs=hw[c, g][:, j0 : j0 + P].bitcast(FP8X4),
-                            rhs_scale=hs[c, g][:, j0 : j0 + P],
+                            rhs=hw[c][:, g, j0 : j0 + P].bitcast(FP8X4),
+                            rhs_scale=hs[c][:, g, j0 : j0 + P],
                             start=(g == 0),
                             stop=(g == GROUPS - 1),
                         )
@@ -270,32 +280,40 @@ def tile_list_reversible_reaction_rates_kernel(
         forward(0)
         backward(1)
         forward(2)
-        net_rates(0)
+        rates_on_vector(0, differences(0))
+        quantize_h(0, 0, 1)
         forward(1)
-        net_rates(1)
-        net_rates(2)
-        place(0, 0, 2)
+        rates_on_vector(1, differences(1))
+        quantize_h(0, 1, 2)
+        rates_on_vector(2, differences(2))
+        place(0, 0, 1)
+        place(0, 1, 2)
         backward(3)
         forward(3)
         place(0, 2, 3)
         backward(4)
         forward(4)
-        for c in range(1, CHUNKS - 1):
+        last = CHUNKS - 1
+        for c in range(1, last):
             s = 2 * c + 1
-            net_rates(s)
+            rates_on_vector(s, differences(s))
+            quantize_h(c, 0, 2)
             backward(s + 2)
             place(c - 1, 3, 4)
             forward(s + 2)
-            place(c, 0, 1)
-            net_rates(s + 1)
-            place(c, 1, 3 if c + 2 < CHUNKS else 2)
-            if s + 3 < len(steps):
+            if c + 1 < last:
+                place(c, 0, 1)
+                rates_on_vector(s + 1, differences(s + 1))
+                place(c, 1, 3)
                 backward(s + 3)
                 forward(s + 3)
-        last = CHUNKS - 1
-        net_rates(len(steps) - 1)
-        place(last - 1, 2, 3)
-        species(last - 1, 3, 4)
+            else:
+                place(c, 0, 2)
+                rates_on_scalar(s + 1, differences(s + 1))
+        rates_on_vector(len(steps) - 1, differences(len(steps) - 1))
+        quantize_h(last, 0, 2)
+        species(last - 1, 2, 4)
+        scatter(2, (last - 1) * JC, last * JC)
         place(last, 0, 1)
         place(last, 1, 3)
         species(last, 3, 4)

@@ -212,11 +212,17 @@ def tile_list_reversible_reaction_rates_kernel(
             made = []
             for u in range(TILES):
                 bank = late_bank()[:].rearrange("p (i j) -> p i j", i=PACK)
-                for i in range(PACK):
-                    for side, first in ((fwd_ring[slot[s]], True), (bwd_ring[slot[s]], False)):
-                        nc.tensor.matmul(
-                            out=bank[:, i, :], lhsT=side[:, u, i, :], rhs=ident[:], is_transpose=True, start=first, stop=not first
-                        )
+                sides = (bwd_ring[slot[s]], fwd_ring[slot[s]])
+                turns = [(i, sides[(k + u) % 2]) for i in range(PACK) for k in range(2)]
+                for k, (i, side) in enumerate(turns):
+                    nc.tensor.matmul(
+                        out=bank[:, i, :],
+                        lhsT=side[:, u, i, :],
+                        rhs=ident[:],
+                        is_transpose=True,
+                        start=k == 0,
+                        stop=k == len(turns) - 1,
+                    )
                 made.append(bank)
             return made
 
@@ -258,8 +264,8 @@ def tile_list_reversible_reaction_rates_kernel(
                             lhsT_scale=wss[:, g, n * P // 4 : (n + 1) * P // 4].bitcast(U8),
                             rhs=hw[c][:, g, j0 : j0 + P].bitcast(FP8X4),
                             rhs_scale=hs[c][:, g, j0 : j0 + P],
-                            start=(g == 0),
-                            stop=(g == GROUPS - 1),
+                            start=(n, j0, g) == (n0, 0, 0),
+                            stop=(n, j0, g) == (n1 - 1, JC - P, GROUPS - 1),
                         )
             nc.scalar.copy(out=y[:, n0:n1, c * JC : (c + 1) * JC], in_=bank[:, : n1 - n0, :])
 

@@ -62,11 +62,9 @@ def tile_list_reversible_reaction_rates_kernel(
         nc.vector.memset(tabs[:], 0)
         nc.vector.memset(wbs[:], 0)
         nc.vector.memset(wss[:], 0)
-        for n in range(NT // 2):
+        for n in range(NT):
             nc.vector.memset(store[n][:].bitcast(I32), 0)
         make_identity(nc, ident[:])
-        for n in range(NT // 2, NT):
-            nc.gpsimd.memset(store[n][:].bitcast(I32), 0)
 
         def load_wbw(g):
             rows = wb_words.rearrange("a p c i -> p a (c i)")[:, :, g * KP * 4 : (g + 1) * KP * 4]
@@ -84,14 +82,14 @@ def tile_list_reversible_reaction_rates_kernel(
                 nc.scalar.dma_start(out=dst[32 * q : 32 * q + 8, :], in_=src[:, 4 * q : 4 * q + 4, :].bitcast(I32))
 
         nc.sync.dma_start(idx[:], offs)
-        load_tabw(0)
         load_packed(tabs, tab_scales)
-        load_tabw(1)
         load_packed(wbs, wb_scales)
+        nc.scalar.dma_start(out=kap[:], in_=kappa.rearrange("(g p t) -> p g t", g=GROUPS, t=PACK))
+        load_tabw(0)
+        load_tabw(1)
         load_wbw(0)
         load_wf(*pieces[0])
         load_wf(*pieces[1])
-        nc.scalar.dma_start(out=kap[:], in_=kappa.rearrange("(g p t) -> p g t", g=GROUPS, t=PACK))
         load_wbw(1)
         load_wf(*pieces[2])
         load_wf(*pieces[3])
@@ -115,11 +113,6 @@ def tile_list_reversible_reaction_rates_kernel(
         def gather_scales(j0, j1):
             nc.vector.tensor_copy(out=vs[:, j0:j1], in_=tabs[:].bitcast(U8).indirect(entries(idx, j0, j1)))
 
-        for half in range(2):
-            lo, hi = half * S // 2, (half + 1) * S // 2
-            gather_words(0, lo, hi)
-            gather_scales(lo, hi)
-            gather_words(1, lo, hi)
 
         wfw = {(g, a): held([P, KP], U32, f"wfw{g}{a}") for g in range(GROUPS) for a in range(PASSES)}
         wfs = {(g, a): held([P, KP], U8, f"wfs{g}{a}") for g in range(GROUPS) for a in range(PASSES)}
@@ -152,8 +145,6 @@ def tile_list_reversible_reaction_rates_kernel(
             quantize_wf(g, a, 0, KP // 2, low)
             quantize_wf(g, a, KP // 2, KP, high)
 
-        for piece in pieces:
-            quantize_wf(*piece, round_wf(*piece, False))
 
         banks = [psum.tile([P, KP], F32, name=f"bank{b}") for b in range(8)]
         fwd_ring = [held([P, TILES, PACK, P], F32, f"fwd{r}") for r in range(RING)]
@@ -178,29 +169,39 @@ def tile_list_reversible_reaction_rates_kernel(
         slot = SLOTS
         planes = held([P, PACK, JC], BF16, "planes")
         h_bf = [wf_bf[1, 1 - r][:].rearrange("p (g j) t -> p g j t", g=GROUPS) for r in range(2)]
+        half = [1, 0]
         hw = [held([P, GROUPS, JC], U32, f"hw{c}") for c in range(CHUNKS)]
         hs = [held([P, GROUPS, JC], U8, f"hs{c}") for c in range(CHUNKS)]
 
         def cells(c, u):
             return slice(c * JC + u * P, c * JC + (u + 1) * P)
 
-        def backward(s, on_vector=False):
+        def backward_tile(s, u):
             c, g = steps[s]
             group = slice(g * KP, (g + 1) * KP)
+            product(banks[u], cells(c, u), lambda a: wbw[g][:, a, :], lambda a: wbs[4 * a :, :].bitcast(U8)[:, group])
+            exp_out(bwd_ring[slot[s]][:, u], banks[u])
+
+        def negate(s, on_vector=False):
             bwd = bwd_ring[slot[s]]
-            for u in range(TILES):
-                product(banks[u], cells(c, u), lambda a: wbw[g][:, a, :], lambda a: wbs[4 * a :, :].bitcast(U8)[:, group])
-                exp_out(bwd[:, u], banks[u])
             if on_vector:
                 nc.vector.tensor_scalar(out=bwd[:], in0=bwd[:], scalar1=-1.0, scalar2=None, op0=MULT)
             else:
                 nc.scalar.activation(out=bwd[:], in_=bwd[:], func=COPY, scale=-1.0)
 
-        def forward(s):
-            c, g = steps[s]
+        def backward(s, on_vector=False):
             for u in range(TILES):
-                product(banks[TILES + u], cells(c, u), lambda a: wfw[g, a][:], lambda a: wfs[g, a][:])
-                exp_out(fwd_ring[slot[s]][:, u], banks[TILES + u])
+                backward_tile(s, u)
+            negate(s, on_vector)
+
+        def forward_tile(s, u):
+            c, g = steps[s]
+            product(banks[TILES + u], cells(c, u), lambda a: wfw[g, a][:], lambda a: wfs[g, a][:])
+            exp_out(fwd_ring[slot[s]][:, u], banks[TILES + u])
+
+        def forward(s):
+            for u in range(TILES):
+                forward_tile(s, u)
 
         late = []
 
@@ -213,7 +214,8 @@ def tile_list_reversible_reaction_rates_kernel(
             for u in range(TILES):
                 bank = late_bank()[:].rearrange("p (i j) -> p i j", i=PACK)
                 sides = (bwd_ring[slot[s]], fwd_ring[slot[s]])
-                turns = [(i, sides[(k + u) % 2]) for i in range(PACK) for k in range(2)]
+                lead = 0 if (u == 0 and s > 2) else 1
+                turns = [(i, sides[(k + lead) % 2]) for i in range(PACK) for k in range(2)]
                 for k, (i, side) in enumerate(turns):
                     nc.tensor.matmul(
                         out=bank[:, i, :],
@@ -228,10 +230,13 @@ def tile_list_reversible_reaction_rates_kernel(
 
         def rates_on_vector(s, made):
             c, g = steps[s]
-            factor = kap[:, g, :].unsqueeze(1).to_broadcast([P, P, PACK])
+            factor = kap[:, g, :].unsqueeze(1).unsqueeze(3).to_broadcast([P, P // 2, PACK, 2])
             for u, bank in enumerate(made):
                 nc.vector.tensor_tensor(
-                    out=h_bf[c % 2][:, g, u * P : (u + 1) * P, :], in0=bank.rearrange("p i j -> p j i"), in1=factor, op=MULT
+                    out=h_bf[c % 2][:, half[g], u * P : (u + 1) * P, :].rearrange("p (w e) i -> p w i e", e=2),
+                    in0=bank.rearrange("p i (w e) -> p w i e", e=2),
+                    in1=factor,
+                    op=MULT,
                 )
 
         def rates_on_scalar(s, made):
@@ -242,7 +247,7 @@ def tile_list_reversible_reaction_rates_kernel(
                         out=planes[:, i, u * P : (u + 1) * P], in_=bank[:, i, :], func=COPY, scale=kap[:, g, i : i + 1]
                     )
             nc.scalar.copy(
-                out=h_bf[c % 2][:, g].rearrange("p (w e) t -> p w t e", e=4),
+                out=h_bf[c % 2][:, half[g]].rearrange("p (w e) t -> p w t e", e=4),
                 in_=planes[:].rearrange("p t (w e) -> p w t e", e=4),
             )
 
@@ -257,15 +262,15 @@ def tile_list_reversible_reaction_rates_kernel(
             bank = late_bank()[:].rearrange("p (n j) -> p n j", j=JC)
             for n in range(n0, n1):
                 for j0 in range(0, JC, P):
-                    for g in range(GROUPS):
+                    for g in reversed(range(GROUPS)):
                         nc.tensor.matmul_mx(
                             out=bank[:, n - n0, j0 : j0 + P],
                             lhsT=wsw[:, g, 2 * n * P : 2 * (n + 1) * P].bitcast(FP4X4),
                             lhsT_scale=wss[:, g, n * P // 4 : (n + 1) * P // 4].bitcast(U8),
-                            rhs=hw[c][:, g, j0 : j0 + P].bitcast(FP8X4),
-                            rhs_scale=hs[c][:, g, j0 : j0 + P],
-                            start=(n, j0, g) == (n0, 0, 0),
-                            stop=(n, j0, g) == (n1 - 1, JC - P, GROUPS - 1),
+                            rhs=hw[c][:, half[g], j0 : j0 + P].bitcast(FP8X4),
+                            rhs_scale=hs[c][:, half[g], j0 : j0 + P],
+                            start=(n, j0, g) == (n0, 0, GROUPS - 1),
+                            stop=(n, j0, g) == (n1 - 1, JC - P, 0),
                         )
             nc.scalar.copy(out=y[:, n0:n1, c * JC : (c + 1) * JC], in_=bank[:, : n1 - n0, :])
 
@@ -281,16 +286,27 @@ def tile_list_reversible_reaction_rates_kernel(
             for n in range(n0, n1):
                 scatter(n, c * JC, (c + 1) * JC)
 
+        gather_words(0, 0 * S // 2, 1 * S // 2)
+        gather_scales(0 * S // 2, 1 * S // 2)
+        gather_words(1, 0 * S // 2, 1 * S // 2)
+        gather_words(0, 1 * S // 2, 2 * S // 2)
+        gather_scales(1 * S // 2, 2 * S // 2)
+        gather_words(1, 1 * S // 2, 2 * S // 2)
+        quantize_wf(*pieces[0], round_wf(*pieces[0], False))
+        quantize_wf(*pieces[1], round_wf(*pieces[1], False))
+        quantize_wf(*pieces[2], round_wf(*pieces[2], False))
+        quantize_wf(*pieces[3], round_wf(*pieces[3], False))
+        quantize_wf(*pieces[4], round_wf(*pieces[4], False))
         backward(0)
         backward(2)
         forward(0)
         backward(1)
         forward(2)
         rates_on_vector(0, differences(0))
-        quantize_h(0, 0, 1)
+        quantize_h(0, 1, 2)
         forward(1)
         rates_on_vector(1, differences(1))
-        quantize_h(0, 1, 2)
+        quantize_h(0, 0, 1)
         rates_on_vector(2, differences(2))
         place(0, 0, 1)
         place(0, 1, 2)

@@ -55,14 +55,14 @@ def tile_list_reversible_reaction_rates_kernel(
         wss = held([P, GROUPS, N // 4], I32, "wss")
         kap = held([P, GROUPS, PACK], F32, "kap")
         wg = held([P, S], F32, "wg")
-        store = [held([P, T2], F32, f"store{n}") for n in range(NT)]
+        store = [held([P, T2], F32, f"store{n}") for n in range(NT // 2)]
         ident = held([P, P], F32, "ident")
         y = held([P, NT, S], F32, "y")
 
-        nc.vector.memset(tabs[:], 0)
         nc.vector.memset(wbs[:], 0)
+        nc.vector.memset(tabs[:], 0)
         nc.vector.memset(wss[:], 0)
-        for n in range(NT):
+        for n in range(NT // 2):
             nc.vector.memset(store[n][:].bitcast(I32), 0)
         make_identity(nc, ident[:])
 
@@ -82,8 +82,8 @@ def tile_list_reversible_reaction_rates_kernel(
                 nc.scalar.dma_start(out=dst[32 * q : 32 * q + 8, :], in_=src[:, 4 * q : 4 * q + 4, :].bitcast(I32))
 
         nc.sync.dma_start(idx[:], offs)
-        load_packed(tabs, tab_scales)
         load_packed(wbs, wb_scales)
+        load_packed(tabs, tab_scales)
         nc.scalar.dma_start(out=kap[:], in_=kappa.rearrange("(g p t) -> p g t", g=GROUPS, t=PACK))
         load_tabw(0)
         load_tabw(1)
@@ -117,10 +117,12 @@ def tile_list_reversible_reaction_rates_kernel(
         wfw = {(g, a): held([P, KP], U32, f"wfw{g}{a}") for g in range(GROUPS) for a in range(PASSES)}
         wfs = {(g, a): held([P, KP], U8, f"wfs{g}{a}") for g in range(GROUPS) for a in range(PASSES)}
 
-        wf_bf = {(g, a): held([P, KP, PACK], BF16, f"wf_bf{g}{a}") for g in range(GROUPS) for a in range(PASSES)}
+        wf_bf = {(g, a, c0): held([P, c1 - c0, PACK], BF16, f"wf_bf{g}{a}{c0}") for g, a, c0, c1 in pieces[:3]}
+        for k, (g, a, c0, c1) in enumerate(pieces[3:]):
+            wf_bf[g, a, c0] = keep.tile([P, c1 - c0, PACK], BF16, name=f"wf_bf{g}{a}{c0}", tag=f"shared{k}", align_bytes=64)
 
         def round_wf(g, a, c0, c1, on_scalar):
-            grouped = wf_bf[g, a][:, c0:c1]
+            grouped = wf_bf[g, a, c0][:]
             dst = grouped[:].rearrange("p (u i) t -> p u t i", i=4)
             src = wf_raw[g, a, c0][:].rearrange("p t (u i) -> p u t i", i=4)
             if on_scalar:
@@ -168,8 +170,14 @@ def tile_list_reversible_reaction_rates_kernel(
         steps = [(c, g) for c in range(CHUNKS) for g in range(GROUPS)]
         slot = SLOTS
         planes = held([P, PACK, JC], BF16, "planes")
-        h_bf = [wf_bf[1, 1 - r][:].rearrange("p (g j) t -> p g j t", g=GROUPS) for r in range(2)]
-        half = [1, 0]
+        whole = [wf_bf[piece[:3]][:].rearrange("p (g j) t -> p g j t", g=GROUPS) for piece in pieces[:3]]
+        h_bf = {(c, g): whole[c - 1][:, g] for c in range(1, CHUNKS) for g in range(GROUPS)}
+        h_bf[0, 0], h_bf[0, 1] = wf_bf[pieces[4][:3]][:], wf_bf[pieces[3][:3]][:]
+
+        def clear_store(k):
+            store.append(keep.tile([P, T2], F32, name=f"store{len(store)}", tag=f"shared{k}", align_bytes=64))
+            nc.gpsimd.memset(store[-1][:].bitcast(I32), 0)
+
         hw = [held([P, GROUPS, JC], U32, f"hw{c}") for c in range(CHUNKS)]
         hs = [held([P, GROUPS, JC], U8, f"hs{c}") for c in range(CHUNKS)]
 
@@ -233,7 +241,7 @@ def tile_list_reversible_reaction_rates_kernel(
             factor = kap[:, g, :].unsqueeze(1).unsqueeze(3).to_broadcast([P, P // 2, PACK, 2])
             for u, bank in enumerate(made):
                 nc.vector.tensor_tensor(
-                    out=h_bf[c % 2][:, half[g], u * P : (u + 1) * P, :].rearrange("p (w e) i -> p w i e", e=2),
+                    out=h_bf[c, g][:, u * P : (u + 1) * P, :].rearrange("p (w e) i -> p w i e", e=2),
                     in0=bank.rearrange("p i (w e) -> p w i e", e=2),
                     in1=factor,
                     op=MULT,
@@ -247,7 +255,7 @@ def tile_list_reversible_reaction_rates_kernel(
                         out=planes[:, i, u * P : (u + 1) * P], in_=bank[:, i, :], func=COPY, scale=kap[:, g, i : i + 1]
                     )
             nc.scalar.copy(
-                out=h_bf[c % 2][:, half[g]].rearrange("p (w e) t -> p w t e", e=4),
+                out=h_bf[c, g].rearrange("p (w e) t -> p w t e", e=4),
                 in_=planes[:].rearrange("p t (w e) -> p w t e", e=4),
             )
 
@@ -255,7 +263,7 @@ def tile_list_reversible_reaction_rates_kernel(
             nc.vector.quantize_mx(
                 out=hw[c][:, g0:g1].rearrange("p g j -> p (g j)").bitcast(FP8X4),
                 scales=hs[c][:, g0:g1].rearrange("p g j -> p (g j)"),
-                in_=h_bf[c % 2][:, g0:g1].rearrange("p g j t -> p (g j t)"),
+                in_=h_bf[c, g0].rearrange("p j t -> p (j t)") if g1 - g0 == 1 else whole[c - 1].rearrange("p g j t -> p (g j t)"),
             )
 
         def species(c, n0, n1):
@@ -267,8 +275,8 @@ def tile_list_reversible_reaction_rates_kernel(
                             out=bank[:, n - n0, j0 : j0 + P],
                             lhsT=wsw[:, g, 2 * n * P : 2 * (n + 1) * P].bitcast(FP4X4),
                             lhsT_scale=wss[:, g, n * P // 4 : (n + 1) * P // 4].bitcast(U8),
-                            rhs=hw[c][:, half[g], j0 : j0 + P].bitcast(FP8X4),
-                            rhs_scale=hs[c][:, half[g], j0 : j0 + P],
+                            rhs=hw[c][:, g, j0 : j0 + P].bitcast(FP8X4),
+                            rhs_scale=hs[c][:, g, j0 : j0 + P],
                             start=(n, j0, g) == (n0, 0, GROUPS - 1),
                             stop=(n, j0, g) == (n1 - 1, JC - P, 0),
                         )
@@ -303,10 +311,12 @@ def tile_list_reversible_reaction_rates_kernel(
         backward(1)
         forward(2)
         rates_on_vector(0, differences(0))
-        quantize_h(0, 1, 2)
+        quantize_h(0, 0, 1)
+        clear_store(1)
         forward(1)
         rates_on_vector(1, differences(1))
-        quantize_h(0, 0, 1)
+        quantize_h(0, 1, 2)
+        clear_store(0)
         rates_on_vector(2, differences(2))
         place(0, 0, 1)
         place(0, 1, 2)

@@ -23,13 +23,15 @@ PACK = 4
 KP = P * PACK
 PASSES = K // KP
 GROUPS = R // KP
+QUADRANTS = 4
 JC = 256
 CHUNKS = S // JC
 TILES = JC // P
 NT = N // P
 PER_COL = 16
+LINE = 2
 RING = 3
-SLOTS = [0, 2, 1, 2, 0, 1, 2, 0]
+BANKS = 8
 
 
 def tile_list_reversible_reaction_rates_kernel(
@@ -49,7 +51,9 @@ def tile_list_reversible_reaction_rates_kernel(
         tabs = held([P, T // 4], I32, "tabs")
         wbs = held([P, R // 4], I32, "wbs")
         wbw = [held([P, PASSES, KP], I32, f"wbw{g}") for g in range(GROUPS)]
-        pieces = [(0, 0, 0, KP), (0, 1, 0, KP), (1, 0, 0, KP), (1, 1, 0, KP // 2), (1, 1, KP // 2, KP)]
+        full_pieces = [(0, 0, 0, KP), (0, 1, 0, KP), (1, 0, 0, KP)]
+        half_pieces = [(1, 1, 0, KP // 2), (1, 1, KP // 2, KP)]
+        pieces = full_pieces + half_pieces
         wf_raw = {(g, a, c0): held([P, PACK, c1 - c0], F32, f"wf_raw{g}{a}{c0}") for g, a, c0, c1 in pieces}
         wsw = held([P, GROUPS, 2 * N], U8, "wsw")
         wss = held([P, GROUPS, N // 4], I32, "wss")
@@ -67,34 +71,29 @@ def tile_list_reversible_reaction_rates_kernel(
         make_identity(nc, ident[:])
 
         def load_wbw(g):
-            rows = wb_words.rearrange("a p c i -> p a (c i)")[:, :, g * KP * 4 : (g + 1) * KP * 4]
+            rows = wb_words.rearrange("a p c i -> p a (c i)")[:, :, g * KP * PACK : (g + 1) * KP * PACK]
             nc.sync.dma_start(out=wbw[g][:], in_=rows.bitcast(I32))
 
         def load_wf(g, a, c0, c1):
             rows = wf[a * KP : (a + 1) * KP, g * KP + c0 : g * KP + c1]
             nc.sync.dma_start(out=wf_raw[g, a, c0][:], in_=rows.rearrange("(p i) c -> p i c", i=PACK))
 
-        def load_tabw(a):
-            nc.sync.dma_start(out=tabw[a][:], in_=tab_words[a].rearrange("p t i -> p (t i)").bitcast(I32))
-
-        def load_packed(dst, src):
-            for q in range(4):
+        def load_scale_rows(dst, src):
+            for q in range(QUADRANTS):
                 nc.scalar.dma_start(out=dst[32 * q : 32 * q + 8, :], in_=src[:, 4 * q : 4 * q + 4, :].bitcast(I32))
 
         nc.sync.dma_start(idx[:], offs)
-        load_packed(wbs, wb_scales)
-        load_packed(tabs, tab_scales)
+        load_scale_rows(wbs, wb_scales)
+        load_scale_rows(tabs, tab_scales)
         nc.scalar.dma_start(out=kap[:], in_=kappa.rearrange("(g p t) -> p g t", g=GROUPS, t=PACK))
-        load_tabw(0)
-        load_tabw(1)
-        load_wbw(0)
-        load_wf(*pieces[0])
-        load_wf(*pieces[1])
-        load_wbw(1)
-        load_wf(*pieces[2])
-        load_wf(*pieces[3])
-        load_wf(*pieces[4])
-        for q in range(4):
+        for a in range(PASSES):
+            nc.sync.dma_start(out=tabw[a][:], in_=tab_words[a].rearrange("p t i -> p (t i)").bitcast(I32))
+        for g in range(GROUPS):
+            load_wbw(g)
+            for piece in pieces:
+                if piece[0] == g:
+                    load_wf(*piece)
+        for q in range(QUADRANTS):
             rows = ws_scales[:, 4 * q : 4 * q + 4, :].rearrange("g q c -> q g c")
             nc.sync.dma_start(out=wss[32 * q : 32 * q + 4, :, :], in_=rows.bitcast(I32))
         nc.sync.dma_start(out=wsw[:].bitcast(I32), in_=ws_words.rearrange("g p c -> p g c").bitcast(I32))
@@ -103,6 +102,36 @@ def tile_list_reversible_reaction_rates_kernel(
 
         vw = [held([P, S], U32, f"vw{a}") for a in range(PASSES)]
         vs = held([P, S], U8, "vs")
+        wfw = {(g, a): held([P, KP], U32, f"wfw{g}{a}") for g in range(GROUPS) for a in range(PASSES)}
+        wfs = {(g, a): held([P, KP], U8, f"wfs{g}{a}") for g in range(GROUPS) for a in range(PASSES)}
+        wf_bf = {(g, a, c0): held([P, c1 - c0, PACK], BF16, f"wf_bf{g}{a}{c0}") for g, a, c0, c1 in full_pieces}
+        for k, (g, a, c0, c1) in enumerate(half_pieces):
+            wf_bf[g, a, c0] = keep.tile([P, c1 - c0, PACK], BF16, name=f"wf_bf{g}{a}{c0}", tag=f"shared{k}", align_bytes=64)
+
+        banks = [psum.tile([P, KP], F32, name=f"bank{b}") for b in range(BANKS)]
+        fwd_ring = [held([P, TILES, PACK, P], F32, f"fwd{r}") for r in range(RING)]
+        bwd_ring = [held([P, TILES, PACK, P], F32, f"bwd{r}") for r in range(RING)]
+        planes = held([P, PACK, JC], BF16, "planes")
+        hw = [held([P, GROUPS, JC], U32, f"hw{c}") for c in range(CHUNKS)]
+        hs = [held([P, GROUPS, JC], U8, f"hs{c}") for c in range(CHUNKS)]
+
+        h_pair = {
+            c: wf_bf[piece[:3]][:].rearrange("p (g j) t -> p g j t", g=GROUPS) for c, piece in enumerate(full_pieces, start=1)
+        }
+        h_bf = {(c, g): h_pair[c][:, g] for c in h_pair for g in range(GROUPS)}
+        for g in range(GROUPS):
+            h_bf[0, g] = wf_bf[half_pieces[GROUPS - 1 - g][:3]][:]
+
+        opening = [(0, 0), (1, 0), (0, 1)]
+        rest = [(c, g) for c in range(1, CHUNKS) for g in range(GROUPS) if (c, g) not in opening]
+        slot = {step: k for k, step in enumerate(opening)}
+        slot.update({step: (RING - 1 + k) % RING for k, step in enumerate(rest)})
+
+        turn = []
+
+        def next_bank():
+            turn.append(banks[BANKS // 2 + len(turn) % (BANKS // 2)])
+            return turn[-1]
 
         def entries(lst, j0, j1):
             return lst[:, j0 // PER_COL : j1 // PER_COL]
@@ -110,124 +139,58 @@ def tile_list_reversible_reaction_rates_kernel(
         def gather_words(a, j0, j1):
             nc.vector.tensor_copy(out=vw[a][:, j0:j1], in_=tabw[a][:].bitcast(U32).indirect(entries(idx, j0, j1)))
 
-        def gather_scales(j0, j1):
-            nc.vector.tensor_copy(out=vs[:, j0:j1], in_=tabs[:].bitcast(U8).indirect(entries(idx, j0, j1)))
-
-
-        wfw = {(g, a): held([P, KP], U32, f"wfw{g}{a}") for g in range(GROUPS) for a in range(PASSES)}
-        wfs = {(g, a): held([P, KP], U8, f"wfs{g}{a}") for g in range(GROUPS) for a in range(PASSES)}
-
-        wf_bf = {(g, a, c0): held([P, c1 - c0, PACK], BF16, f"wf_bf{g}{a}{c0}") for g, a, c0, c1 in pieces[:3]}
-        for k, (g, a, c0, c1) in enumerate(pieces[3:]):
-            wf_bf[g, a, c0] = keep.tile([P, c1 - c0, PACK], BF16, name=f"wf_bf{g}{a}{c0}", tag=f"shared{k}", align_bytes=64)
-
-        def round_wf(g, a, c0, c1, on_scalar):
+        def prepare_wf(g, a, c0, c1):
             grouped = wf_bf[g, a, c0][:]
-            dst = grouped[:].rearrange("p (u i) t -> p u t i", i=4)
-            src = wf_raw[g, a, c0][:].rearrange("p t (u i) -> p u t i", i=4)
-            if on_scalar:
-                nc.scalar.copy(out=dst, in_=src)
-            else:
-                nc.vector.tensor_copy(out=dst, in_=src)
-            return grouped
-
-        def quantize_wf(g, a, c0, c1, grouped):
+            nc.vector.tensor_copy(
+                out=grouped.rearrange("p (u i) t -> p u t i", i=LINE),
+                in_=wf_raw[g, a, c0][:].rearrange("p t (u i) -> p u t i", i=LINE),
+            )
             nc.vector.quantize_mx(
                 out=wfw[g, a][:, c0:c1].bitcast(FP8X4),
                 scales=wfs[g, a][:, c0:c1],
-                in_=grouped[:].rearrange("p c t -> p (c t)"),
+                in_=grouped.rearrange("p c t -> p (c t)"),
             )
 
-        def prepare_whole(g, a, on_scalar):
-            quantize_wf(g, a, 0, KP, round_wf(g, a, 0, KP, on_scalar))
-
-        def prepare_shared(g, a):
-            low = round_wf(g, a, 0, KP // 2, False)
-            high = round_wf(g, a, KP // 2, KP, True)
-            quantize_wf(g, a, 0, KP // 2, low)
-            quantize_wf(g, a, KP // 2, KP, high)
-
-
-        banks = [psum.tile([P, KP], F32, name=f"bank{b}") for b in range(8)]
-        fwd_ring = [held([P, TILES, PACK, P], F32, f"fwd{r}") for r in range(RING)]
-        bwd_ring = [held([P, TILES, PACK, P], F32, f"bwd{r}") for r in range(RING)]
-
-        def product(bank, cells, words, scales):
+        def exp_of_product(dst, bank, c, u, words, scales):
+            cells = slice(c * JC + u * P, c * JC + (u + 1) * P)
             for a in range(PASSES):
                 nc.tensor.matmul_mx(
                     out=bank[:],
                     lhsT=vw[a][:, cells].bitcast(FP8X4),
                     lhsT_scale=vs[4 * a :, cells],
-                    rhs=words(a).bitcast(FP8X4),
-                    rhs_scale=scales(a),
+                    rhs=words[a].bitcast(FP8X4),
+                    rhs_scale=scales[a],
                     start=(a == 0),
                     stop=(a == PASSES - 1),
                 )
+            nc.scalar.activation(out=dst, in_=bank[:].rearrange("p (m t) -> p t m", t=PACK), func=EXP)
 
-        def exp_out(dst, bank):
-            nc.scalar.activation(out=dst, in_=bank[:].rearrange("p (m i) -> p i m", i=PACK), func=EXP)
-
-        steps = [(c, g) for c in range(CHUNKS) for g in range(GROUPS)]
-        slot = SLOTS
-        planes = held([P, PACK, JC], BF16, "planes")
-        whole = [wf_bf[piece[:3]][:].rearrange("p (g j) t -> p g j t", g=GROUPS) for piece in pieces[:3]]
-        h_bf = {(c, g): whole[c - 1][:, g] for c in range(1, CHUNKS) for g in range(GROUPS)}
-        h_bf[0, 0], h_bf[0, 1] = wf_bf[pieces[4][:3]][:], wf_bf[pieces[3][:3]][:]
-
-        def clear_store(k):
-            store.append(keep.tile([P, T2], F32, name=f"store{len(store)}", tag=f"shared{k}", align_bytes=64))
-            nc.gpsimd.memset(store[-1][:].bitcast(I32), 0)
-
-        hw = [held([P, GROUPS, JC], U32, f"hw{c}") for c in range(CHUNKS)]
-        hs = [held([P, GROUPS, JC], U8, f"hs{c}") for c in range(CHUNKS)]
-
-        def cells(c, u):
-            return slice(c * JC + u * P, c * JC + (u + 1) * P)
-
-        def backward_tile(s, u):
-            c, g = steps[s]
-            group = slice(g * KP, (g + 1) * KP)
-            product(banks[u], cells(c, u), lambda a: wbw[g][:, a, :], lambda a: wbs[4 * a :, :].bitcast(U8)[:, group])
-            exp_out(bwd_ring[slot[s]][:, u], banks[u])
-
-        def negate(s, on_vector=False):
-            bwd = bwd_ring[slot[s]]
-            if on_vector:
-                nc.vector.tensor_scalar(out=bwd[:], in0=bwd[:], scalar1=-1.0, scalar2=None, op0=MULT)
-            else:
-                nc.scalar.activation(out=bwd[:], in_=bwd[:], func=COPY, scale=-1.0)
-
-        def backward(s, on_vector=False):
+        def backward(c, g):
+            bwd = bwd_ring[slot[c, g]]
+            words = [wbw[g][:, a, :] for a in range(PASSES)]
+            scales = [wbs[4 * a :, :].bitcast(U8)[:, g * KP : (g + 1) * KP] for a in range(PASSES)]
             for u in range(TILES):
-                backward_tile(s, u)
-            negate(s, on_vector)
+                exp_of_product(bwd[:, u], banks[u], c, u, words, scales)
+            nc.scalar.activation(out=bwd[:], in_=bwd[:], func=COPY, scale=-1.0)
 
-        def forward_tile(s, u):
-            c, g = steps[s]
-            product(banks[TILES + u], cells(c, u), lambda a: wfw[g, a][:], lambda a: wfs[g, a][:])
-            exp_out(fwd_ring[slot[s]][:, u], banks[TILES + u])
-
-        def forward(s):
+        def forward(c, g):
+            words = [wfw[g, a][:] for a in range(PASSES)]
+            scales = [wfs[g, a][:] for a in range(PASSES)]
             for u in range(TILES):
-                forward_tile(s, u)
+                exp_of_product(fwd_ring[slot[c, g]][:, u], banks[TILES + u], c, u, words, scales)
 
-        late = []
-
-        def late_bank():
-            late.append(banks[4 + len(late) % 4])
-            return late[-1]
-
-        def differences(s):
+        def differences(c, g):
             made = []
             for u in range(TILES):
-                bank = late_bank()[:].rearrange("p (i j) -> p i j", i=PACK)
-                sides = (bwd_ring[slot[s]], fwd_ring[slot[s]])
-                lead = 0 if (u == 0 and s > 2) else 1
-                turns = [(i, sides[(k + lead) % 2]) for i in range(PACK) for k in range(2)]
-                for k, (i, side) in enumerate(turns):
+                bank = next_bank()[:].rearrange("p (t j) -> p t j", t=PACK)
+                sides = [fwd_ring[slot[c, g]], bwd_ring[slot[c, g]]]
+                if u == 0 and (c, g) in rest:
+                    sides.reverse()
+                turns = [(t, side) for t in range(PACK) for side in sides]
+                for k, (t, side) in enumerate(turns):
                     nc.tensor.matmul(
-                        out=bank[:, i, :],
-                        lhsT=side[:, u, i, :],
+                        out=bank[:, t, :],
+                        lhsT=side[:, u, t, :],
                         rhs=ident[:],
                         is_transpose=True,
                         start=k == 0,
@@ -236,38 +199,46 @@ def tile_list_reversible_reaction_rates_kernel(
                 made.append(bank)
             return made
 
-        def rates_on_vector(s, made):
-            c, g = steps[s]
+        def rates_on_vector(c, g):
             factor = kap[:, g, :].unsqueeze(1).unsqueeze(3).to_broadcast([P, P // 2, PACK, 2])
-            for u, bank in enumerate(made):
+            for u, bank in enumerate(differences(c, g)):
                 nc.vector.tensor_tensor(
-                    out=h_bf[c, g][:, u * P : (u + 1) * P, :].rearrange("p (w e) i -> p w i e", e=2),
-                    in0=bank.rearrange("p i (w e) -> p w i e", e=2),
+                    out=h_bf[c, g][:, u * P : (u + 1) * P, :].rearrange("p (w e) t -> p w t e", e=2),
+                    in0=bank.rearrange("p t (w e) -> p w t e", e=2),
                     in1=factor,
                     op=MULT,
                 )
 
-        def rates_on_scalar(s, made):
-            c, g = steps[s]
-            for u, bank in enumerate(made):
-                for i in range(PACK):
+        def rates_on_scalar(c, g):
+            for u, bank in enumerate(differences(c, g)):
+                for t in range(PACK):
                     nc.scalar.activation(
-                        out=planes[:, i, u * P : (u + 1) * P], in_=bank[:, i, :], func=COPY, scale=kap[:, g, i : i + 1]
+                        out=planes[:, t, u * P : (u + 1) * P], in_=bank[:, t, :], func=COPY, scale=kap[:, g, t : t + 1]
                     )
             nc.scalar.copy(
-                out=h_bf[c, g].rearrange("p (w e) t -> p w t e", e=4),
-                in_=planes[:].rearrange("p t (w e) -> p w t e", e=4),
+                out=h_bf[c, g].rearrange("p (w e) t -> p w t e", e=LINE),
+                in_=planes[:].rearrange("p t (w e) -> p w t e", e=LINE),
             )
 
-        def quantize_h(c, g0, g1):
+        def quantize_group(c, g):
             nc.vector.quantize_mx(
-                out=hw[c][:, g0:g1].rearrange("p g j -> p (g j)").bitcast(FP8X4),
-                scales=hs[c][:, g0:g1].rearrange("p g j -> p (g j)"),
-                in_=h_bf[c, g0].rearrange("p j t -> p (j t)") if g1 - g0 == 1 else whole[c - 1].rearrange("p g j t -> p (g j t)"),
+                out=hw[c][:, g].bitcast(FP8X4), scales=hs[c][:, g], in_=h_bf[c, g].rearrange("p j t -> p (j t)")
             )
+
+        def quantize_chunk(c):
+            nc.vector.quantize_mx(
+                out=hw[c][:].rearrange("p g j -> p (g j)").bitcast(FP8X4),
+                scales=hs[c][:].rearrange("p g j -> p (g j)"),
+                in_=h_pair[c].rearrange("p g j t -> p (g j t)"),
+            )
+
+        def clear_store_behind(g):
+            tag = f"shared{GROUPS - 1 - g}"
+            store.append(keep.tile([P, T2], F32, name=f"store{len(store)}", tag=tag, align_bytes=64))
+            nc.gpsimd.memset(store[-1][:].bitcast(I32), 0)
 
         def species(c, n0, n1):
-            bank = late_bank()[:].rearrange("p (n j) -> p n j", j=JC)
+            bank = next_bank()[:].rearrange("p (n j) -> p n j", j=JC)
             for n in range(n0, n1):
                 for j0 in range(0, JC, P):
                     for g in reversed(range(GROUPS)):
@@ -282,71 +253,68 @@ def tile_list_reversible_reaction_rates_kernel(
                         )
             nc.scalar.copy(out=y[:, n0:n1, c * JC : (c + 1) * JC], in_=bank[:, : n1 - n0, :])
 
-        def scatter(n, j0, j1):
+        def scatter(n, c0, c1):
+            j0, j1 = c0 * JC, c1 * JC
             nc.vector.tensor_tensor(
                 out=store[n][:].indirect(entries(idx2, j0, j1)), in0=y[:, n, j0:j1], in1=wg[:, j0:j1], op=MULT
             )
-            if j1 == S:
+            if c1 == CHUNKS:
                 nc.sync.dma_start(out=out[n * P : (n + 1) * P, :], in_=store[n][:])
 
         def place(c, n0, n1):
             species(c, n0, n1)
             for n in range(n0, n1):
-                scatter(n, c * JC, (c + 1) * JC)
+                scatter(n, c, c + 1)
 
-        gather_words(0, 0 * S // 2, 1 * S // 2)
-        gather_scales(0 * S // 2, 1 * S // 2)
-        gather_words(1, 0 * S // 2, 1 * S // 2)
-        gather_words(0, 1 * S // 2, 2 * S // 2)
-        gather_scales(1 * S // 2, 2 * S // 2)
-        gather_words(1, 1 * S // 2, 2 * S // 2)
-        quantize_wf(*pieces[0], round_wf(*pieces[0], False))
-        quantize_wf(*pieces[1], round_wf(*pieces[1], False))
-        quantize_wf(*pieces[2], round_wf(*pieces[2], False))
-        quantize_wf(*pieces[3], round_wf(*pieces[3], False))
-        quantize_wf(*pieces[4], round_wf(*pieces[4], False))
-        backward(0)
-        backward(2)
-        forward(0)
-        backward(1)
-        forward(2)
-        rates_on_vector(0, differences(0))
-        quantize_h(0, 0, 1)
-        clear_store(1)
-        forward(1)
-        rates_on_vector(1, differences(1))
-        quantize_h(0, 1, 2)
-        clear_store(0)
-        rates_on_vector(2, differences(2))
+        for j0 in range(0, S, S // 2):
+            j1 = j0 + S // 2
+            gather_words(0, j0, j1)
+            nc.vector.tensor_copy(out=vs[:, j0:j1], in_=tabs[:].bitcast(U8).indirect(entries(idx, j0, j1)))
+            gather_words(1, j0, j1)
+        for piece in pieces:
+            prepare_wf(*piece)
+
+        backward(0, 0)
+        backward(1, 0)
+        forward(0, 0)
+        backward(0, 1)
+        forward(1, 0)
+        rates_on_vector(0, 0)
+        quantize_group(0, 0)
+        clear_store_behind(0)
+        forward(0, 1)
+        rates_on_vector(0, 1)
+        quantize_group(0, 1)
+        clear_store_behind(1)
+        rates_on_vector(1, 0)
         place(0, 0, 1)
         place(0, 1, 2)
-        backward(3)
-        forward(3)
+        backward(1, 1)
+        forward(1, 1)
         place(0, 2, 3)
-        backward(4)
-        forward(4)
+
         last = CHUNKS - 1
         for c in range(1, last):
-            s = 2 * c + 1
-            rates_on_vector(s, differences(s))
-            quantize_h(c, 0, 2)
-            backward(s + 2)
-            place(c - 1, 3, 4)
-            forward(s + 2)
+            backward(c + 1, 0)
+            forward(c + 1, 0)
+            rates_on_vector(c, 1)
+            quantize_chunk(c)
+            backward(c + 1, 1)
+            place(c - 1, NT - 1, NT)
+            forward(c + 1, 1)
             if c + 1 < last:
                 place(c, 0, 1)
-                rates_on_vector(s + 1, differences(s + 1))
-                place(c, 1, 3)
-                backward(s + 3)
-                forward(s + 3)
+                rates_on_vector(c + 1, 0)
+                place(c, 1, NT - 1)
             else:
-                place(c, 0, 2)
-                rates_on_scalar(s + 1, differences(s + 1))
-        rates_on_vector(len(steps) - 1, differences(len(steps) - 1))
-        quantize_h(last, 0, 2)
-        species(last - 1, 2, 4)
-        scatter(2, (last - 1) * JC, last * JC)
+                place(c, 0, NT // 2)
+                rates_on_scalar(c + 1, 0)
+
+        rates_on_vector(last, 1)
+        quantize_chunk(last)
+        species(last - 1, NT // 2, NT)
+        scatter(NT // 2, last - 1, last)
         place(last, 0, 1)
-        place(last, 1, 3)
-        species(last, 3, 4)
-        scatter(3, (last - 1) * JC, S)
+        place(last, 1, NT - 1)
+        species(last, NT - 1, NT)
+        scatter(NT - 1, last - 1, CHUNKS)

@@ -63,11 +63,11 @@ def tile_list_reversible_reaction_rates_kernel(
         ident = held([P, P], F32, "ident")
         y = held([P, NT, S], F32, "y")
 
-        nc.vector.memset(wbs[:], 0)
         nc.vector.memset(tabs[:], 0)
-        nc.vector.memset(wss[:], 0)
         for n in range(NT // 2):
             nc.vector.memset(store[n][:].bitcast(I32), 0)
+        nc.vector.memset(wbs[:], 0)
+        nc.vector.memset(wss[:], 0)
         make_identity(nc, ident[:])
 
         def load_wbw(g):
@@ -80,14 +80,13 @@ def tile_list_reversible_reaction_rates_kernel(
 
         def load_scale_rows(dst, src):
             for q in range(QUADRANTS):
-                nc.scalar.dma_start(out=dst[32 * q : 32 * q + 8, :], in_=src[:, 4 * q : 4 * q + 4, :].bitcast(I32))
+                nc.sync.dma_start(out=dst[32 * q : 32 * q + 8, :], in_=src[:, 4 * q : 4 * q + 4, :].bitcast(I32))
 
         nc.sync.dma_start(idx[:], offs)
-        load_scale_rows(wbs, wb_scales)
-        load_scale_rows(tabs, tab_scales)
         nc.scalar.dma_start(out=kap[:], in_=kappa.rearrange("(g p t) -> p g t", g=GROUPS, t=PACK))
         for a in range(PASSES):
             nc.sync.dma_start(out=tabw[a][:], in_=tab_words[a].rearrange("p t i -> p (t i)").bitcast(I32))
+            load_scale_rows(*[(tabs, tab_scales), (wbs, wb_scales)][a])
         for g in range(GROUPS):
             load_wbw(g)
             for piece in pieces:
@@ -266,10 +265,9 @@ def tile_list_reversible_reaction_rates_kernel(
             for n in range(n0, n1):
                 scatter(n, c, c + 1)
 
-        for j0 in range(0, S, S // 2):
-            j1 = j0 + S // 2
-            gather_words(0, j0, j1)
-            nc.vector.tensor_copy(out=vs[:, j0:j1], in_=tabs[:].bitcast(U8).indirect(entries(idx, j0, j1)))
+        gather_words(0, 0, S)
+        nc.vector.tensor_copy(out=vs[:], in_=tabs[:].bitcast(U8).indirect(idx[:]))
+        for j0, j1 in ((0, JC), (JC, 2 * JC), (2 * JC, S)):
             gather_words(1, j0, j1)
         for piece in pieces:
             prepare_wf(*piece)

@@ -30,7 +30,7 @@ TILES = JC // P
 NT = N // P
 PER_COL = 16
 LINE = 2
-RING = 3
+RING = 4
 BANKS = 8
 
 
@@ -47,8 +47,8 @@ def tile_list_reversible_reaction_rates_kernel(
 
         idx = held([P, S // PER_COL], U16, "idx")
         idx2 = held([P, S // PER_COL], U16, "idx2")
-        tabw = [held([P, T], I32, f"tabw{a}") for a in range(PASSES)]
-        tabs = held([P, T // 4], I32, "tabs")
+        tabw = [keep.tile([P, T], I32, name=f"tabw{a}", tag=f"table{a}", align_bytes=64) for a in range(PASSES)]
+        tabs = keep.tile([P, T // 4], I32, name="tabs", tag="table_scales", align_bytes=64)
         wbs = held([P, R // 4], I32, "wbs")
         wbw = [held([P, PASSES, KP], I32, f"wbw{g}") for g in range(GROUPS)]
         full_pieces = [(0, 0, 0, KP), (0, 1, 0, KP), (1, 0, 0, KP)]
@@ -89,9 +89,8 @@ def tile_list_reversible_reaction_rates_kernel(
             load_scale_rows(*[(tabs, tab_scales), (wbs, wb_scales)][a])
         for g in range(GROUPS):
             load_wbw(g)
-            for piece in pieces:
-                if piece[0] == g:
-                    load_wf(*piece)
+        for piece in pieces:
+            load_wf(*piece)
         for q in range(QUADRANTS):
             rows = ws_scales[:, 4 * q : 4 * q + 4, :].rearrange("g q c -> q g c")
             nc.sync.dma_start(out=wss[32 * q : 32 * q + 4, :, :], in_=rows.bitcast(I32))
@@ -109,7 +108,7 @@ def tile_list_reversible_reaction_rates_kernel(
 
         banks = [psum.tile([P, KP], F32, name=f"bank{b}") for b in range(BANKS)]
         fwd_ring = [held([P, TILES, PACK, P], F32, f"fwd{r}") for r in range(RING)]
-        bwd_ring = [held([P, TILES, PACK, P], F32, f"bwd{r}") for r in range(RING)]
+        bwd = {(c, g): held([P, TILES, PACK, P], F32, f"bwd{c}{g}") for c in range(CHUNKS) for g in range(GROUPS)}
         planes = held([P, PACK, JC], BF16, "planes")
         hw = [held([P, GROUPS, JC], U32, f"hw{c}") for c in range(CHUNKS)]
         hs = [held([P, GROUPS, JC], U8, f"hs{c}") for c in range(CHUNKS)]
@@ -121,16 +120,13 @@ def tile_list_reversible_reaction_rates_kernel(
         for g in range(GROUPS):
             h_bf[0, g] = wf_bf[half_pieces[GROUPS - 1 - g][:3]][:]
 
-        opening = [(0, 0), (1, 0), (0, 1)]
-        rest = [(c, g) for c in range(1, CHUNKS) for g in range(GROUPS) if (c, g) not in opening]
-        slot = {step: k for k, step in enumerate(opening)}
-        slot.update({step: (RING - 1 + k) % RING for k, step in enumerate(rest)})
+        products = []
+        fwd = {}
+        opened = {}
 
-        turn = []
-
-        def next_bank():
-            turn.append(banks[BANKS // 2 + len(turn) % (BANKS // 2)])
-            return turn[-1]
+        def product_bank():
+            products.append(banks[len(products) % (BANKS // 2)])
+            return products[-1]
 
         def entries(lst, j0, j1):
             return lst[:, j0 // PER_COL : j1 // PER_COL]
@@ -150,7 +146,8 @@ def tile_list_reversible_reaction_rates_kernel(
                 in_=grouped.rearrange("p c t -> p (c t)"),
             )
 
-        def exp_of_product(dst, bank, c, u, words, scales):
+        def exp_of_product(dst, c, u, words, scales):
+            bank = product_bank()
             cells = slice(c * JC + u * P, c * JC + (u + 1) * P)
             for a in range(PASSES):
                 nc.tensor.matmul_mx(
@@ -165,54 +162,66 @@ def tile_list_reversible_reaction_rates_kernel(
             nc.scalar.activation(out=dst, in_=bank[:].rearrange("p (m t) -> p t m", t=PACK), func=EXP)
 
         def backward(c, g):
-            bwd = bwd_ring[slot[c, g]]
             words = [wbw[g][:, a, :] for a in range(PASSES)]
             scales = [wbs[4 * a :, :].bitcast(U8)[:, g * KP : (g + 1) * KP] for a in range(PASSES)]
             for u in range(TILES):
-                exp_of_product(bwd[:, u], banks[u], c, u, words, scales)
-            nc.scalar.activation(out=bwd[:], in_=bwd[:], func=COPY, scale=-1.0)
+                exp_of_product(bwd[c, g][:, u], c, u, words, scales)
+
+        def negate_on_vector(c, g):
+            flat = bwd[c, g][:].rearrange("p u t m -> p (u t m)")
+            nc.vector.tensor_scalar(out=flat, in0=flat, scalar1=-1.0, scalar2=None, op0=MULT)
+
+        def negate_on_scalar(c, g):
+            for u in range(TILES):
+                nc.scalar.activation(out=bwd[c, g][:, u], in_=bwd[c, g][:, u], func=COPY, scale=-1.0)
 
         def forward(c, g):
+            fwd[c, g] = fwd_ring[len(fwd) % RING]
             words = [wfw[g, a][:] for a in range(PASSES)]
             scales = [wfs[g, a][:] for a in range(PASSES)]
             for u in range(TILES):
-                exp_of_product(fwd_ring[slot[c, g]][:, u], banks[TILES + u], c, u, words, scales)
+                exp_of_product(fwd[c, g][:, u], c, u, words, scales)
 
-        def differences(c, g):
-            made = []
-            for u in range(TILES):
-                bank = next_bank()[:].rearrange("p (t j) -> p t j", t=PACK)
-                sides = [fwd_ring[slot[c, g]], bwd_ring[slot[c, g]]]
-                if u == 0 and (c, g) in rest:
-                    sides.reverse()
-                turns = [(t, side) for t in range(PACK) for side in sides]
-                for k, (t, side) in enumerate(turns):
+        def turn_over(c, g, side, opens):
+            for k, bank in enumerate(opened[c, g]):
+                if c < CHUNKS // 2:
+                    blocks = [(k, t) for t in range(PACK)]
+                else:
+                    blocks = [(u, t) for t in (2 * k, 2 * k + 1) for u in range(TILES)]
+                for i, (u, t) in enumerate(blocks):
                     nc.tensor.matmul(
-                        out=bank[:, t, :],
+                        out=bank[:, i * P : (i + 1) * P],
                         lhsT=side[:, u, t, :],
                         rhs=ident[:],
                         is_transpose=True,
-                        start=k == 0,
-                        stop=k == len(turns) - 1,
+                        start=opens and i == 0,
+                        stop=not opens and i == len(blocks) - 1,
                     )
-                made.append(bank)
-            return made
+
+        def open_differences(c, g, first, second):
+            opened[c, g] = [banks[first], banks[second]]
+            turn_over(c, g, bwd[c, g], True)
+
+        def differences(c, g):
+            turn_over(c, g, fwd[c, g], False)
+            return opened[c, g]
 
         def rates_on_vector(c, g):
             factor = kap[:, g, :].unsqueeze(1).unsqueeze(3).to_broadcast([P, P // 2, PACK, 2])
             for u, bank in enumerate(differences(c, g)):
                 nc.vector.tensor_tensor(
                     out=h_bf[c, g][:, u * P : (u + 1) * P, :].rearrange("p (w e) t -> p w t e", e=2),
-                    in0=bank.rearrange("p t (w e) -> p w t e", e=2),
+                    in0=bank[:].rearrange("p (t w e) -> p w t e", t=PACK, e=2),
                     in1=factor,
                     op=MULT,
                 )
 
         def rates_on_scalar(c, g):
-            for u, bank in enumerate(differences(c, g)):
-                for t in range(PACK):
+            for k, bank in enumerate(differences(c, g)):
+                for i in range(2):
+                    t = 2 * k + i
                     nc.scalar.activation(
-                        out=planes[:, t, u * P : (u + 1) * P], in_=bank[:, t, :], func=COPY, scale=kap[:, g, t : t + 1]
+                        out=planes[:, t, :], in_=bank[:, i * JC : (i + 1) * JC], func=COPY, scale=kap[:, g, t : t + 1]
                     )
             nc.scalar.copy(
                 out=h_bf[c, g].rearrange("p (w e) t -> p w t e", e=LINE),
@@ -231,25 +240,19 @@ def tile_list_reversible_reaction_rates_kernel(
                 in_=h_pair[c].rearrange("p g j t -> p (g j t)"),
             )
 
-        def clear_store_behind(g):
-            tag = f"shared{GROUPS - 1 - g}"
-            store.append(keep.tile([P, T2], F32, name=f"store{len(store)}", tag=tag, align_bytes=64))
-            nc.gpsimd.memset(store[-1][:].bitcast(I32), 0)
-
-        def species(c, n0, n1):
-            bank = next_bank()[:].rearrange("p (n j) -> p n j", j=JC)
+        def species(c, n0, n1, b):
+            bank = banks[b][:].rearrange("p (n j) -> p n j", j=JC)
             for n in range(n0, n1):
-                for j0 in range(0, JC, P):
-                    for g in reversed(range(GROUPS)):
-                        nc.tensor.matmul_mx(
-                            out=bank[:, n - n0, j0 : j0 + P],
-                            lhsT=wsw[:, g, 2 * n * P : 2 * (n + 1) * P].bitcast(FP4X4),
-                            lhsT_scale=wss[:, g, n * P // 4 : (n + 1) * P // 4].bitcast(U8),
-                            rhs=hw[c][:, g, j0 : j0 + P].bitcast(FP8X4),
-                            rhs_scale=hs[c][:, g, j0 : j0 + P],
-                            start=(n, j0, g) == (n0, 0, GROUPS - 1),
-                            stop=(n, j0, g) == (n1 - 1, JC - P, 0),
-                        )
+                for g in reversed(range(GROUPS)):
+                    nc.tensor.matmul_mx(
+                        out=bank[:, n - n0, :],
+                        lhsT=wsw[:, g, 2 * n * P : 2 * (n + 1) * P].bitcast(FP4X4),
+                        lhsT_scale=wss[:, g, n * P // 4 : (n + 1) * P // 4].bitcast(U8),
+                        rhs=hw[c][:, g].bitcast(FP8X4),
+                        rhs_scale=hs[c][:, g],
+                        start=(n, g) == (n0, GROUPS - 1),
+                        stop=(n, g) == (n1 - 1, 0),
+                    )
             nc.scalar.copy(out=y[:, n0:n1, c * JC : (c + 1) * JC], in_=bank[:, : n1 - n0, :])
 
         def scatter(n, c0, c1):
@@ -260,8 +263,8 @@ def tile_list_reversible_reaction_rates_kernel(
             if c1 == CHUNKS:
                 nc.sync.dma_start(out=out[n * P : (n + 1) * P, :], in_=store[n][:])
 
-        def place(c, n0, n1):
-            species(c, n0, n1)
+        def place(c, n0, n1, b):
+            species(c, n0, n1, b)
             for n in range(n0, n1):
                 scatter(n, c, c + 1)
 
@@ -269,50 +272,60 @@ def tile_list_reversible_reaction_rates_kernel(
         nc.vector.tensor_copy(out=vs[:], in_=tabs[:].bitcast(U8).indirect(idx[:]))
         for j0, j1 in ((0, JC), (JC, 2 * JC), (2 * JC, S)):
             gather_words(1, j0, j1)
+        for tag in ("table0", "table_scales"):
+            store.append(keep.tile([P, T2], F32, name=f"store{len(store)}", tag=tag, align_bytes=64))
+            nc.gpsimd.memset(store[-1][:].bitcast(I32), 0)
         for piece in pieces:
             prepare_wf(*piece)
 
-        backward(0, 0)
-        backward(1, 0)
+        for c, g in ((0, 0), (1, 0), (0, 1), (1, 1)):
+            backward(c, g)
+            negate_on_vector(c, g)
+        backward(2, 0)
+        open_differences(0, 0, 4, 5)
+        backward(2, 1)
+        open_differences(1, 0, 6, 7)
+        backward(3, 0)
         forward(0, 0)
-        backward(0, 1)
         forward(1, 0)
+        negate_on_scalar(2, 0)
         rates_on_vector(0, 0)
         quantize_group(0, 0)
-        clear_store_behind(0)
+        rates_on_vector(1, 0)
+        negate_on_scalar(2, 1)
         forward(0, 1)
+        forward(1, 1)
+        open_differences(0, 1, 4, 5)
         rates_on_vector(0, 1)
         quantize_group(0, 1)
-        clear_store_behind(1)
-        rates_on_vector(1, 0)
-        place(0, 0, 1)
-        place(0, 1, 2)
-        backward(1, 1)
-        forward(1, 1)
-        place(0, 2, 3)
-
-        last = CHUNKS - 1
-        for c in range(1, last):
-            backward(c + 1, 0)
-            forward(c + 1, 0)
-            rates_on_vector(c, 1)
-            quantize_chunk(c)
-            backward(c + 1, 1)
-            place(c - 1, NT - 1, NT)
-            forward(c + 1, 1)
-            if c + 1 < last:
-                place(c, 0, 1)
-                rates_on_vector(c + 1, 0)
-                place(c, 1, NT - 1)
-            else:
-                place(c, 0, NT // 2)
-                rates_on_scalar(c + 1, 0)
-
-        rates_on_vector(last, 1)
-        quantize_chunk(last)
-        species(last - 1, NT // 2, NT)
-        scatter(NT // 2, last - 1, last)
-        place(last, 0, 1)
-        place(last, 1, NT - 1)
-        species(last, NT - 1, NT)
-        scatter(NT - 1, last - 1, CHUNKS)
+        open_differences(1, 1, 6, 7)
+        rates_on_vector(1, 1)
+        quantize_chunk(1)
+        forward(2, 0)
+        place(0, 0, 2, 4)
+        forward(2, 1)
+        place(0, 2, 4, 5)
+        open_differences(2, 0, 7, 4)
+        rates_on_scalar(2, 0)
+        place(1, 0, 2, 6)
+        open_differences(2, 1, 5, 6)
+        backward(3, 1)
+        rates_on_scalar(2, 1)
+        quantize_chunk(2)
+        forward(3, 0)
+        place(1, 2, 4, 5)
+        negate_on_scalar(3, 0)
+        open_differences(3, 0, 7, 4)
+        forward(3, 1)
+        rates_on_scalar(3, 0)
+        place(2, 0, 2, 7)
+        negate_on_scalar(3, 1)
+        open_differences(3, 1, 6, 5)
+        rates_on_scalar(3, 1)
+        quantize_chunk(3)
+        species(2, 2, 4, 6)
+        scatter(2, 2, 3)
+        place(3, 0, 2, 4)
+        species(3, 2, 4, 7)
+        scatter(2, 3, 4)
+        scatter(3, 2, 4)

@@ -54,7 +54,10 @@ def tile_list_reversible_reaction_rates_kernel(
         full_pieces = [(0, 0, 0, KP), (0, 1, 0, KP), (1, 0, 0, KP)]
         half_pieces = [(1, 1, 0, KP // 2), (1, 1, KP // 2, KP)]
         pieces = full_pieces + half_pieces
-        wf_raw = {(g, a, c0): held([P, PACK, c1 - c0], F32, f"wf_raw{g}{a}{c0}") for g, a, c0, c1 in pieces}
+        wf_raw = {
+            (g, a, c0): keep.tile([P, PACK, c1 - c0], F32, name=f"wf_raw{k}", tag=f"raw{k}", align_bytes=64)
+            for k, (g, a, c0, c1) in enumerate(pieces)
+        }
         wsw = held([P, GROUPS, 2 * N], U8, "wsw")
         wss = held([P, GROUPS, N // 4], I32, "wss")
         kap = held([P, GROUPS, PACK], F32, "kap")
@@ -64,9 +67,9 @@ def tile_list_reversible_reaction_rates_kernel(
         y = held([P, NT, S], F32, "y")
 
         nc.vector.memset(tabs[:], 0)
+        nc.vector.memset(wbs[:], 0)
         for n in range(NT // 2):
             nc.vector.memset(store[n][:].bitcast(I32), 0)
-        nc.vector.memset(wbs[:], 0)
         nc.vector.memset(wss[:], 0)
         make_identity(nc, ident[:])
 
@@ -120,9 +123,12 @@ def tile_list_reversible_reaction_rates_kernel(
         for g in range(GROUPS):
             h_bf[0, g] = wf_bf[half_pieces[GROUPS - 1 - g][:3]][:]
 
+        whole = [(a, 0, KP) for a in range(PASSES)]
         products = []
         fwd = {}
+        on_scalar = [(3, 0), (3, 1)]
         opened = {}
+        negated = {}
 
         def product_bank():
             products.append(banks[len(products) % (BANKS // 2)])
@@ -146,18 +152,18 @@ def tile_list_reversible_reaction_rates_kernel(
                 in_=grouped.rearrange("p c t -> p (c t)"),
             )
 
-        def exp_of_product(dst, c, u, words, scales):
+        def exp_of_product(dst, c, u, words, scales, parts):
             bank = product_bank()
             cells = slice(c * JC + u * P, c * JC + (u + 1) * P)
-            for a in range(PASSES):
+            for k, (a, c0, c1) in enumerate(parts):
                 nc.tensor.matmul_mx(
-                    out=bank[:],
+                    out=bank[:, c0:c1],
                     lhsT=vw[a][:, cells].bitcast(FP8X4),
                     lhsT_scale=vs[4 * a :, cells],
-                    rhs=words[a].bitcast(FP8X4),
-                    rhs_scale=scales[a],
-                    start=(a == 0),
-                    stop=(a == PASSES - 1),
+                    rhs=words[a][:, c0:c1].bitcast(FP8X4),
+                    rhs_scale=scales[a][:, c0:c1],
+                    start=k == 0,
+                    stop=k == len(parts) - 1,
                 )
             nc.scalar.activation(out=dst, in_=bank[:].rearrange("p (m t) -> p t m", t=PACK), func=EXP)
 
@@ -165,26 +171,40 @@ def tile_list_reversible_reaction_rates_kernel(
             words = [wbw[g][:, a, :] for a in range(PASSES)]
             scales = [wbs[4 * a :, :].bitcast(U8)[:, g * KP : (g + 1) * KP] for a in range(PASSES)]
             for u in range(TILES):
-                exp_of_product(bwd[c, g][:, u], c, u, words, scales)
+                exp_of_product(bwd[c, g][:, u], c, u, words, scales, whole)
 
-        def negate_on_vector(c, g):
-            flat = bwd[c, g][:].rearrange("p u t m -> p (u t m)")
-            nc.vector.tensor_scalar(out=flat, in0=flat, scalar1=-1.0, scalar2=None, op0=MULT)
+        def negated_tile(c, g, behind):
+            if behind is None:
+                negated[c, g] = bwd[c, g]
+            else:
+                negated[c, g] = keep.tile([P, TILES, PACK, P], F32, name=f"neg{c}{g}", tag=f"raw{behind}", align_bytes=64)
+            return negated[c, g]
 
-        def negate_on_scalar(c, g):
+        def negate_on_vector(c, g, behind=None):
+            nc.vector.tensor_scalar(
+                out=negated_tile(c, g, behind)[:].rearrange("p u t m -> p (u t m)"),
+                in0=bwd[c, g][:].rearrange("p u t m -> p (u t m)"),
+                scalar1=-1.0,
+                scalar2=None,
+                op0=MULT,
+            )
+
+        def negate_on_scalar(c, g, behind=None):
+            dst = negated_tile(c, g, behind)
             for u in range(TILES):
-                nc.scalar.activation(out=bwd[c, g][:, u], in_=bwd[c, g][:, u], func=COPY, scale=-1.0)
+                nc.scalar.activation(out=dst[:, u], in_=bwd[c, g][:, u], func=COPY, scale=-1.0)
 
-        def forward(c, g):
-            fwd[c, g] = fwd_ring[len(fwd) % RING]
+        def forward(c, g, tiles=range(TILES)):
+            fwd.setdefault((c, g), fwd_ring[len(fwd) % RING])
             words = [wfw[g, a][:] for a in range(PASSES)]
             scales = [wfs[g, a][:] for a in range(PASSES)]
-            for u in range(TILES):
-                exp_of_product(fwd[c, g][:, u], c, u, words, scales)
+            parts = [piece[1:] for piece in pieces if piece[0] == g] if c < CHUNKS // 2 else whole
+            for u in tiles:
+                exp_of_product(fwd[c, g][:, u], c, u, words, scales, parts)
 
         def turn_over(c, g, side, opens):
             for k, bank in enumerate(opened[c, g]):
-                if c < CHUNKS // 2:
+                if (c, g) not in on_scalar:
                     blocks = [(k, t) for t in range(PACK)]
                 else:
                     blocks = [(u, t) for t in (2 * k, 2 * k + 1) for u in range(TILES)]
@@ -200,7 +220,7 @@ def tile_list_reversible_reaction_rates_kernel(
 
         def open_differences(c, g, first, second):
             opened[c, g] = [banks[first], banks[second]]
-            turn_over(c, g, bwd[c, g], True)
+            turn_over(c, g, negated[c, g], True)
 
         def differences(c, g):
             turn_over(c, g, fwd[c, g], False)
@@ -216,13 +236,15 @@ def tile_list_reversible_reaction_rates_kernel(
                     op=MULT,
                 )
 
-        def rates_on_scalar(c, g):
+        def scale_on_scalar(c, g):
             for k, bank in enumerate(differences(c, g)):
                 for i in range(2):
                     t = 2 * k + i
                     nc.scalar.activation(
                         out=planes[:, t, :], in_=bank[:, i * JC : (i + 1) * JC], func=COPY, scale=kap[:, g, t : t + 1]
                     )
+
+        def interleave_on_scalar(c, g):
             nc.scalar.copy(
                 out=h_bf[c, g].rearrange("p (w e) t -> p w t e", e=LINE),
                 in_=planes[:].rearrange("p t (w e) -> p w t e", e=LINE),
@@ -240,8 +262,8 @@ def tile_list_reversible_reaction_rates_kernel(
                 in_=h_pair[c].rearrange("p g j t -> p (g j t)"),
             )
 
-        def species(c, n0, n1, b):
-            bank = banks[b][:].rearrange("p (n j) -> p n j", j=JC)
+        def species(c, n0, n1, b=None):
+            bank = (product_bank() if b is None else banks[b])[:].rearrange("p (n j) -> p n j", j=JC)
             for n in range(n0, n1):
                 for g in reversed(range(GROUPS)):
                     nc.tensor.matmul_mx(
@@ -263,7 +285,7 @@ def tile_list_reversible_reaction_rates_kernel(
             if c1 == CHUNKS:
                 nc.sync.dma_start(out=out[n * P : (n + 1) * P, :], in_=store[n][:])
 
-        def place(c, n0, n1, b):
+        def place(c, n0, n1, b=None):
             species(c, n0, n1, b)
             for n in range(n0, n1):
                 scatter(n, c, c + 1)
@@ -278,54 +300,65 @@ def tile_list_reversible_reaction_rates_kernel(
         for piece in pieces:
             prepare_wf(*piece)
 
-        for c, g in ((0, 0), (1, 0), (0, 1), (1, 1)):
-            backward(c, g)
-            negate_on_vector(c, g)
-        backward(2, 0)
+        backward(0, 0)
+        negate_on_vector(0, 0)
+        backward(0, 1)
+        negate_on_vector(0, 1, 0)
+        backward(1, 0)
+        backward(1, 1)
         open_differences(0, 0, 4, 5)
+        backward(2, 0)
         backward(2, 1)
-        open_differences(1, 0, 6, 7)
-        backward(3, 0)
+        open_differences(0, 1, 6, 7)
+        negate_on_scalar(1, 0)
         forward(0, 0)
         forward(1, 0)
-        negate_on_scalar(2, 0)
         rates_on_vector(0, 0)
         quantize_group(0, 0)
-        rates_on_vector(1, 0)
-        negate_on_scalar(2, 1)
         forward(0, 1)
-        forward(1, 1)
-        open_differences(0, 1, 4, 5)
         rates_on_vector(0, 1)
         quantize_group(0, 1)
+        forward(1, 1)
+        negate_on_scalar(1, 1, 2)
+        negate_on_scalar(2, 0, 3)
+        open_differences(1, 0, 4, 5)
+        rates_on_vector(1, 0)
+        place(0, 0, 1)
+        place(0, 1, 2)
+        forward(2, 0, [0])
         open_differences(1, 1, 6, 7)
         rates_on_vector(1, 1)
         quantize_chunk(1)
-        forward(2, 0)
-        place(0, 0, 2, 4)
+        negate_on_scalar(2, 1, 4)
+        forward(2, 0, [1])
         forward(2, 1)
-        place(0, 2, 4, 5)
-        open_differences(2, 0, 7, 4)
-        rates_on_scalar(2, 0)
-        place(1, 0, 2, 6)
-        open_differences(2, 1, 5, 6)
-        backward(3, 1)
-        rates_on_scalar(2, 1)
-        quantize_chunk(2)
-        forward(3, 0)
-        place(1, 2, 4, 5)
+        place(0, 2, 4, 4)
+        backward(3, 0)
+        open_differences(2, 0, 6, 7)
+        rates_on_vector(2, 0)
         negate_on_scalar(3, 0)
-        open_differences(3, 0, 7, 4)
+        forward(3, 0)
+        open_differences(2, 1, 4, 5)
+        rates_on_vector(2, 1)
+        quantize_chunk(2)
+        backward(3, 1)
+        place(1, 0, 1, 4)
+        place(1, 1, 2, 5)
+        place(1, 2, 4, 4)
+        open_differences(3, 0, 6, 7)
+        scale_on_scalar(3, 0)
         forward(3, 1)
-        rates_on_scalar(3, 0)
-        place(2, 0, 2, 7)
         negate_on_scalar(3, 1)
-        open_differences(3, 1, 6, 5)
-        rates_on_scalar(3, 1)
+        interleave_on_scalar(3, 0)
+        place(2, 0, 2, 6)
+        open_differences(3, 1, 5, 4)
+        scale_on_scalar(3, 1)
+        interleave_on_scalar(3, 1)
         quantize_chunk(3)
-        species(2, 2, 4, 6)
+        species(2, 2, 4, 5)
         scatter(2, 2, 3)
-        place(3, 0, 2, 4)
-        species(3, 2, 4, 7)
+        place(3, 0, 1, 7)
+        place(3, 1, 2, 6)
+        species(3, 2, 4, 4)
         scatter(2, 3, 4)
         scatter(3, 2, 4)

@@ -30,7 +30,6 @@ TILES = JC // P
 NT = N // P
 PER_COL = 16
 LINE = 2
-RING = 4
 BANKS = 8
 
 
@@ -49,8 +48,8 @@ def tile_list_reversible_reaction_rates_kernel(
         idx2 = held([P, S // PER_COL], U16, "idx2")
         tabw = [keep.tile([P, T], I32, name=f"tabw{a}", tag=f"table{a}", align_bytes=64) for a in range(PASSES)]
         tabs = keep.tile([P, T // 4], I32, name="tabs", tag="table_scales", align_bytes=64)
-        wbs = held([P, R // 4], I32, "wbs")
-        wbw = [held([P, PASSES, KP], I32, f"wbw{g}") for g in range(GROUPS)]
+        wbs = held([P, PASSES, R // 4], I32, "wbs")
+        wbw = {(g, a): held([P, KP], I32, f"wbw{g}{a}") for g in range(GROUPS) for a in range(PASSES)}
         full_pieces = [(0, 0, 0, KP), (0, 1, 0, KP), (1, 0, 0, KP)]
         half_pieces = [(1, 1, 0, KP // 2), (1, 1, KP // 2, KP)]
         pieces = full_pieces + half_pieces
@@ -64,7 +63,7 @@ def tile_list_reversible_reaction_rates_kernel(
         wg = held([P, S], F32, "wg")
         store = [held([P, T2], F32, f"store{n}") for n in range(NT // 2)]
         ident = held([P, P], F32, "ident")
-        y = held([P, NT, S], F32, "y")
+        y = held([P, NT * S], F32, "y")
 
         nc.vector.memset(tabs[:], 0)
         nc.vector.memset(wbs[:], 0)
@@ -73,30 +72,36 @@ def tile_list_reversible_reaction_rates_kernel(
         nc.vector.memset(wss[:], 0)
         make_identity(nc, ident[:])
 
-        def load_wbw(g):
-            rows = wb_words.rearrange("a p c i -> p a (c i)")[:, :, g * KP * PACK : (g + 1) * KP * PACK]
-            nc.sync.dma_start(out=wbw[g][:], in_=rows.bitcast(I32))
+        def load_wbw(g, a):
+            rows = wb_words[a].rearrange("p c i -> p (c i)")[:, g * KP * PACK : (g + 1) * KP * PACK]
+            nc.sync.dma_start(out=wbw[g, a][:], in_=rows.bitcast(I32))
 
         def load_wf(g, a, c0, c1):
             rows = wf[a * KP : (a + 1) * KP, g * KP + c0 : g * KP + c1]
             nc.sync.dma_start(out=wf_raw[g, a, c0][:], in_=rows.rearrange("(p i) c -> p i c", i=PACK))
 
-        def load_scale_rows(dst, src):
+        def load_planes(dst, src):
             for q in range(QUADRANTS):
-                nc.sync.dma_start(out=dst[32 * q : 32 * q + 8, :], in_=src[:, 4 * q : 4 * q + 4, :].bitcast(I32))
+                rows = src[:, 4 * q : 4 * q + 4, :].rearrange("a i c -> i a c")
+                nc.sync.dma_start(out=dst[32 * q : 32 * q + 4, :, :], in_=rows.bitcast(I32))
+
+        def load_table(a):
+            nc.sync.dma_start(out=tabw[a][:], in_=tab_words[a].rearrange("p t i -> p (t i)").bitcast(I32))
 
         nc.sync.dma_start(idx[:], offs)
-        nc.scalar.dma_start(out=kap[:], in_=kappa.rearrange("(g p t) -> p g t", g=GROUPS, t=PACK))
+        load_table(0)
+        for q in range(QUADRANTS):
+            nc.sync.dma_start(out=tabs[32 * q : 32 * q + 8, :], in_=tab_scales[:, 4 * q : 4 * q + 4, :].bitcast(I32))
+        load_planes(wbs, wb_scales)
+        load_wbw(0, 0)
+        load_table(1)
+        load_wbw(0, 1)
         for a in range(PASSES):
-            nc.sync.dma_start(out=tabw[a][:], in_=tab_words[a].rearrange("p t i -> p (t i)").bitcast(I32))
-            load_scale_rows(*[(tabs, tab_scales), (wbs, wb_scales)][a])
-        for g in range(GROUPS):
-            load_wbw(g)
+            load_wbw(1, a)
         for piece in pieces:
             load_wf(*piece)
-        for q in range(QUADRANTS):
-            rows = ws_scales[:, 4 * q : 4 * q + 4, :].rearrange("g q c -> q g c")
-            nc.sync.dma_start(out=wss[32 * q : 32 * q + 4, :, :], in_=rows.bitcast(I32))
+        nc.sync.dma_start(out=kap[:], in_=kappa.rearrange("(g p t) -> p g t", g=GROUPS, t=PACK))
+        load_planes(wss, ws_scales)
         nc.sync.dma_start(out=wsw[:].bitcast(I32), in_=ws_words.rearrange("g p c -> p g c").bitcast(I32))
         nc.sync.dma_start(idx2[:], offs2)
         nc.sync.dma_start(out=wg[:], in_=wgo)
@@ -105,28 +110,22 @@ def tile_list_reversible_reaction_rates_kernel(
         vs = held([P, S], U8, "vs")
         wfw = {(g, a): held([P, KP], U32, f"wfw{g}{a}") for g in range(GROUPS) for a in range(PASSES)}
         wfs = {(g, a): held([P, KP], U8, f"wfs{g}{a}") for g in range(GROUPS) for a in range(PASSES)}
-        wf_bf = {(g, a, c0): held([P, c1 - c0, PACK], BF16, f"wf_bf{g}{a}{c0}") for g, a, c0, c1 in full_pieces}
-        for k, (g, a, c0, c1) in enumerate(half_pieces):
-            wf_bf[g, a, c0] = keep.tile([P, c1 - c0, PACK], BF16, name=f"wf_bf{g}{a}{c0}", tag=f"shared{k}", align_bytes=64)
+        wf_bf = {}
 
         banks = [psum.tile([P, KP], F32, name=f"bank{b}") for b in range(BANKS)]
-        fwd_ring = [held([P, TILES, PACK, P], F32, f"fwd{r}") for r in range(RING)]
-        bwd = {(c, g): held([P, TILES, PACK, P], F32, f"bwd{c}{g}") for c in range(CHUNKS) for g in range(GROUPS)}
+        steps = [(c, g) for c in range(CHUNKS) for g in range(GROUPS)]
+        fwd = {(c, g): keep.tile([P, TILES, PACK, P], F32, name=f"fwd{c}{g}", tag=f"fwd{c}{g}", align_bytes=64) for c, g in steps}
+        bwd = {(c, g): held([P, TILES, PACK, P], F32, f"bwd{c}{g}") for c, g in steps}
         planes = held([P, PACK, JC], BF16, "planes")
         hw = [held([P, GROUPS, JC], U32, f"hw{c}") for c in range(CHUNKS)]
         hs = [held([P, GROUPS, JC], U8, f"hs{c}") for c in range(CHUNKS)]
 
-        h_pair = {
-            c: wf_bf[piece[:3]][:].rearrange("p (g j) t -> p g j t", g=GROUPS) for c, piece in enumerate(full_pieces, start=1)
-        }
+        h_pair = {c: held([P, GROUPS, JC, PACK], BF16, f"h{c}")[:] for c in range(1, CHUNKS)}
         h_bf = {(c, g): h_pair[c][:, g] for c in h_pair for g in range(GROUPS)}
-        for g in range(GROUPS):
-            h_bf[0, g] = wf_bf[half_pieces[GROUPS - 1 - g][:3]][:]
 
         whole = [(a, 0, KP) for a in range(PASSES)]
         products = []
-        fwd = {}
-        on_scalar = [(3, 0), (3, 1)]
+        on_scalar = [(2, 1), (3, 0), (3, 1)]
         opened = {}
         negated = {}
 
@@ -141,6 +140,8 @@ def tile_list_reversible_reaction_rates_kernel(
             nc.vector.tensor_copy(out=vw[a][:, j0:j1], in_=tabw[a][:].bitcast(U32).indirect(entries(idx, j0, j1)))
 
         def prepare_wf(g, a, c0, c1):
+            tag = "raw2" if (g, a, c0, c1) == half_pieces[0] else "rounded"
+            wf_bf[g, a, c0] = keep.tile([P, c1 - c0, PACK], BF16, name=f"wf_bf{g}{a}{c0}", tag=tag, align_bytes=64)
             grouped = wf_bf[g, a, c0][:]
             nc.vector.tensor_copy(
                 out=grouped.rearrange("p (u i) t -> p u t i", i=LINE),
@@ -152,32 +153,37 @@ def tile_list_reversible_reaction_rates_kernel(
                 in_=grouped.rearrange("p c t -> p (c t)"),
             )
 
-        def exp_of_product(dst, c, u, words, scales, parts):
-            bank = product_bank()
-            cells = slice(c * JC + u * P, c * JC + (u + 1) * P)
+        def exponentials(dst, c, tiles, words, scales, parts, between=None):
+            held_banks = {u: product_bank() for u in tiles}
             for k, (a, c0, c1) in enumerate(parts):
-                nc.tensor.matmul_mx(
-                    out=bank[:, c0:c1],
-                    lhsT=vw[a][:, cells].bitcast(FP8X4),
-                    lhsT_scale=vs[4 * a :, cells],
-                    rhs=words[a][:, c0:c1].bitcast(FP8X4),
-                    rhs_scale=scales[a][:, c0:c1],
-                    start=k == 0,
-                    stop=k == len(parts) - 1,
-                )
-            nc.scalar.activation(out=dst, in_=bank[:].rearrange("p (m t) -> p t m", t=PACK), func=EXP)
+                for u, bank in held_banks.items():
+                    cells = slice(c * JC + u * P, c * JC + (u + 1) * P)
+                    nc.tensor.matmul_mx(
+                        out=bank[:, c0:c1],
+                        lhsT=vw[a][:, cells].bitcast(FP8X4),
+                        lhsT_scale=vs[4 * a :, cells],
+                        rhs=words[a][:, c0:c1].bitcast(FP8X4),
+                        rhs_scale=scales[a][:, c0:c1],
+                        start=k == 0,
+                        stop=k == len(parts) - 1,
+                    )
+            if between is not None:
+                between()
+            for u, bank in held_banks.items():
+                nc.scalar.activation(out=dst[:, u], in_=bank[:].rearrange("p (m t) -> p t m", t=PACK), func=EXP)
 
         def backward(c, g):
-            words = [wbw[g][:, a, :] for a in range(PASSES)]
-            scales = [wbs[4 * a :, :].bitcast(U8)[:, g * KP : (g + 1) * KP] for a in range(PASSES)]
-            for u in range(TILES):
-                exp_of_product(bwd[c, g][:, u], c, u, words, scales, whole)
+            words = [wbw[g, a][:] for a in range(PASSES)]
+            scales = [wbs[:, a, :].bitcast(U8)[:, g * KP : (g + 1) * KP] for a in range(PASSES)]
+            together = [range(TILES)] if (c, g) == (0, 0) else [[u] for u in range(TILES)]
+            for tiles in together:
+                exponentials(bwd[c, g], c, tiles, words, scales, whole)
 
         def negated_tile(c, g, behind):
             if behind is None:
                 negated[c, g] = bwd[c, g]
             else:
-                negated[c, g] = keep.tile([P, TILES, PACK, P], F32, name=f"neg{c}{g}", tag=f"raw{behind}", align_bytes=64)
+                negated[c, g] = keep.tile([P, TILES, PACK, P], F32, name=f"neg{c}{g}", tag=behind, align_bytes=64)
             return negated[c, g]
 
         def negate_on_vector(c, g, behind=None):
@@ -194,13 +200,14 @@ def tile_list_reversible_reaction_rates_kernel(
             for u in range(TILES):
                 nc.scalar.activation(out=dst[:, u], in_=bwd[c, g][:, u], func=COPY, scale=-1.0)
 
-        def forward(c, g, tiles=range(TILES)):
-            fwd.setdefault((c, g), fwd_ring[len(fwd) % RING])
+        def forward(c, g, tiles=range(TILES), between=None):
             words = [wfw[g, a][:] for a in range(PASSES)]
             scales = [wfs[g, a][:] for a in range(PASSES)]
-            parts = [piece[1:] for piece in pieces if piece[0] == g] if c < CHUNKS // 2 else whole
-            for u in tiles:
-                exp_of_product(fwd[c, g][:, u], c, u, words, scales, parts)
+            if (c, g) == (0, 1):
+                exponentials(fwd[c, g], c, tiles, words, scales, [piece[1:] for piece in pieces if piece[0] == g])
+            else:
+                for u in tiles:
+                    exponentials(fwd[c, g], c, [u], words, scales, whole, between)
 
         def turn_over(c, g, side, opens):
             for k, bank in enumerate(opened[c, g]):
@@ -262,36 +269,43 @@ def tile_list_reversible_reaction_rates_kernel(
                 in_=h_pair[c].rearrange("p g j t -> p (g j t)"),
             )
 
-        def species(c, n0, n1, b=None):
-            bank = (product_bank() if b is None else banks[b])[:].rearrange("p (n j) -> p n j", j=JC)
-            for n in range(n0, n1):
+        def y_column(c, n):
+            order = list(range(NT)) if c + 1 < CHUNKS else [3, 2, 0, 1]
+            return (c * NT + order.index(n)) * JC
+
+        def species(c, rows, b=None):
+            bank = product_bank() if b is None else banks[b]
+            for k, n in enumerate(rows):
                 for g in reversed(range(GROUPS)):
                     nc.tensor.matmul_mx(
-                        out=bank[:, n - n0, :],
+                        out=bank[:, k * JC : (k + 1) * JC],
                         lhsT=wsw[:, g, 2 * n * P : 2 * (n + 1) * P].bitcast(FP4X4),
                         lhsT_scale=wss[:, g, n * P // 4 : (n + 1) * P // 4].bitcast(U8),
                         rhs=hw[c][:, g].bitcast(FP8X4),
                         rhs_scale=hs[c][:, g],
-                        start=(n, g) == (n0, GROUPS - 1),
-                        stop=(n, g) == (n1 - 1, 0),
+                        start=(k, g) == (0, GROUPS - 1),
+                        stop=(k, g) == (len(rows) - 1, 0),
                     )
-            nc.scalar.copy(out=y[:, n0:n1, c * JC : (c + 1) * JC], in_=bank[:, : n1 - n0, :])
+            first = y_column(c, rows[0])
+            nc.scalar.copy(out=y[:, first : first + len(rows) * JC], in_=bank[:, : len(rows) * JC])
 
         def scatter(n, c0, c1):
             j0, j1 = c0 * JC, c1 * JC
+            first = y_column(c0, n)
             nc.vector.tensor_tensor(
-                out=store[n][:].indirect(entries(idx2, j0, j1)), in0=y[:, n, j0:j1], in1=wg[:, j0:j1], op=MULT
+                out=store[n][:].indirect(entries(idx2, j0, j1)), in0=y[:, first : first + j1 - j0], in1=wg[:, j0:j1], op=MULT
             )
             if c1 == CHUNKS:
                 nc.sync.dma_start(out=out[n * P : (n + 1) * P, :], in_=store[n][:])
 
         def place(c, n0, n1, b=None):
-            species(c, n0, n1, b)
+            species(c, range(n0, n1), b)
             for n in range(n0, n1):
                 scatter(n, c, c + 1)
 
         gather_words(0, 0, S)
-        nc.vector.tensor_copy(out=vs[:], in_=tabs[:].bitcast(U8).indirect(idx[:]))
+        for j0, j1 in ((0, JC), (JC, S)):
+            nc.vector.tensor_copy(out=vs[:, j0:j1], in_=tabs[:].bitcast(U8).indirect(entries(idx, j0, j1)))
         for j0, j1 in ((0, JC), (JC, 2 * JC), (2 * JC, S)):
             gather_words(1, j0, j1)
         for tag in ("table0", "table_scales"):
@@ -299,17 +313,20 @@ def tile_list_reversible_reaction_rates_kernel(
             nc.gpsimd.memset(store[-1][:].bitcast(I32), 0)
         for piece in pieces:
             prepare_wf(*piece)
+        for g in range(GROUPS):
+            h_bf[0, g] = wf_bf[half_pieces[GROUPS - 1 - g][:3]][:]
 
         backward(0, 0)
         negate_on_vector(0, 0)
         backward(0, 1)
-        negate_on_vector(0, 1, 0)
+        negate_on_vector(0, 1)
         backward(1, 0)
         backward(1, 1)
         open_differences(0, 0, 4, 5)
         backward(2, 0)
         backward(2, 1)
         open_differences(0, 1, 6, 7)
+        backward(3, 0)
         negate_on_scalar(1, 0)
         forward(0, 0)
         forward(1, 0)
@@ -319,46 +336,43 @@ def tile_list_reversible_reaction_rates_kernel(
         rates_on_vector(0, 1)
         quantize_group(0, 1)
         forward(1, 1)
-        negate_on_scalar(1, 1, 2)
-        negate_on_scalar(2, 0, 3)
+        negate_on_scalar(1, 1, "fwd00")
         open_differences(1, 0, 4, 5)
         rates_on_vector(1, 0)
-        place(0, 0, 1)
-        place(0, 1, 2)
-        forward(2, 0, [0])
+        forward(2, 0, [0], lambda: [place(0, n, n + 1) for n in range(2)])
+        negate_on_scalar(2, 1, "fwd01")
+        forward(2, 0, [1])
         open_differences(1, 1, 6, 7)
         rates_on_vector(1, 1)
         quantize_chunk(1)
-        negate_on_scalar(2, 1, 4)
-        forward(2, 0, [1])
+        negate_on_scalar(2, 0, "fwd10")
         forward(2, 1)
         place(0, 2, 4, 4)
-        backward(3, 0)
+        backward(3, 1)
         open_differences(2, 0, 6, 7)
         rates_on_vector(2, 0)
-        negate_on_scalar(3, 0)
+        place(1, 0, 2, 5)
         forward(3, 0)
         open_differences(2, 1, 4, 5)
-        rates_on_vector(2, 1)
+        scale_on_scalar(2, 1)
+        interleave_on_scalar(2, 1)
         quantize_chunk(2)
-        backward(3, 1)
-        place(1, 0, 1, 4)
-        place(1, 1, 2, 5)
         place(1, 2, 4, 4)
+        negate_on_scalar(3, 0, "fwd11")
+        forward(3, 1)
         open_differences(3, 0, 6, 7)
         scale_on_scalar(3, 0)
-        forward(3, 1)
+        place(2, 0, 2, 6)
         negate_on_scalar(3, 1)
         interleave_on_scalar(3, 0)
-        place(2, 0, 2, 6)
         open_differences(3, 1, 5, 4)
         scale_on_scalar(3, 1)
         interleave_on_scalar(3, 1)
         quantize_chunk(3)
-        species(2, 2, 4, 5)
+        species(2, [2, 3], 5)
         scatter(2, 2, 3)
         place(3, 0, 1, 7)
         place(3, 1, 2, 6)
-        species(3, 2, 4, 4)
+        species(3, [3, 2], 4)
         scatter(2, 3, 4)
         scatter(3, 2, 4)

@@ -31,6 +31,9 @@ NT = N // P
 PER_COL = 16
 LINE = 2
 BANKS = 8
+AHEAD = 6
+ON_VECTOR = 5
+LAG = 3
 
 
 def tile_list_reversible_reaction_rates_kernel(
@@ -113,8 +116,12 @@ def tile_list_reversible_reaction_rates_kernel(
         wf_bf = {}
 
         banks = [psum.tile([P, KP], F32, name=f"bank{b}") for b in range(BANKS)]
+        pairs = [banks[BANKS // 2 + TILES * g : BANKS // 2 + TILES * (g + 1)] for g in range(GROUPS)]
         steps = [(c, g) for c in range(CHUNKS) for g in range(GROUPS)]
-        fwd = {(c, g): keep.tile([P, TILES, PACK, P], F32, name=f"fwd{c}{g}", tag=f"fwd{c}{g}", align_bytes=64) for c, g in steps}
+        fwd = {
+            step: keep.tile([P, TILES, PACK, P], F32, name=f"fwd{s}", tag=f"fwd{s}", align_bytes=64)
+            for s, step in enumerate(steps)
+        }
         bwd = {(c, g): held([P, TILES, PACK, P], F32, f"bwd{c}{g}") for c, g in steps}
         planes = held([P, PACK, JC], BF16, "planes")
         hw = [held([P, GROUPS, JC], U32, f"hw{c}") for c in range(CHUNKS)]
@@ -125,8 +132,7 @@ def tile_list_reversible_reaction_rates_kernel(
 
         whole = [(a, 0, KP) for a in range(PASSES)]
         products = []
-        on_scalar = [(2, 1), (3, 0), (3, 1)]
-        opened = {}
+        on_scalar = steps[ON_VECTOR:]
         negated = {}
 
         def product_bank():
@@ -153,7 +159,7 @@ def tile_list_reversible_reaction_rates_kernel(
                 in_=grouped.rearrange("p c t -> p (c t)"),
             )
 
-        def exponentials(dst, c, tiles, words, scales, parts, between=None):
+        def exponentials(dst, c, tiles, words, scales, parts):
             held_banks = {u: product_bank() for u in tiles}
             for k, (a, c0, c1) in enumerate(parts):
                 for u, bank in held_banks.items():
@@ -167,8 +173,6 @@ def tile_list_reversible_reaction_rates_kernel(
                         start=k == 0,
                         stop=k == len(parts) - 1,
                     )
-            if between is not None:
-                between()
             for u, bank in held_banks.items():
                 nc.scalar.activation(out=dst[:, u], in_=bank[:].rearrange("p (m t) -> p t m", t=PACK), func=EXP)
 
@@ -179,38 +183,30 @@ def tile_list_reversible_reaction_rates_kernel(
             for tiles in together:
                 exponentials(bwd[c, g], c, tiles, words, scales, whole)
 
-        def negated_tile(c, g, behind):
-            if behind is None:
-                negated[c, g] = bwd[c, g]
+        def negate(c, g):
+            s = steps.index((c, g))
+            negated[c, g] = bwd[c, g]
+            if s >= LAG:
+                tag = f"fwd{s - LAG}"
+                negated[c, g] = keep.tile([P, TILES, PACK, P], F32, name=f"neg{c}{g}", tag=tag, align_bytes=64)
+            if c == 0:
+                flat = bwd[c, g][:].rearrange("p u t m -> p (u t m)")
+                nc.vector.tensor_scalar(out=flat, in0=flat, scalar1=-1.0, scalar2=None, op0=MULT)
             else:
-                negated[c, g] = keep.tile([P, TILES, PACK, P], F32, name=f"neg{c}{g}", tag=behind, align_bytes=64)
-            return negated[c, g]
+                for u in range(TILES):
+                    nc.scalar.activation(out=negated[c, g][:, u], in_=bwd[c, g][:, u], func=COPY, scale=-1.0)
 
-        def negate_on_vector(c, g, behind=None):
-            nc.vector.tensor_scalar(
-                out=negated_tile(c, g, behind)[:].rearrange("p u t m -> p (u t m)"),
-                in0=bwd[c, g][:].rearrange("p u t m -> p (u t m)"),
-                scalar1=-1.0,
-                scalar2=None,
-                op0=MULT,
-            )
-
-        def negate_on_scalar(c, g, behind=None):
-            dst = negated_tile(c, g, behind)
-            for u in range(TILES):
-                nc.scalar.activation(out=dst[:, u], in_=bwd[c, g][:, u], func=COPY, scale=-1.0)
-
-        def forward(c, g, tiles=range(TILES), between=None):
+        def forward(c, g):
             words = [wfw[g, a][:] for a in range(PASSES)]
             scales = [wfs[g, a][:] for a in range(PASSES)]
-            if (c, g) == (0, 1):
-                exponentials(fwd[c, g], c, tiles, words, scales, [piece[1:] for piece in pieces if piece[0] == g])
+            if (c, g) == (0, GROUPS - 1):
+                exponentials(fwd[c, g], c, range(TILES), words, scales, [piece[1:] for piece in pieces if piece[0] == g])
             else:
-                for u in tiles:
-                    exponentials(fwd[c, g], c, [u], words, scales, whole, between)
+                for u in range(TILES):
+                    exponentials(fwd[c, g], c, [u], words, scales, whole)
 
         def turn_over(c, g, side, opens):
-            for k, bank in enumerate(opened[c, g]):
+            for k, bank in enumerate(pairs[g]):
                 if (c, g) not in on_scalar:
                     blocks = [(k, t) for t in range(PACK)]
                 else:
@@ -225,13 +221,11 @@ def tile_list_reversible_reaction_rates_kernel(
                         stop=not opens and i == len(blocks) - 1,
                     )
 
-        def open_differences(c, g, first, second):
-            opened[c, g] = [banks[first], banks[second]]
-            turn_over(c, g, negated[c, g], True)
-
         def differences(c, g):
+            if c > 0:
+                turn_over(c, g, negated[c, g], True)
             turn_over(c, g, fwd[c, g], False)
-            return opened[c, g]
+            return pairs[g]
 
         def rates_on_vector(c, g):
             factor = kap[:, g, :].unsqueeze(1).unsqueeze(3).to_broadcast([P, P // 2, PACK, 2])
@@ -243,15 +237,13 @@ def tile_list_reversible_reaction_rates_kernel(
                     op=MULT,
                 )
 
-        def scale_on_scalar(c, g):
+        def rates_on_scalar(c, g):
             for k, bank in enumerate(differences(c, g)):
                 for i in range(2):
                     t = 2 * k + i
                     nc.scalar.activation(
                         out=planes[:, t, :], in_=bank[:, i * JC : (i + 1) * JC], func=COPY, scale=kap[:, g, t : t + 1]
                     )
-
-        def interleave_on_scalar(c, g):
             nc.scalar.copy(
                 out=h_bf[c, g].rearrange("p (w e) t -> p w t e", e=LINE),
                 in_=planes[:].rearrange("p t (w e) -> p w t e", e=LINE),
@@ -273,8 +265,7 @@ def tile_list_reversible_reaction_rates_kernel(
             order = list(range(NT)) if c + 1 < CHUNKS else [3, 2, 0, 1]
             return (c * NT + order.index(n)) * JC
 
-        def species(c, rows, b=None):
-            bank = product_bank() if b is None else banks[b]
+        def species(c, rows, bank):
             for k, n in enumerate(rows):
                 for g in reversed(range(GROUPS)):
                     nc.tensor.matmul_mx(
@@ -298,10 +289,17 @@ def tile_list_reversible_reaction_rates_kernel(
             if c1 == CHUNKS:
                 nc.sync.dma_start(out=out[n * P : (n + 1) * P, :], in_=store[n][:])
 
-        def place(c, n0, n1, b=None):
-            species(c, range(n0, n1), b)
-            for n in range(n0, n1):
-                scatter(n, c, c + 1)
+        def rates(c, g):
+            if (c, g) in on_scalar:
+                rates_on_scalar(c, g)
+            else:
+                rates_on_vector(c, g)
+
+        def exponentials_of(c, g):
+            if (c, g) not in steps[:AHEAD]:
+                backward(c, g)
+            forward(c, g)
+            negate(c, g)
 
         gather_words(0, 0, S)
         for j0, j1 in ((0, JC), (JC, S)):
@@ -316,63 +314,37 @@ def tile_list_reversible_reaction_rates_kernel(
         for g in range(GROUPS):
             h_bf[0, g] = wf_bf[half_pieces[GROUPS - 1 - g][:3]][:]
 
-        backward(0, 0)
-        negate_on_vector(0, 0)
-        backward(0, 1)
-        negate_on_vector(0, 1)
-        backward(1, 0)
-        backward(1, 1)
-        open_differences(0, 0, 4, 5)
-        backward(2, 0)
-        backward(2, 1)
-        open_differences(0, 1, 6, 7)
-        backward(3, 0)
-        negate_on_scalar(1, 0)
-        forward(0, 0)
-        forward(1, 0)
-        rates_on_vector(0, 0)
-        quantize_group(0, 0)
-        forward(0, 1)
-        rates_on_vector(0, 1)
-        quantize_group(0, 1)
-        forward(1, 1)
-        negate_on_scalar(1, 1, "fwd00")
-        open_differences(1, 0, 4, 5)
-        rates_on_vector(1, 0)
-        forward(2, 0, [0], lambda: [place(0, n, n + 1) for n in range(2)])
-        negate_on_scalar(2, 1, "fwd01")
-        forward(2, 0, [1])
-        open_differences(1, 1, 6, 7)
-        rates_on_vector(1, 1)
-        quantize_chunk(1)
-        negate_on_scalar(2, 0, "fwd10")
-        forward(2, 1)
-        place(0, 2, 4, 4)
-        backward(3, 1)
-        open_differences(2, 0, 6, 7)
-        rates_on_vector(2, 0)
-        place(1, 0, 2, 5)
-        forward(3, 0)
-        open_differences(2, 1, 4, 5)
-        scale_on_scalar(2, 1)
-        interleave_on_scalar(2, 1)
-        quantize_chunk(2)
-        place(1, 2, 4, 4)
-        negate_on_scalar(3, 0, "fwd11")
-        forward(3, 1)
-        open_differences(3, 0, 6, 7)
-        scale_on_scalar(3, 0)
-        place(2, 0, 2, 6)
-        negate_on_scalar(3, 1)
-        interleave_on_scalar(3, 0)
-        open_differences(3, 1, 5, 4)
-        scale_on_scalar(3, 1)
-        interleave_on_scalar(3, 1)
-        quantize_chunk(3)
-        species(2, [2, 3], 5)
-        scatter(2, 2, 3)
-        place(3, 0, 1, 7)
-        place(3, 1, 2, 6)
-        species(3, [3, 2], 4)
-        scatter(2, 3, 4)
-        scatter(3, 2, 4)
+        for c, g in steps[:AHEAD]:
+            backward(c, g)
+            if c == 0:
+                negate(c, g)
+        for g in range(GROUPS):
+            turn_over(0, g, negated[0, g], True)
+        for g in range(GROUPS):
+            forward(0, g)
+            rates(0, g)
+            quantize_group(0, g)
+            forward(1, g)
+            negate(1, g)
+
+        for c in range(CHUNKS):
+            ahead = c + 1 < CHUNKS
+            if ahead and (c + 1, 0) not in on_scalar:
+                rates(c + 1, 0)
+            for n in range(NT // 2):
+                species(c, [n], product_bank())
+                scatter(n, c, c + 1)
+            if ahead and (c + 1, 0) in on_scalar:
+                rates(c + 1, 0)
+            if c + 2 < CHUNKS:
+                exponentials_of(c + 2, 0)
+            if ahead:
+                rates(c + 1, 1)
+                quantize_chunk(c + 1)
+            freed = pairs[1] if (c + 1, 1) in on_scalar else pairs[0]
+            species(c, sorted(range(NT // 2, NT), key=lambda n: y_column(c, n)), freed[0])
+            scatter(NT - 2, c, c + 1)
+            if c + 2 != CHUNKS:
+                scatter(NT - 1, min(c, CHUNKS - 2), c + 1)
+            if c + 2 < CHUNKS:
+                exponentials_of(c + 2, 1)

@@ -31,7 +31,7 @@ NT = N // P
 PER_COL = 16
 LINE = 2
 BANKS = 8
-AHEAD = 6
+AHEAD = 7
 ON_VECTOR = 5
 LAG = 3
 

@@ -295,12 +295,6 @@ def tile_list_reversible_reaction_rates_kernel(
             else:
                 rates_on_vector(c, g)
 
-        def exponentials_of(c, g):
-            if (c, g) not in steps[:AHEAD]:
-                backward(c, g)
-            forward(c, g)
-            negate(c, g)
-
         gather_words(0, 0, S)
         for j0, j1 in ((0, JC), (JC, S)):
             nc.vector.tensor_copy(out=vs[:, j0:j1], in_=tabs[:].bitcast(U8).indirect(entries(idx, j0, j1)))
@@ -337,7 +331,8 @@ def tile_list_reversible_reaction_rates_kernel(
             if ahead and (c + 1, 0) in on_scalar:
                 rates(c + 1, 0)
             if c + 2 < CHUNKS:
-                exponentials_of(c + 2, 0)
+                forward(c + 2, 0)
+                negate(c + 2, 0)
             if ahead:
                 rates(c + 1, 1)
                 quantize_chunk(c + 1)
@@ -347,4 +342,8 @@ def tile_list_reversible_reaction_rates_kernel(
             if c + 2 != CHUNKS:
                 scatter(NT - 1, min(c, CHUNKS - 2), c + 1)
             if c + 2 < CHUNKS:
-                exponentials_of(c + 2, 1)
+                forward(c + 2, 1)
+                negate(c + 2, 1)
+            if c == 0:
+                for step in steps[AHEAD:]:
+                    backward(*step)

@@ -31,7 +31,7 @@ NT = N // P
 PER_COL = 16
 LINE = 2
 BANKS = 8
-AHEAD = 7
+AHEAD = 6
 ON_VECTOR = 5
 LAG = 3
 

@@ -49,8 +49,8 @@ def tile_list_reversible_reaction_rates_kernel(
 
         idx = held([P, S // PER_COL], U16, "idx")
         idx2 = held([P, S // PER_COL], U16, "idx2")
-        tabw = [keep.tile([P, T], I32, name=f"tabw{a}", tag=f"table{a}", align_bytes=64) for a in range(PASSES)]
-        tabs = keep.tile([P, T // 4], I32, name="tabs", tag="table_scales", align_bytes=64)
+        tabw = [held([P, T], I32, f"tabw{a}") for a in range(PASSES)]
+        tabs = held([P, T // 4], I32, "tabs")
         wbs = held([P, PASSES, R // 4], I32, "wbs")
         wbw = {(g, a): held([P, KP], I32, f"wbw{g}{a}") for g in range(GROUPS) for a in range(PASSES)}
         full_pieces = [(0, 0, 0, KP), (0, 1, 0, KP), (1, 0, 0, KP)]
@@ -64,16 +64,16 @@ def tile_list_reversible_reaction_rates_kernel(
         wss = held([P, GROUPS, N // 4], I32, "wss")
         kap = held([P, GROUPS, PACK], F32, "kap")
         wg = held([P, S], F32, "wg")
-        store = [held([P, T2], F32, f"store{n}") for n in range(NT // 2)]
+        store = [held([P, T2], F32, f"store{n}") for n in range(NT)]
         ident = held([P, P], F32, "ident")
         y = held([P, NT * S], F32, "y")
 
         nc.vector.memset(tabs[:], 0)
         nc.vector.memset(wbs[:], 0)
-        for n in range(NT // 2):
-            nc.vector.memset(store[n][:].bitcast(I32), 0)
         nc.vector.memset(wss[:], 0)
         make_identity(nc, ident[:])
+        for n in range(NT):
+            nc.gpsimd.memset(store[n][:].bitcast(I32), 0)
 
         def load_wbw(g, a):
             rows = wb_words[a].rearrange("p c i -> p (c i)")[:, g * KP * PACK : (g + 1) * KP * PACK]
@@ -92,11 +92,11 @@ def tile_list_reversible_reaction_rates_kernel(
             nc.sync.dma_start(out=tabw[a][:], in_=tab_words[a].rearrange("p t i -> p (t i)").bitcast(I32))
 
         nc.sync.dma_start(idx[:], offs)
-        load_table(0)
+        load_wbw(0, 0)
         for q in range(QUADRANTS):
             nc.sync.dma_start(out=tabs[32 * q : 32 * q + 8, :], in_=tab_scales[:, 4 * q : 4 * q + 4, :].bitcast(I32))
+        load_table(0)
         load_planes(wbs, wb_scales)
-        load_wbw(0, 0)
         load_table(1)
         load_wbw(0, 1)
         for a in range(PASSES):
@@ -295,14 +295,11 @@ def tile_list_reversible_reaction_rates_kernel(
             else:
                 rates_on_vector(c, g)
 
-        gather_words(0, 0, S)
+        nc.vector.tensor_copy(out=vs[:], in_=tabs[:].bitcast(U8).indirect(idx[:]))
         for j0, j1 in ((0, JC), (JC, S)):
-            nc.vector.tensor_copy(out=vs[:, j0:j1], in_=tabs[:].bitcast(U8).indirect(entries(idx, j0, j1)))
+            gather_words(0, j0, j1)
         for j0, j1 in ((0, JC), (JC, 2 * JC), (2 * JC, S)):
             gather_words(1, j0, j1)
-        for tag in ("table0", "table_scales"):
-            store.append(keep.tile([P, T2], F32, name=f"store{len(store)}", tag=tag, align_bytes=64))
-            nc.gpsimd.memset(store[-1][:].bitcast(I32), 0)
         for piece in pieces:
             prepare_wf(*piece)
         for g in range(GROUPS):

@@ -32,8 +32,6 @@ PER_COL = 16
 LINE = 2
 BANKS = 8
 AHEAD = 6
-ON_VECTOR = 5
-LAG = 3
 
 
 def tile_list_reversible_reaction_rates_kernel(
@@ -49,8 +47,8 @@ def tile_list_reversible_reaction_rates_kernel(
 
         idx = held([P, S // PER_COL], U16, "idx")
         idx2 = held([P, S // PER_COL], U16, "idx2")
-        tabw = [held([P, T], I32, f"tabw{a}") for a in range(PASSES)]
-        tabs = held([P, T // 4], I32, "tabs")
+        tabw = [keep.tile([P, T], I32, name=f"tabw{a}", tag=f"table{a}", align_bytes=64) for a in range(PASSES)]
+        tabs = keep.tile([P, T // 4], I32, name="tabs", tag="table_scales", align_bytes=64)
         wbs = held([P, PASSES, R // 4], I32, "wbs")
         wbw = {(g, a): held([P, KP], I32, f"wbw{g}{a}") for g in range(GROUPS) for a in range(PASSES)}
         full_pieces = [(0, 0, 0, KP), (0, 1, 0, KP), (1, 0, 0, KP)]
@@ -64,16 +62,16 @@ def tile_list_reversible_reaction_rates_kernel(
         wss = held([P, GROUPS, N // 4], I32, "wss")
         kap = held([P, GROUPS, PACK], F32, "kap")
         wg = held([P, S], F32, "wg")
-        store = [held([P, T2], F32, f"store{n}") for n in range(NT)]
+        store = [held([P, T2], F32, f"store{n}") for n in range(NT // 2)]
         ident = held([P, P], F32, "ident")
         y = held([P, NT * S], F32, "y")
 
         nc.vector.memset(tabs[:], 0)
         nc.vector.memset(wbs[:], 0)
+        for n in range(NT // 2):
+            nc.vector.memset(store[n][:].bitcast(I32), 0)
         nc.vector.memset(wss[:], 0)
         make_identity(nc, ident[:])
-        for n in range(NT):
-            nc.gpsimd.memset(store[n][:].bitcast(I32), 0)
 
         def load_wbw(g, a):
             rows = wb_words[a].rearrange("p c i -> p (c i)")[:, g * KP * PACK : (g + 1) * KP * PACK]
@@ -127,17 +125,23 @@ def tile_list_reversible_reaction_rates_kernel(
         hw = [held([P, GROUPS, JC], U32, f"hw{c}") for c in range(CHUNKS)]
         hs = [held([P, GROUPS, JC], U8, f"hs{c}") for c in range(CHUNKS)]
 
-        h_pair = {c: held([P, GROUPS, JC, PACK], BF16, f"h{c}")[:] for c in range(1, CHUNKS)}
-        h_bf = {(c, g): h_pair[c][:, g] for c in h_pair for g in range(GROUPS)}
+        h_pair = {}
+        h_bf = {}
 
         whole = [(a, 0, KP) for a in range(PASSES)]
         products = []
-        on_scalar = steps[ON_VECTOR:]
+        on_scalar = [(c, GROUPS - 1) for c in range(1, CHUNKS)]
         negated = {}
 
         def product_bank():
-            products.append(banks[len(products) % (BANKS // 2)])
+            products.append((banks[:2] + pairs[1] + banks[2:4])[(len(products) + 4) % 6])
             return products[-1]
+
+        taken = []
+
+        def ring_bank():
+            taken.append(ring[len(taken) % len(ring)])
+            return taken[-1]
 
         def entries(lst, j0, j1):
             return lst[:, j0 // PER_COL : j1 // PER_COL]
@@ -145,7 +149,7 @@ def tile_list_reversible_reaction_rates_kernel(
         def gather_words(a, j0, j1):
             nc.vector.tensor_copy(out=vw[a][:, j0:j1], in_=tabw[a][:].bitcast(U32).indirect(entries(idx, j0, j1)))
 
-        def prepare_wf(g, a, c0, c1):
+        def round_wf(g, a, c0, c1):
             tag = "raw2" if (g, a, c0, c1) == half_pieces[0] else "rounded"
             wf_bf[g, a, c0] = keep.tile([P, c1 - c0, PACK], BF16, name=f"wf_bf{g}{a}{c0}", tag=tag, align_bytes=64)
             grouped = wf_bf[g, a, c0][:]
@@ -153,14 +157,15 @@ def tile_list_reversible_reaction_rates_kernel(
                 out=grouped.rearrange("p (u i) t -> p u t i", i=LINE),
                 in_=wf_raw[g, a, c0][:].rearrange("p t (u i) -> p u t i", i=LINE),
             )
+
+        def quantize_wf(g, a, c0, c1):
             nc.vector.quantize_mx(
                 out=wfw[g, a][:, c0:c1].bitcast(FP8X4),
                 scales=wfs[g, a][:, c0:c1],
-                in_=grouped.rearrange("p c t -> p (c t)"),
+                in_=wf_bf[g, a, c0][:].rearrange("p c t -> p (c t)"),
             )
 
-        def exponentials(dst, c, tiles, words, scales, parts):
-            held_banks = {u: product_bank() for u in tiles}
+        def exponentials(dst, c, held_banks, words, scales, parts):
             for k, (a, c0, c1) in enumerate(parts):
                 for u, bank in held_banks.items():
                     cells = slice(c * JC + u * P, c * JC + (u + 1) * P)
@@ -176,37 +181,41 @@ def tile_list_reversible_reaction_rates_kernel(
             for u, bank in held_banks.items():
                 nc.scalar.activation(out=dst[:, u], in_=bank[:].rearrange("p (m t) -> p t m", t=PACK), func=EXP)
 
-        def backward(c, g):
+        def backward(c, g, pick):
             words = [wbw[g, a][:] for a in range(PASSES)]
             scales = [wbs[:, a, :].bitcast(U8)[:, g * KP : (g + 1) * KP] for a in range(PASSES)]
             together = [range(TILES)] if (c, g) == (0, 0) else [[u] for u in range(TILES)]
             for tiles in together:
-                exponentials(bwd[c, g], c, tiles, words, scales, whole)
+                exponentials(bwd[c, g], c, {u: pick() for u in tiles}, words, scales, whole)
 
-        def negate(c, g):
-            s = steps.index((c, g))
+        def negate(c, g, tag=None):
             negated[c, g] = bwd[c, g]
-            if s >= LAG:
-                tag = f"fwd{s - LAG}"
+            if tag:
                 negated[c, g] = keep.tile([P, TILES, PACK, P], F32, name=f"neg{c}{g}", tag=tag, align_bytes=64)
             if c == 0:
-                flat = bwd[c, g][:].rearrange("p u t m -> p (u t m)")
-                nc.vector.tensor_scalar(out=flat, in0=flat, scalar1=-1.0, scalar2=None, op0=MULT)
+                flat = "p u t m -> p (u t m)"
+                nc.vector.tensor_scalar(
+                    out=negated[c, g][:].rearrange(flat), in0=bwd[c, g][:].rearrange(flat), scalar1=-1.0, scalar2=None, op0=MULT
+                )
             else:
                 for u in range(TILES):
                     nc.scalar.activation(out=negated[c, g][:, u], in_=bwd[c, g][:, u], func=COPY, scale=-1.0)
 
-        def forward(c, g):
+        def forward(c, g, into):
             words = [wfw[g, a][:] for a in range(PASSES)]
             scales = [wfs[g, a][:] for a in range(PASSES)]
             if (c, g) == (0, GROUPS - 1):
-                exponentials(fwd[c, g], c, range(TILES), words, scales, [piece[1:] for piece in pieces if piece[0] == g])
+                parts = [piece[1:] for piece in pieces if piece[0] == g]
+                exponentials(fwd[c, g], c, dict(enumerate(into)), words, scales, parts)
             else:
                 for u in range(TILES):
-                    exponentials(fwd[c, g], c, [u], words, scales, whole)
+                    exponentials(fwd[c, g], c, {u: into[u]}, words, scales, whole)
+
+        def difference_banks(c, g):
+            return banks[:TILES] if (c, g) == (0, 0) else pairs[g]
 
         def turn_over(c, g, side, opens):
-            for k, bank in enumerate(pairs[g]):
+            for k, bank in enumerate(difference_banks(c, g)):
                 if (c, g) not in on_scalar:
                     blocks = [(k, t) for t in range(PACK)]
                 else:
@@ -222,10 +231,9 @@ def tile_list_reversible_reaction_rates_kernel(
                     )
 
         def differences(c, g):
-            if c > 0:
-                turn_over(c, g, negated[c, g], True)
+            turn_over(c, g, negated[c, g], True)
             turn_over(c, g, fwd[c, g], False)
-            return pairs[g]
+            return difference_banks(c, g)
 
         def rates_on_vector(c, g):
             factor = kap[:, g, :].unsqueeze(1).unsqueeze(3).to_broadcast([P, P // 2, PACK, 2])
@@ -300,47 +308,65 @@ def tile_list_reversible_reaction_rates_kernel(
             gather_words(0, j0, j1)
         for j0, j1 in ((0, JC), (JC, 2 * JC), (2 * JC, S)):
             gather_words(1, j0, j1)
-        for piece in pieces:
-            prepare_wf(*piece)
-        for g in range(GROUPS):
-            h_bf[0, g] = wf_bf[half_pieces[GROUPS - 1 - g][:3]][:]
+        for tag in ("table_scales", "table0"):
+            store.append(keep.tile([P, T2], F32, name=f"store{len(store)}", tag=tag, align_bytes=64))
+            nc.gpsimd.memset(store[-1][:].bitcast(I32), 0)
 
         for c, g in steps[:AHEAD]:
-            backward(c, g)
+            backward(c, g, product_bank)
             if c == 0:
                 negate(c, g)
+        for k, piece in enumerate(pieces):
+            round_wf(*piece)
+            quantize_wf(*piece)
         for g in range(GROUPS):
-            turn_over(0, g, negated[0, g], True)
-        for g in range(GROUPS):
-            forward(0, g)
-            rates(0, g)
-            quantize_group(0, g)
-            forward(1, g)
-            negate(1, g)
+            h_bf[0, g] = wf_bf[half_pieces[GROUPS - 1 - g][:3]][:]
+        for c in range(1, CHUNKS):
+            tag = "raw2" if c == 1 else f"h{c}"
+            h_pair[c] = keep.tile([P, GROUPS, JC, PACK], BF16, name=f"h{c}", tag=tag, align_bytes=64)[:]
+            for g in range(GROUPS):
+                h_bf[c, g] = h_pair[c][:, g]
+        forward(0, 0, banks[:2])
+        rates(0, 0)
+        quantize_group(0, 0)
+        forward(0, 1, banks[2:4])
+        rates(0, 1)
+        quantize_group(0, 1)
+        negate(1, 0)
+        forward(1, 0, pairs[0])
+        forward(1, 1, [banks[0], banks[3]])
+        negate(1, 1)
+        rates(1, 0)
 
+        ring = [banks[b] for b in (1, 3, 2, 0)]
         for c in range(CHUNKS):
-            ahead = c + 1 < CHUNKS
-            if ahead and (c + 1, 0) not in on_scalar:
-                rates(c + 1, 0)
-            for n in range(NT // 2):
-                species(c, [n], product_bank())
+            early = range(NT - 1) if c + 2 < CHUNKS else range(NT // 2)
+            late = [n for n in range(NT) if n not in early]
+            for n in early:
+                species(c, [n], ring_bank())
                 scatter(n, c, c + 1)
-            if ahead and (c + 1, 0) in on_scalar:
-                rates(c + 1, 0)
-            if c + 2 < CHUNKS:
-                forward(c + 2, 0)
-                negate(c + 2, 0)
-            if ahead:
+            if c == 0:
+                forward(2, 0, [banks[0], ring_bank()])
+                negate(2, 0, "fwd0")
+                forward(2, 1, [ring_bank(), ring_bank()])
+                negate(2, 1, "fwd1")
+            if c == 1:
+                forward(3, 0, [ring_bank(), ring_bank()])
+                negate(3, 0, "fwd3")
+            if c + 1 < CHUNKS:
                 rates(c + 1, 1)
+            if c + 2 < CHUNKS:
+                rates(c + 2, 0)
+            if c + 1 < CHUNKS:
                 quantize_chunk(c + 1)
-            freed = pairs[1] if (c + 1, 1) in on_scalar else pairs[0]
-            species(c, sorted(range(NT // 2, NT), key=lambda n: y_column(c, n)), freed[0])
-            scatter(NT - 2, c, c + 1)
+            species(c, sorted(late, key=lambda n: y_column(c, n)), pairs[1][0])
+            if c + 2 >= CHUNKS:
+                scatter(NT - 2, c, c + 1)
             if c + 2 != CHUNKS:
                 scatter(NT - 1, min(c, CHUNKS - 2), c + 1)
-            if c + 2 < CHUNKS:
-                forward(c + 2, 1)
-                negate(c + 2, 1)
             if c == 0:
                 for step in steps[AHEAD:]:
-                    backward(*step)
+                    backward(*step, ring_bank)
+            if c == 1:
+                negate(3, 1, "fwd4")
+                forward(3, 1, [ring_bank(), ring_bank()])

@@ -17,6 +17,7 @@ FP4X4 = mybir.dt.float4_e2m1fn_x4
 EXP = mybir.ActivationFunctionType.Exp
 COPY = mybir.ActivationFunctionType.Copy
 MULT = mybir.AluOpType.mult
+ADD = mybir.AluOpType.add
 
 P = 128
 PACK = 4
@@ -30,8 +31,8 @@ TILES = JC // P
 NT = N // P
 PER_COL = 16
 LINE = 2
-BANKS = 8
-AHEAD = 6
+KIB = 1024
+AHEAD = 7
 
 
 def tile_list_reversible_reaction_rates_kernel(
@@ -40,24 +41,26 @@ def tile_list_reversible_reaction_rates_kernel(
     nc = tc.nc
     with ExitStack() as ctx:
         keep = ctx.enter_context(tc.tile_pool(name="keep", bufs=1))
+        shared = ctx.enter_context(tc.tile_pool(name="shared", bufs=1))
         psum = ctx.enter_context(tc.psum_pool(name="psum", bufs=1))
 
-        def held(shape, dtype, name):
-            return keep.tile(shape, dtype, name=name, align_bytes=64)
+        def held(shape, dtype, name, tag=None):
+            return keep.tile(shape, dtype, name=name, tag=tag or name, align_bytes=64)
+
+        def placed(shape, dtype, name, kib):
+            return shared.tile(shape, dtype, name=name, offset=kib * KIB)
 
         idx = held([P, S // PER_COL], U16, "idx")
         idx2 = held([P, S // PER_COL], U16, "idx2")
-        tabw = [keep.tile([P, T], I32, name=f"tabw{a}", tag=f"table{a}", align_bytes=64) for a in range(PASSES)]
-        tabs = keep.tile([P, T // 4], I32, name="tabs", tag="table_scales", align_bytes=64)
+        tabw = [held([P, T], I32, f"tabw{a}", f"table{a}") for a in range(PASSES)]
+        tabs = held([P, T // 4], I32, "tabs", "table_scales")
         wbs = held([P, PASSES, R // 4], I32, "wbs")
         wbw = {(g, a): held([P, KP], I32, f"wbw{g}{a}") for g in range(GROUPS) for a in range(PASSES)}
-        full_pieces = [(0, 0, 0, KP), (0, 1, 0, KP), (1, 0, 0, KP)]
-        half_pieces = [(1, 1, 0, KP // 2), (1, 1, KP // 2, KP)]
-        pieces = full_pieces + half_pieces
-        wf_raw = {
-            (g, a, c0): keep.tile([P, PACK, c1 - c0], F32, name=f"wf_raw{k}", tag=f"raw{k}", align_bytes=64)
+        pieces = [(0, 0, 0, KP), (0, 1, 0, KP), (1, 0, 0, KP), (1, 1, 0, KP // 2), (1, 1, KP // 2, KP)]
+        wf_raw = [
+            placed([P, PACK, KP], F32, "wf_raw2", 0) if k == 2 else held([P, PACK, c1 - c0], F32, f"wf_raw{k}")
             for k, (g, a, c0, c1) in enumerate(pieces)
-        }
+        ]
         wsw = held([P, GROUPS, 2 * N], U8, "wsw")
         wss = held([P, GROUPS, N // 4], I32, "wss")
         kap = held([P, GROUPS, PACK], F32, "kap")
@@ -65,6 +68,7 @@ def tile_list_reversible_reaction_rates_kernel(
         store = [held([P, T2], F32, f"store{n}") for n in range(NT // 2)]
         ident = held([P, P], F32, "ident")
         y = held([P, NT * S], F32, "y")
+        y_second = placed([P, JC], F32, "y_second", 16)
 
         nc.vector.memset(tabs[:], 0)
         nc.vector.memset(wbs[:], 0)
@@ -76,10 +80,6 @@ def tile_list_reversible_reaction_rates_kernel(
         def load_wbw(g, a):
             rows = wb_words[a].rearrange("p c i -> p (c i)")[:, g * KP * PACK : (g + 1) * KP * PACK]
             nc.sync.dma_start(out=wbw[g, a][:], in_=rows.bitcast(I32))
-
-        def load_wf(g, a, c0, c1):
-            rows = wf[a * KP : (a + 1) * KP, g * KP + c0 : g * KP + c1]
-            nc.sync.dma_start(out=wf_raw[g, a, c0][:], in_=rows.rearrange("(p i) c -> p i c", i=PACK))
 
         def load_planes(dst, src):
             for q in range(QUADRANTS):
@@ -99,8 +99,9 @@ def tile_list_reversible_reaction_rates_kernel(
         load_wbw(0, 1)
         for a in range(PASSES):
             load_wbw(1, a)
-        for piece in pieces:
-            load_wf(*piece)
+        for k, (g, a, c0, c1) in enumerate(pieces):
+            rows = wf[a * KP : (a + 1) * KP, g * KP + c0 : g * KP + c1]
+            nc.sync.dma_start(out=wf_raw[k][:], in_=rows.rearrange("(p i) c -> p i c", i=PACK))
         nc.sync.dma_start(out=kap[:], in_=kappa.rearrange("(g p t) -> p g t", g=GROUPS, t=PACK))
         load_planes(wss, ws_scales)
         nc.sync.dma_start(out=wsw[:].bitcast(I32), in_=ws_words.rearrange("g p c -> p g c").bitcast(I32))
@@ -111,37 +112,19 @@ def tile_list_reversible_reaction_rates_kernel(
         vs = held([P, S], U8, "vs")
         wfw = {(g, a): held([P, KP], U32, f"wfw{g}{a}") for g in range(GROUPS) for a in range(PASSES)}
         wfs = {(g, a): held([P, KP], U8, f"wfs{g}{a}") for g in range(GROUPS) for a in range(PASSES)}
-        wf_bf = {}
-
-        banks = [psum.tile([P, KP], F32, name=f"bank{b}") for b in range(BANKS)]
-        pairs = [banks[BANKS // 2 + TILES * g : BANKS // 2 + TILES * (g + 1)] for g in range(GROUPS)]
+        banks = [psum.tile([P, KP], F32, name=f"bank{b}") for b in range(8)]
+        pairs = [banks[4:6], banks[6:8]]
         steps = [(c, g) for c in range(CHUNKS) for g in range(GROUPS)]
-        fwd = {
-            step: keep.tile([P, TILES, PACK, P], F32, name=f"fwd{s}", tag=f"fwd{s}", align_bytes=64)
-            for s, step in enumerate(steps)
-        }
+        fwd = {(c, g): held([P, TILES, PACK, P], F32, f"fwd{c}{g}") for c, g in steps}
         bwd = {(c, g): held([P, TILES, PACK, P], F32, f"bwd{c}{g}") for c, g in steps}
-        planes = held([P, PACK, JC], BF16, "planes")
+        planes = held([P, 2, JC, 2], BF16, "planes")
         hw = [held([P, GROUPS, JC], U32, f"hw{c}") for c in range(CHUNKS)]
         hs = [held([P, GROUPS, JC], U8, f"hs{c}") for c in range(CHUNKS)]
-
-        h_pair = {}
-        h_bf = {}
-
+        on_scalar = [(1, 1), (2, 1), (3, 0), (3, 1)]
         whole = [(a, 0, KP) for a in range(PASSES)]
-        products = []
-        on_scalar = [(c, GROUPS - 1) for c in range(1, CHUNKS)]
         negated = {}
-
-        def product_bank():
-            products.append((banks[:2] + pairs[1] + banks[2:4])[(len(products) + 4) % 6])
-            return products[-1]
-
-        taken = []
-
-        def ring_bank():
-            taken.append(ring[len(taken) % len(ring)])
-            return taken[-1]
+        h_bf = {}
+        h_pair = {}
 
         def entries(lst, j0, j1):
             return lst[:, j0 // PER_COL : j1 // PER_COL]
@@ -149,25 +132,21 @@ def tile_list_reversible_reaction_rates_kernel(
         def gather_words(a, j0, j1):
             nc.vector.tensor_copy(out=vw[a][:, j0:j1], in_=tabw[a][:].bitcast(U32).indirect(entries(idx, j0, j1)))
 
-        def round_wf(g, a, c0, c1):
-            tag = "raw2" if (g, a, c0, c1) == half_pieces[0] else "rounded"
-            wf_bf[g, a, c0] = keep.tile([P, c1 - c0, PACK], BF16, name=f"wf_bf{g}{a}{c0}", tag=tag, align_bytes=64)
-            grouped = wf_bf[g, a, c0][:]
+        def prepare_wf(k, grouped):
+            g, a, c0, c1 = pieces[k]
             nc.vector.tensor_copy(
-                out=grouped.rearrange("p (u i) t -> p u t i", i=LINE),
-                in_=wf_raw[g, a, c0][:].rearrange("p t (u i) -> p u t i", i=LINE),
+                out=grouped[:].rearrange("p (u i) t -> p u t i", i=LINE),
+                in_=wf_raw[k][:].rearrange("p t (u i) -> p u t i", i=LINE),
             )
-
-        def quantize_wf(g, a, c0, c1):
             nc.vector.quantize_mx(
                 out=wfw[g, a][:, c0:c1].bitcast(FP8X4),
                 scales=wfs[g, a][:, c0:c1],
-                in_=wf_bf[g, a, c0][:].rearrange("p c t -> p (c t)"),
+                in_=grouped[:].rearrange("p c t -> p (c t)"),
             )
 
-        def exponentials(dst, c, held_banks, words, scales, parts):
+        def exponentials(dst, c, into, words, scales, parts):
             for k, (a, c0, c1) in enumerate(parts):
-                for u, bank in held_banks.items():
+                for u, bank in into.items():
                     cells = slice(c * JC + u * P, c * JC + (u + 1) * P)
                     nc.tensor.matmul_mx(
                         out=bank[:, c0:c1],
@@ -178,28 +157,14 @@ def tile_list_reversible_reaction_rates_kernel(
                         start=k == 0,
                         stop=k == len(parts) - 1,
                     )
-            for u, bank in held_banks.items():
+            for u, bank in into.items():
                 nc.scalar.activation(out=dst[:, u], in_=bank[:].rearrange("p (m t) -> p t m", t=PACK), func=EXP)
 
-        def backward(c, g, pick):
+        def backward(c, g, into):
             words = [wbw[g, a][:] for a in range(PASSES)]
             scales = [wbs[:, a, :].bitcast(U8)[:, g * KP : (g + 1) * KP] for a in range(PASSES)]
-            together = [range(TILES)] if (c, g) == (0, 0) else [[u] for u in range(TILES)]
-            for tiles in together:
-                exponentials(bwd[c, g], c, {u: pick() for u in tiles}, words, scales, whole)
-
-        def negate(c, g, tag=None):
-            negated[c, g] = bwd[c, g]
-            if tag:
-                negated[c, g] = keep.tile([P, TILES, PACK, P], F32, name=f"neg{c}{g}", tag=tag, align_bytes=64)
-            if c == 0:
-                flat = "p u t m -> p (u t m)"
-                nc.vector.tensor_scalar(
-                    out=negated[c, g][:].rearrange(flat), in0=bwd[c, g][:].rearrange(flat), scalar1=-1.0, scalar2=None, op0=MULT
-                )
-            else:
-                for u in range(TILES):
-                    nc.scalar.activation(out=negated[c, g][:, u], in_=bwd[c, g][:, u], func=COPY, scale=-1.0)
+            for u in range(TILES):
+                exponentials(bwd[c, g], c, {u: into[u]}, words, scales, whole)
 
         def forward(c, g, into):
             words = [wfw[g, a][:] for a in range(PASSES)]
@@ -211,51 +176,67 @@ def tile_list_reversible_reaction_rates_kernel(
                 for u in range(TILES):
                     exponentials(fwd[c, g], c, {u: into[u]}, words, scales, whole)
 
-        def difference_banks(c, g):
-            return banks[:TILES] if (c, g) == (0, 0) else pairs[g]
+        flat = "p u t m -> p (u t m)"
 
-        def turn_over(c, g, side, opens):
-            for k, bank in enumerate(difference_banks(c, g)):
-                if (c, g) not in on_scalar:
-                    blocks = [(k, t) for t in range(PACK)]
-                else:
-                    blocks = [(u, t) for t in (2 * k, 2 * k + 1) for u in range(TILES)]
-                for i, (u, t) in enumerate(blocks):
-                    nc.tensor.matmul(
-                        out=bank[:, i * P : (i + 1) * P],
-                        lhsT=side[:, u, t, :],
-                        rhs=ident[:],
-                        is_transpose=True,
-                        start=opens and i == 0,
-                        stop=not opens and i == len(blocks) - 1,
-                    )
+        def negate_on_vector(c, g):
+            negated[c, g] = bwd[c, g]
+            values = bwd[c, g][:].rearrange(flat)
+            nc.vector.tensor_scalar(out=values, in0=values, scalar1=-1.0, scalar2=None, op0=MULT)
 
-        def differences(c, g):
-            turn_over(c, g, negated[c, g], True)
-            turn_over(c, g, fwd[c, g], False)
-            return difference_banks(c, g)
+        def negate_on_scalar(c, g):
+            negated[c, g] = bwd[c, g]
+            for u in range(TILES):
+                nc.scalar.activation(out=bwd[c, g][:, u], in_=bwd[c, g][:, u], func=COPY, scale=-1.0)
 
-        def rates_on_vector(c, g):
-            factor = kap[:, g, :].unsqueeze(1).unsqueeze(3).to_broadcast([P, P // 2, PACK, 2])
-            for u, bank in enumerate(differences(c, g)):
-                nc.vector.tensor_tensor(
-                    out=h_bf[c, g][:, u * P : (u + 1) * P, :].rearrange("p (w e) t -> p w t e", e=2),
-                    in0=bank[:].rearrange("p (t w e) -> p w t e", t=PACK, e=2),
-                    in1=factor,
-                    op=MULT,
-                )
-
-        def rates_on_scalar(c, g):
-            for k, bank in enumerate(differences(c, g)):
-                for i in range(2):
-                    t = 2 * k + i
-                    nc.scalar.activation(
-                        out=planes[:, t, :], in_=bank[:, i * JC : (i + 1) * JC], func=COPY, scale=kap[:, g, t : t + 1]
-                    )
-            nc.scalar.copy(
-                out=h_bf[c, g].rearrange("p (w e) t -> p w t e", e=LINE),
-                in_=planes[:].rearrange("p t (w e) -> p w t e", e=LINE),
+        def negate_on_gpsimd(c, g, kib):
+            negated[c, g] = placed([P, TILES, PACK, P], F32, f"neg{c}{g}", kib)
+            nc.gpsimd.tensor_scalar(
+                out=negated[c, g][:].rearrange(flat),
+                in0=bwd[c, g][:].rearrange(flat),
+                scalar1=-1.0,
+                scalar2=0.0,
+                op0=MULT,
+                op1=ADD,
             )
+
+        def differences(c, g, into):
+            for side, opens in ((negated[c, g], True), (fwd[c, g], False)):
+                for k, bank in enumerate(into):
+                    if (c, g) not in on_scalar:
+                        blocks = [(k, t) for t in range(PACK)]
+                    else:
+                        blocks = [(u, t) for t in (2 * k, 2 * k + 1) for u in range(TILES)]
+                    for i, (u, t) in enumerate(blocks):
+                        nc.tensor.matmul(
+                            out=bank[:, i * P : (i + 1) * P],
+                            lhsT=side[:, u, t, :],
+                            rhs=ident[:],
+                            is_transpose=True,
+                            start=opens and i == 0,
+                            stop=not opens and i == len(blocks) - 1,
+                        )
+
+        def rates(c, g, into):
+            differences(c, g, into)
+            if (c, g) not in on_scalar:
+                factor = kap[:, g, :].unsqueeze(1).unsqueeze(3).to_broadcast([P, P // 2, PACK, 2])
+                for u, bank in enumerate(into):
+                    nc.vector.tensor_tensor(
+                        out=h_bf[c, g][:, u * P : (u + 1) * P, :].rearrange("p (w e) t -> p w t e", e=2),
+                        in0=bank[:].rearrange("p (t w e) -> p w t e", t=PACK, e=2),
+                        in1=factor,
+                        op=MULT,
+                    )
+            else:
+                for k, bank in enumerate(into):
+                    for i in range(2):
+                        t = 2 * k + i
+                        nc.scalar.activation(
+                            out=planes[:, k, :, i], in_=bank[:, i * JC : (i + 1) * JC], func=COPY, scale=kap[:, g, t : t + 1]
+                        )
+                nc.scalar.copy(
+                    out=h_bf[c, g].bitcast(U32), in_=planes[:].bitcast(U32).rearrange("p k j e -> p j (k e)")
+                )
 
         def quantize_group(c, g):
             nc.vector.quantize_mx(
@@ -273,6 +254,10 @@ def tile_list_reversible_reaction_rates_kernel(
             order = list(range(NT)) if c + 1 < CHUNKS else [3, 2, 0, 1]
             return (c * NT + order.index(n)) * JC
 
+        def y_run(c, n, width):
+            first = y_column(c, n)
+            return y_second[:] if (c, n) == (0, 1) else y[:, first : first + width]
+
         def species(c, rows, bank):
             for k, n in enumerate(rows):
                 for g in reversed(range(GROUPS)):
@@ -285,23 +270,15 @@ def tile_list_reversible_reaction_rates_kernel(
                         start=(k, g) == (0, GROUPS - 1),
                         stop=(k, g) == (len(rows) - 1, 0),
                     )
-            first = y_column(c, rows[0])
-            nc.scalar.copy(out=y[:, first : first + len(rows) * JC], in_=bank[:, : len(rows) * JC])
+            nc.scalar.copy(out=y_run(c, rows[0], len(rows) * JC), in_=bank[:, : len(rows) * JC])
 
         def scatter(n, c0, c1):
             j0, j1 = c0 * JC, c1 * JC
-            first = y_column(c0, n)
             nc.vector.tensor_tensor(
-                out=store[n][:].indirect(entries(idx2, j0, j1)), in0=y[:, first : first + j1 - j0], in1=wg[:, j0:j1], op=MULT
+                out=store[n][:].indirect(entries(idx2, j0, j1)), in0=y_run(c0, n, j1 - j0), in1=wg[:, j0:j1], op=MULT
             )
             if c1 == CHUNKS:
                 nc.sync.dma_start(out=out[n * P : (n + 1) * P, :], in_=store[n][:])
-
-        def rates(c, g):
-            if (c, g) in on_scalar:
-                rates_on_scalar(c, g)
-            else:
-                rates_on_vector(c, g)
 
         nc.vector.tensor_copy(out=vs[:], in_=tabs[:].bitcast(U8).indirect(idx[:]))
         for j0, j1 in ((0, JC), (JC, S)):
@@ -309,54 +286,64 @@ def tile_list_reversible_reaction_rates_kernel(
         for j0, j1 in ((0, JC), (JC, 2 * JC), (2 * JC, S)):
             gather_words(1, j0, j1)
         for tag in ("table_scales", "table0"):
-            store.append(keep.tile([P, T2], F32, name=f"store{len(store)}", tag=tag, align_bytes=64))
+            store.append(held([P, T2], F32, f"store{len(store)}", tag))
             nc.gpsimd.memset(store[-1][:].bitcast(I32), 0)
 
-        for c, g in steps[:AHEAD]:
-            backward(c, g, product_bank)
+        opening_ring = [banks[2:4], banks[0:2], pairs[1]]
+        for s, (c, g) in enumerate(steps[:AHEAD]):
+            backward(c, g, opening_ring[s % 3])
             if c == 0:
-                negate(c, g)
-        for k, piece in enumerate(pieces):
-            round_wf(*piece)
-            quantize_wf(*piece)
-        for g in range(GROUPS):
-            h_bf[0, g] = wf_bf[half_pieces[GROUPS - 1 - g][:3]][:]
+                negate_on_vector(c, g)
+        for k in range(3):
+            prepare_wf(k, placed([P, KP, PACK], BF16, f"wf_bf{k}", 10))
+        first_half = placed([P, KP // 2, PACK], BF16, "wf_bf3", 3)
+        prepare_wf(3, first_half)
+        prepare_wf(4, placed([P, KP // 2, PACK], BF16, "wf_bf4", 11))
+        h_bf[0, 0] = placed([P, JC, PACK], BF16, "h00", 10)[:]
+        h_bf[0, 1] = first_half[:]
+        negate_on_gpsimd(1, 1, 12)
+        forward(0, 0, banks[0:2])
+        rates(0, 0, banks[0:2])
+        quantize_group(0, 0)
+        negate_on_gpsimd(2, 0, 8)
+        forward(0, 1, banks[2:4])
+        rates(0, 1, pairs[1])
+        quantize_group(0, 1)
+        negate_on_gpsimd(2, 1, 4)
         for c in range(1, CHUNKS):
-            tag = "raw2" if c == 1 else f"h{c}"
-            h_pair[c] = keep.tile([P, GROUPS, JC, PACK], BF16, name=f"h{c}", tag=tag, align_bytes=64)[:]
+            shape = [P, GROUPS, JC, PACK]
+            h_pair[c] = (placed(shape, BF16, "h1", 0) if c == 1 else held(shape, BF16, f"h{c}"))[:]
             for g in range(GROUPS):
                 h_bf[c, g] = h_pair[c][:, g]
-        forward(0, 0, banks[:2])
-        rates(0, 0)
-        quantize_group(0, 0)
-        forward(0, 1, banks[2:4])
-        rates(0, 1)
-        quantize_group(0, 1)
-        negate(1, 0)
+        negate_on_scalar(1, 0)
         forward(1, 0, pairs[0])
         forward(1, 1, [banks[0], banks[3]])
-        negate(1, 1)
-        rates(1, 0)
+        rates(1, 0, pairs[0])
 
         ring = [banks[b] for b in (1, 3, 2, 0)]
+        taken = []
+
+        def ring_banks(count):
+            for k in range(count):
+                taken.append(ring[len(taken) % len(ring)])
+            return taken[-count:]
+
         for c in range(CHUNKS):
             early = range(NT - 1) if c + 2 < CHUNKS else range(NT // 2)
             late = [n for n in range(NT) if n not in early]
+            if c == 2:
+                rates(3, 0, pairs[0])
             for n in early:
-                species(c, [n], ring_bank())
+                species(c, [n], pairs[0][n] if c == 2 else ring_banks(1)[0])
                 scatter(n, c, c + 1)
             if c == 0:
-                forward(2, 0, [banks[0], ring_bank()])
-                negate(2, 0, "fwd0")
-                forward(2, 1, [ring_bank(), ring_bank()])
-                negate(2, 1, "fwd1")
-            if c == 1:
-                forward(3, 0, [ring_bank(), ring_bank()])
-                negate(3, 0, "fwd3")
+                negate_on_gpsimd(3, 0, 16)
+                forward(2, 0, [banks[0]] + ring_banks(1))
+                forward(2, 1, ring_banks(2))
             if c + 1 < CHUNKS:
-                rates(c + 1, 1)
-            if c + 2 < CHUNKS:
-                rates(c + 2, 0)
+                rates(c + 1, 1, pairs[1])
+            if c == 0:
+                rates(2, 0, pairs[0])
             if c + 1 < CHUNKS:
                 quantize_chunk(c + 1)
             species(c, sorted(late, key=lambda n: y_column(c, n)), pairs[1][0])
@@ -366,7 +353,8 @@ def tile_list_reversible_reaction_rates_kernel(
                 scatter(NT - 1, min(c, CHUNKS - 2), c + 1)
             if c == 0:
                 for step in steps[AHEAD:]:
-                    backward(*step, ring_bank)
+                    backward(*step, ring_banks(2))
             if c == 1:
-                negate(3, 1, "fwd4")
-                forward(3, 1, [ring_bank(), ring_bank()])
+                for g in range(GROUPS):
+                    forward(3, g, ring_banks(2))
+                negate_on_scalar(3, 1)

@@ -33,6 +33,7 @@ PER_COL = 16
 LINE = 2
 KIB = 1024
 AHEAD = 7
+WB_ROW = 12
 
 
 def tile_list_reversible_reaction_rates_kernel(
@@ -81,10 +82,10 @@ def tile_list_reversible_reaction_rates_kernel(
             rows = wb_words[a].rearrange("p c i -> p (c i)")[:, g * KP * PACK : (g + 1) * KP * PACK]
             nc.sync.dma_start(out=wbw[g, a][:], in_=rows.bitcast(I32))
 
-        def load_planes(dst, src):
+        def load_planes(dst, src, row):
             for q in range(QUADRANTS):
                 rows = src[:, 4 * q : 4 * q + 4, :].rearrange("a i c -> i a c")
-                nc.sync.dma_start(out=dst[32 * q : 32 * q + 4, :, :], in_=rows.bitcast(I32))
+                nc.sync.dma_start(out=dst[32 * q + row : 32 * q + row + 4, :, :], in_=rows.bitcast(I32))
 
         def load_table(a):
             nc.sync.dma_start(out=tabw[a][:], in_=tab_words[a].rearrange("p t i -> p (t i)").bitcast(I32))
@@ -94,7 +95,7 @@ def tile_list_reversible_reaction_rates_kernel(
         for q in range(QUADRANTS):
             nc.sync.dma_start(out=tabs[32 * q : 32 * q + 8, :], in_=tab_scales[:, 4 * q : 4 * q + 4, :].bitcast(I32))
         load_table(0)
-        load_planes(wbs, wb_scales)
+        load_planes(wbs, wb_scales, WB_ROW)
         load_table(1)
         load_wbw(0, 1)
         for a in range(PASSES):
@@ -103,7 +104,7 @@ def tile_list_reversible_reaction_rates_kernel(
             rows = wf[a * KP : (a + 1) * KP, g * KP + c0 : g * KP + c1]
             nc.sync.dma_start(out=wf_raw[k][:], in_=rows.rearrange("(p i) c -> p i c", i=PACK))
         nc.sync.dma_start(out=kap[:], in_=kappa.rearrange("(g p t) -> p g t", g=GROUPS, t=PACK))
-        load_planes(wss, ws_scales)
+        load_planes(wss, ws_scales, 0)
         nc.sync.dma_start(out=wsw[:].bitcast(I32), in_=ws_words.rearrange("g p c -> p g c").bitcast(I32))
         nc.sync.dma_start(idx2[:], offs2)
         nc.sync.dma_start(out=wg[:], in_=wgo)
@@ -134,18 +135,23 @@ def tile_list_reversible_reaction_rates_kernel(
 
         def prepare_wf(k, grouped):
             g, a, c0, c1 = pieces[k]
-            nc.vector.tensor_copy(
-                out=grouped[:].rearrange("p (u i) t -> p u t i", i=LINE),
-                in_=wf_raw[k][:].rearrange("p t (u i) -> p u t i", i=LINE),
-            )
-            nc.vector.quantize_mx(
-                out=wfw[g, a][:, c0:c1].bitcast(FP8X4),
-                scales=wfs[g, a][:, c0:c1],
-                in_=grouped[:].rearrange("p c t -> p (c t)"),
-            )
+            width = (c1 - c0) // (1 + g)
+            runs = [slice(j, j + width) for j in range(0, c1 - c0, width)]
+            for run in runs:
+                nc.vector.tensor_copy(
+                    out=grouped[:, run].rearrange("p (u i) t -> p u t i", i=LINE),
+                    in_=wf_raw[k][:, :, run].rearrange("p t (u i) -> p u t i", i=LINE),
+                )
+            for run in runs:
+                nc.vector.quantize_mx(
+                    out=wfw[g, a][:, c0:c1][:, run].bitcast(FP8X4),
+                    scales=wfs[g, a][:, c0:c1][:, run],
+                    in_=grouped[:, run].rearrange("p c t -> p (c t)"),
+                )
 
-        def exponentials(dst, c, into, words, scales, parts):
-            for k, (a, c0, c1) in enumerate(parts):
+        def products(c, into, words, scales, parts, chosen):
+            for k in chosen:
+                a, c0, c1 = parts[k]
                 for u, bank in into.items():
                     cells = slice(c * JC + u * P, c * JC + (u + 1) * P)
                     nc.tensor.matmul_mx(
@@ -157,14 +163,19 @@ def tile_list_reversible_reaction_rates_kernel(
                         start=k == 0,
                         stop=k == len(parts) - 1,
                     )
+
+        def exponentials(dst, c, into, words, scales, parts, done=0):
+            products(c, into, words, scales, parts, range(done, len(parts)))
             for u, bank in into.items():
                 nc.scalar.activation(out=dst[:, u], in_=bank[:].rearrange("p (m t) -> p t m", t=PACK), func=EXP)
 
-        def backward(c, g, into):
+        def backward_weights(g):
             words = [wbw[g, a][:] for a in range(PASSES)]
-            scales = [wbs[:, a, :].bitcast(U8)[:, g * KP : (g + 1) * KP] for a in range(PASSES)]
+            return words, [wbs[WB_ROW:, a, :].bitcast(U8)[:, g * KP : (g + 1) * KP] for a in range(PASSES)]
+
+        def backward(c, g, into, done=0):
             for u in range(TILES):
-                exponentials(bwd[c, g], c, {u: into[u]}, words, scales, whole)
+                exponentials(bwd[c, g], c, {u: into[u]}, *backward_weights(g), whole, done)
 
         def forward(c, g, into):
             words = [wfw[g, a][:] for a in range(PASSES)]
@@ -281,17 +292,19 @@ def tile_list_reversible_reaction_rates_kernel(
                 nc.sync.dma_start(out=out[n * P : (n + 1) * P, :], in_=store[n][:])
 
         nc.vector.tensor_copy(out=vs[:], in_=tabs[:].bitcast(U8).indirect(idx[:]))
-        for j0, j1 in ((0, JC), (JC, S)):
-            gather_words(0, j0, j1)
-        for j0, j1 in ((0, JC), (JC, 2 * JC), (2 * JC, S)):
-            gather_words(1, j0, j1)
+        for a in range(PASSES):
+            for j0, j1 in ((0, JC), (JC, 2 * JC), (2 * JC, S)):
+                gather_words(a, j0, j1)
         for tag in ("table_scales", "table0"):
             store.append(held([P, T2], F32, f"store{len(store)}", tag))
             nc.gpsimd.memset(store[-1][:].bitcast(I32), 0)
 
         opening_ring = [banks[2:4], banks[0:2], pairs[1]]
+        begun = [(0, 0), (1, 0)]
+        for c, g in begun:
+            products(c, dict(enumerate(opening_ring[steps.index((c, g))])), *backward_weights(g), whole, [0])
         for s, (c, g) in enumerate(steps[:AHEAD]):
-            backward(c, g, opening_ring[s % 3])
+            backward(c, g, opening_ring[s % 3], int((c, g) in begun))
             if c == 0:
                 negate_on_vector(c, g)
         for k in range(3):

from contextlib import ExitStack

import concourse.mybir as mybir
from concourse.masks import make_identity

K, R, N, T, T2, S = 1024, 1024, 512, 2048, 2048, 1024
FLOPS = 2 * S * (2 * K * R + R * N)

F32 = mybir.dt.float32
BF16 = mybir.dt.bfloat16
I32 = mybir.dt.int32
U32 = mybir.dt.uint32
U16 = mybir.dt.uint16
U8 = mybir.dt.uint8
FP8X4 = mybir.dt.float8_e4m3fn_x4
FP4X4 = mybir.dt.float4_e2m1fn_x4
EXP = mybir.ActivationFunctionType.Exp
COPY = mybir.ActivationFunctionType.Copy
MULT = mybir.AluOpType.mult
ADD = mybir.AluOpType.add

P = 128
PACK = 4
KP = P * PACK
PASSES = K // KP
GROUPS = R // KP
QUADRANTS = 4
JC = 256
CHUNKS = S // JC
TILES = JC // P
NT = N // P
PER_COL = 16
LINE = 2
KIB = 1024
AHEAD = 7
WB_ROW = 12


def tile_list_reversible_reaction_rates_kernel(
    tc, tab_words, tab_scales, wf, wb_words, wb_scales, kappa, ws_words, ws_scales, wgo, offs, offs2, out
):
    nc = tc.nc
    with ExitStack() as ctx:
        keep = ctx.enter_context(tc.tile_pool(name="keep", bufs=1))
        shared = ctx.enter_context(tc.tile_pool(name="shared", bufs=1))
        psum = ctx.enter_context(tc.psum_pool(name="psum", bufs=1))

        def held(shape, dtype, name, tag=None):
            return keep.tile(shape, dtype, name=name, tag=tag or name, align_bytes=64)

        def placed(shape, dtype, name, kib):
            return shared.tile(shape, dtype, name=name, offset=kib * KIB)

        idx = held([P, S // PER_COL], U16, "idx")
        idx2 = held([P, S // PER_COL], U16, "idx2")
        tabw = [held([P, T], I32, f"tabw{a}", f"table{a}") for a in range(PASSES)]
        tabs = held([P, T // 4], I32, "tabs", "table_scales")
        wbs = held([P, PASSES, R // 4], I32, "wbs")
        wbw = {(g, a): held([P, KP], I32, f"wbw{g}{a}") for g in range(GROUPS) for a in range(PASSES)}
        pieces = [(0, 0, 0, KP), (0, 1, 0, KP), (1, 0, 0, KP), (1, 1, 0, KP // 2), (1, 1, KP // 2, KP)]
        wf_raw = [
            placed([P, PACK, KP], F32, "wf_raw2", 0) if k == 2 else held([P, PACK, c1 - c0], F32, f"wf_raw{k}")
            for k, (g, a, c0, c1) in enumerate(pieces)
        ]
        wsw = held([P, GROUPS, 2 * N], U8, "wsw")
        wss = held([P, GROUPS, N // 4], I32, "wss")
        kap = held([P, GROUPS, PACK], F32, "kap")
        wg = held([P, S], F32, "wg")
        store = [held([P, T2], F32, f"store{n}") for n in range(NT // 2)]
        ident = held([P, P], F32, "ident")
        y = held([P, NT * S], F32, "y")
        y_second = placed([P, JC], F32, "y_second", 16)

        nc.vector.memset(tabs[:], 0)
        nc.vector.memset(wbs[:], 0)
        for n in range(NT // 2):
            nc.vector.memset(store[n][:].bitcast(I32), 0)
        nc.vector.memset(wss[:], 0)
        make_identity(nc, ident[:])

        def load_wbw(g, a):
            rows = wb_words[a].rearrange("p c i -> p (c i)")[:, g * KP * PACK : (g + 1) * KP * PACK]
            nc.sync.dma_start(out=wbw[g, a][:], in_=rows.bitcast(I32))

        def load_planes(dst, src, row):
            for q in range(QUADRANTS):
                rows = src[:, 4 * q : 4 * q + 4, :].rearrange("a i c -> i a c")
                nc.sync.dma_start(out=dst[32 * q + row : 32 * q + row + 4, :, :], in_=rows.bitcast(I32))

        def load_table(a):
            nc.sync.dma_start(out=tabw[a][:], in_=tab_words[a].rearrange("p t i -> p (t i)").bitcast(I32))

        nc.sync.dma_start(idx[:], offs)
        load_wbw(0, 0)
        for q in range(QUADRANTS):
            nc.sync.dma_start(out=tabs[32 * q : 32 * q + 8, :], in_=tab_scales[:, 4 * q : 4 * q + 4, :].bitcast(I32))
        load_table(0)
        load_planes(wbs, wb_scales, WB_ROW)
        load_table(1)
        load_wbw(0, 1)
        for a in range(PASSES):
            load_wbw(1, a)
        for k, (g, a, c0, c1) in enumerate(pieces):
            rows = wf[a * KP : (a + 1) * KP, g * KP + c0 : g * KP + c1]
            nc.sync.dma_start(out=wf_raw[k][:], in_=rows.rearrange("(p i) c -> p i c", i=PACK))
        nc.sync.dma_start(out=kap[:], in_=kappa.rearrange("(g p t) -> p g t", g=GROUPS, t=PACK))
        load_planes(wss, ws_scales, 0)
        nc.sync.dma_start(out=wsw[:].bitcast(I32), in_=ws_words.rearrange("g p c -> p g c").bitcast(I32))
        nc.sync.dma_start(idx2[:], offs2)
        nc.sync.dma_start(out=wg[:], in_=wgo)

        vw = [held([P, S], U32, f"vw{a}") for a in range(PASSES)]
        vs = held([P, S], U8, "vs")
        wfw = {(g, a): held([P, KP], U32, f"wfw{g}{a}") for g in range(GROUPS) for a in range(PASSES)}
        wfs = {(g, a): held([P, KP], U8, f"wfs{g}{a}") for g in range(GROUPS) for a in range(PASSES)}
        banks = [psum.tile([P, KP], F32, name=f"bank{b}") for b in range(8)]
        pairs = [banks[4:6], banks[6:8]]
        steps = [(c, g) for c in range(CHUNKS) for g in range(GROUPS)]
        fwd = {(c, g): held([P, TILES, PACK, P], F32, f"fwd{c}{g}") for c, g in steps}
        bwd = {(c, g): held([P, TILES, PACK, P], F32, f"bwd{c}{g}") for c, g in steps}
        planes = held([P, 2, JC, 2], BF16, "planes")
        hw = [held([P, GROUPS, JC], U32, f"hw{c}") for c in range(CHUNKS)]
        hs = [held([P, GROUPS, JC], U8, f"hs{c}") for c in range(CHUNKS)]
        on_scalar = [(1, 1), (2, 1), (3, 0), (3, 1)]
        whole = [(a, 0, KP) for a in range(PASSES)]
        negated = {}
        h_bf = {}
        h_pair = {}

        def entries(lst, j0, j1):
            return lst[:, j0 // PER_COL : j1 // PER_COL]

        def gather_words(a, j0, j1):
            nc.vector.tensor_copy(out=vw[a][:, j0:j1], in_=tabw[a][:].bitcast(U32).indirect(entries(idx, j0, j1)))

        def prepare_wf(k, grouped):
            g, a, c0, c1 = pieces[k]
            width = (c1 - c0) // (1 + g)
            runs = [slice(j, j + width) for j in range(0, c1 - c0, width)]
            for run in runs:
                nc.vector.tensor_copy(
                    out=grouped[:, run].rearrange("p (u i) t -> p u t i", i=LINE),
                    in_=wf_raw[k][:, :, run].rearrange("p t (u i) -> p u t i", i=LINE),
                )
            for run in runs:
                nc.vector.quantize_mx(
                    out=wfw[g, a][:, c0:c1][:, run].bitcast(FP8X4),
                    scales=wfs[g, a][:, c0:c1][:, run],
                    in_=grouped[:, run].rearrange("p c t -> p (c t)"),
                )

        def products(c, into, words, scales, parts, chosen):
            for k in chosen:
                a, c0, c1 = parts[k]
                for u, bank in into.items():
                    cells = slice(c * JC + u * P, c * JC + (u + 1) * P)
                    nc.tensor.matmul_mx(
                        out=bank[:, c0:c1],
                        lhsT=vw[a][:, cells].bitcast(FP8X4),
                        lhsT_scale=vs[4 * a :, cells],
                        rhs=words[a][:, c0:c1].bitcast(FP8X4),
                        rhs_scale=scales[a][:, c0:c1],
                        start=k == 0,
                        stop=k == len(parts) - 1,
                    )

        def exponentials(dst, c, into, words, scales, parts, done=0):
            products(c, into, words, scales, parts, range(done, len(parts)))
            for u, bank in into.items():
                nc.scalar.activation(out=dst[:, u], in_=bank[:].rearrange("p (m t) -> p t m", t=PACK), func=EXP)

        def backward_weights(g):
            words = [wbw[g, a][:] for a in range(PASSES)]
            return words, [wbs[WB_ROW:, a, :].bitcast(U8)[:, g * KP : (g + 1) * KP] for a in range(PASSES)]

        def backward(c, g, into, done=0):
            for u in range(TILES):
                exponentials(bwd[c, g], c, {u: into[u]}, *backward_weights(g), whole, done)

        def forward(c, g, into):
            words = [wfw[g, a][:] for a in range(PASSES)]
            scales = [wfs[g, a][:] for a in range(PASSES)]
            if (c, g) == (0, GROUPS - 1):
                parts = [piece[1:] for piece in pieces if piece[0] == g]
                exponentials(fwd[c, g], c, dict(enumerate(into)), words, scales, parts)
            else:
                for u in range(TILES):
                    exponentials(fwd[c, g], c, {u: into[u]}, words, scales, whole)

        flat = "p u t m -> p (u t m)"

        def negate_on_vector(c, g):
            negated[c, g] = bwd[c, g]
            values = bwd[c, g][:].rearrange(flat)
            nc.vector.tensor_scalar(out=values, in0=values, scalar1=-1.0, scalar2=None, op0=MULT)

        def negate_on_scalar(c, g):
            negated[c, g] = bwd[c, g]
            for u in range(TILES):
                nc.scalar.activation(out=bwd[c, g][:, u], in_=bwd[c, g][:, u], func=COPY, scale=-1.0)

        def negate_on_gpsimd(c, g, kib):
            negated[c, g] = placed([P, TILES, PACK, P], F32, f"neg{c}{g}", kib)
            nc.gpsimd.tensor_scalar(
                out=negated[c, g][:].rearrange(flat),
                in0=bwd[c, g][:].rearrange(flat),
                scalar1=-1.0,
                scalar2=0.0,
                op0=MULT,
                op1=ADD,
            )

        def differences(c, g, into):
            for side, opens in ((negated[c, g], True), (fwd[c, g], False)):
                for k, bank in enumerate(into):
                    if (c, g) not in on_scalar:
                        blocks = [(k, t) for t in range(PACK)]
                    else:
                        blocks = [(u, t) for t in (2 * k, 2 * k + 1) for u in range(TILES)]
                    for i, (u, t) in enumerate(blocks):
                        nc.tensor.matmul(
                            out=bank[:, i * P : (i + 1) * P],
                            lhsT=side[:, u, t, :],
                            rhs=ident[:],
                            is_transpose=True,
                            start=opens and i == 0,
                            stop=not opens and i == len(blocks) - 1,
                        )

        def rates(c, g, into):
            differences(c, g, into)
            if (c, g) not in on_scalar:
                factor = kap[:, g, :].unsqueeze(1).unsqueeze(3).to_broadcast([P, P // 2, PACK, 2])
                for u, bank in enumerate(into):
                    nc.vector.tensor_tensor(
                        out=h_bf[c, g][:, u * P : (u + 1) * P, :].rearrange("p (w e) t -> p w t e", e=2),
                        in0=bank[:].rearrange("p (t w e) -> p w t e", t=PACK, e=2),
                        in1=factor,
                        op=MULT,
                    )
            else:
                for k, bank in enumerate(into):
                    for i in range(2):
                        t = 2 * k + i
                        nc.scalar.activation(
                            out=planes[:, k, :, i], in_=bank[:, i * JC : (i + 1) * JC], func=COPY, scale=kap[:, g, t : t + 1]
                        )
                nc.scalar.copy(
                    out=h_bf[c, g].bitcast(U32), in_=planes[:].bitcast(U32).rearrange("p k j e -> p j (k e)")
                )

        def quantize_group(c, g):
            nc.vector.quantize_mx(
                out=hw[c][:, g].bitcast(FP8X4), scales=hs[c][:, g], in_=h_bf[c, g].rearrange("p j t -> p (j t)")
            )

        def quantize_chunk(c):
            nc.vector.quantize_mx(
                out=hw[c][:].rearrange("p g j -> p (g j)").bitcast(FP8X4),
                scales=hs[c][:].rearrange("p g j -> p (g j)"),
                in_=h_pair[c].rearrange("p g j t -> p (g j t)"),
            )

        def y_column(c, n):
            order = list(range(NT)) if c + 1 < CHUNKS else [3, 2, 0, 1]
            return (c * NT + order.index(n)) * JC

        def y_run(c, n, width):
            first = y_column(c, n)
            return y_second[:] if (c, n) == (0, 1) else y[:, first : first + width]

        def species(c, rows, bank):
            for k, n in enumerate(rows):
                for g in reversed(range(GROUPS)):
                    nc.tensor.matmul_mx(
                        out=bank[:, k * JC : (k + 1) * JC],
                        lhsT=wsw[:, g, 2 * n * P : 2 * (n + 1) * P].bitcast(FP4X4),
                        lhsT_scale=wss[:, g, n * P // 4 : (n + 1) * P // 4].bitcast(U8),
                        rhs=hw[c][:, g].bitcast(FP8X4),
                        rhs_scale=hs[c][:, g],
                        start=(k, g) == (0, GROUPS - 1),
                        stop=(k, g) == (len(rows) - 1, 0),
                    )
            nc.scalar.copy(out=y_run(c, rows[0], len(rows) * JC), in_=bank[:, : len(rows) * JC])

        def scatter(n, c0, c1):
            j0, j1 = c0 * JC, c1 * JC
            nc.vector.tensor_tensor(
                out=store[n][:].indirect(entries(idx2, j0, j1)), in0=y_run(c0, n, j1 - j0), in1=wg[:, j0:j1], op=MULT
            )
            if c1 == CHUNKS:
                nc.sync.dma_start(out=out[n * P : (n + 1) * P, :], in_=store[n][:])

        nc.vector.tensor_copy(out=vs[:], in_=tabs[:].bitcast(U8).indirect(idx[:]))
        for a in range(PASSES):
            for j0, j1 in ((0, JC), (JC, 2 * JC), (2 * JC, S)):
                gather_words(a, j0, j1)
        for tag in ("table_scales", "table0"):
            store.append(held([P, T2], F32, f"store{len(store)}", tag))
            nc.gpsimd.memset(store[-1][:].bitcast(I32), 0)

        opening_ring = [banks[2:4], banks[0:2], pairs[1]]
        begun = [(0, 0), (1, 0)]
        for c, g in begun:
            products(c, dict(enumerate(opening_ring[steps.index((c, g))])), *backward_weights(g), whole, [0])
        for s, (c, g) in enumerate(steps[:AHEAD]):
            backward(c, g, opening_ring[s % 3], int((c, g) in begun))
            if c == 0:
                negate_on_vector(c, g)
        for k in range(3):
            prepare_wf(k, placed([P, KP, PACK], BF16, f"wf_bf{k}", 10))
        first_half = placed([P, KP // 2, PACK], BF16, "wf_bf3", 3)
        prepare_wf(3, first_half)
        prepare_wf(4, placed([P, KP // 2, PACK], BF16, "wf_bf4", 11))
        h_bf[0, 0] = placed([P, JC, PACK], BF16, "h00", 10)[:]
        h_bf[0, 1] = first_half[:]
        negate_on_gpsimd(1, 1, 12)
        forward(0, 0, banks[0:2])
        rates(0, 0, banks[0:2])
        quantize_group(0, 0)
        negate_on_gpsimd(2, 0, 8)
        forward(0, 1, banks[2:4])
        rates(0, 1, pairs[1])
        quantize_group(0, 1)
        negate_on_gpsimd(2, 1, 4)
        for c in range(1, CHUNKS):
            shape = [P, GROUPS, JC, PACK]
            h_pair[c] = (placed(shape, BF16, "h1", 0) if c == 1 else held(shape, BF16, f"h{c}"))[:]
            for g in range(GROUPS):
                h_bf[c, g] = h_pair[c][:, g]
        negate_on_scalar(1, 0)
        forward(1, 0, pairs[0])
        forward(1, 1, [banks[0], banks[3]])
        rates(1, 0, pairs[0])

        ring = [banks[b] for b in (1, 3, 2, 0)]
        taken = []

        def ring_banks(count):
            for k in range(count):
                taken.append(ring[len(taken) % len(ring)])
            return taken[-count:]

        for c in range(CHUNKS):
            early = range(NT - 1) if c + 2 < CHUNKS else range(NT // 2)
            late = [n for n in range(NT) if n not in early]
            if c == 2:
                rates(3, 0, pairs[0])
            for n in early:
                species(c, [n], pairs[0][n] if c == 2 else ring_banks(1)[0])
                scatter(n, c, c + 1)
            if c == 0:
                negate_on_gpsimd(3, 0, 16)
                forward(2, 0, [banks[0]] + ring_banks(1))
                forward(2, 1, ring_banks(2))
            if c + 1 < CHUNKS:
                rates(c + 1, 1, pairs[1])
            if c == 0:
                rates(2, 0, pairs[0])
            if c + 1 < CHUNKS:
                quantize_chunk(c + 1)
            species(c, sorted(late, key=lambda n: y_column(c, n)), pairs[1][0])
            if c + 2 >= CHUNKS:
                scatter(NT - 2, c, c + 1)
            if c + 2 != CHUNKS:
                scatter(NT - 1, min(c, CHUNKS - 2), c + 1)
            if c == 0:
                for step in steps[AHEAD:]:
                    backward(*step, ring_banks(2))
            if c == 1:
                for g in range(GROUPS):
                    forward(3, g, ring_banks(2))
                negate_on_scalar(3, 1)
